import numpy as np
import ml_dtypes


def mxq(x, axis, fmt="e4m3"):
    dtype, down = {"e4m3": (ml_dtypes.float8_e4m3fn, 7), "e5m2": (ml_dtypes.float8_e5m2, 14)}[fmt]
    v = np.moveaxis(np.asarray(x, np.float32).astype(ml_dtypes.bfloat16).astype(np.float64), axis, -1)
    blocks = v.reshape(v.shape[:-1] + (-1, 32))
    amax = np.abs(blocks).max(-1, keepdims=True)
    byte = np.maximum(np.where(amax > 0, np.frexp(amax)[1] - 1 + 127, 0) - down, 1)
    scale = np.exp2(byte - 127.0)
    codes = (blocks / scale).astype(np.float32).astype(dtype).astype(np.float64)
    return np.moveaxis((codes * scale).reshape(v.shape), -1, axis)


WIDE = False


def mx_kscale(k):
    if not WIDE:
        return np.ones(k)
    levels = np.array([10, -10, 5, -5, 0])
    if k % 512:
        return np.exp2(np.random.permutation(np.resize(levels, k // 32))).repeat(32)
    a = np.empty((k // 512, 16))
    for p in range(k // 512):
        a[p, :8] = np.random.permutation(np.resize(levels, 8))
        for g in range(8):
            far = levels[np.abs(levels - a[p, g]) >= 10]
            a[p, g + 8] = far[np.random.randint(len(far))]
    return np.exp2(a.ravel()).repeat(32)


def f64(x):
    return np.asarray(x).astype(np.float64)


def striped(idx):
    return np.tile(idx.reshape(-1, 16).T, (8, 1)).astype(np.uint16)


def unstriped(offs):
    return offs[:16].T.reshape(-1).astype(np.int64)


def striped8(idx):
    return np.concatenate([x.reshape(-1, 16).T for x in idx]).astype(np.uint16)


def runs(offs, k):
    lists = np.stack([offs[16 * r : 16 * r + 16].T.reshape(-1) for r in range(8)]).astype(np.int64)
    return lists[np.arange(k) % 512 // 64]


def pack_weight(w):
    k, n = w.shape
    w = f64(np.asarray(w, np.float32).astype(ml_dtypes.bfloat16)).reshape(k // 32, 32, n)
    amax = np.abs(w).max(1)
    byte = np.clip(np.where(amax > 0, np.frexp(amax)[1] - 1 + 127 - 7, 1), 1, 254)
    scaled = (w * np.exp2(127.0 - byte)[:, None, :]).reshape(k, n).astype(np.float32)
    words = np.ascontiguousarray(scaled.reshape(k // 512, 128, 4, n).transpose(0, 1, 3, 2)).astype(ml_dtypes.float8_e4m3fn).view(np.uint8)
    return words, np.ascontiguousarray(byte.astype(np.uint8).reshape(k // 512, 16, n))


def unpack_weight(words, scales):
    g, p, n, _ = words.shape
    vals = np.ascontiguousarray(words).view(ml_dtypes.float8_e4m3fn).astype(np.float64) * np.repeat(np.exp2(scales.astype(np.float64) - 127.0), 8, axis=1)[..., None]
    return vals.transpose(0, 1, 3, 2).reshape(g * 512, n)


def sigmoid(v):
    return 1.0 / (1.0 + np.exp(-np.maximum(v, -700.0)))

def planes(y):
    n, m = y.shape
    v = y.astype(np.float32).astype(ml_dtypes.bfloat16).astype(np.float64).reshape(n // 32, 32, m)
    top = np.abs(v).max(1)
    byte = np.clip(np.where(top > 0, np.frexp(top)[1] - 1 + 127 - 7, 1), 1, 254)
    codes = (v * np.exp2(127.0 - byte)[:, None, :]).reshape(n, m).astype(np.float32).astype(ml_dtypes.float8_e4m3fn).view(np.uint8)
    words = codes.reshape(n // 512, 128, 4, m).transpose(0, 1, 3, 2)
    return np.ascontiguousarray(words), np.ascontiguousarray(byte.astype(np.uint8).reshape(n // 512, 16, m))


K, T, S, N, H = 512, 2048, 512, 512, 512


def setup_inputs():
    n = np.random.standard_normal
    s = mx_kscale(K)[:, None]
    u = mx_kscale(H)
    packed_xT = pack_weight(n((K, T)) * s)
    packed_w1 = pack_weight(n((K, H)) / np.sqrt(K) / s)
    packed_w2 = pack_weight(n((K, H)) / np.sqrt(K) / s)
    packed_w4 = pack_weight(n((H, N)) / np.sqrt(H) / u[:, None])
    return {
        "x_words": packed_xT[0],
        "x_scales": packed_xT[1],
        "w1_words": packed_w1[0],
        "w1_scales": packed_w1[1],
        "w2_words": packed_w2[0],
        "w2_scales": packed_w2[1],
        "w3": (n((K, H)) / np.sqrt(K) / s * u).astype(np.float32),
        "w4_words": packed_w4[0],
        "w4_scales": packed_w4[1],
        "offs": striped(np.random.permutation(T)[:S]),
        "p1": striped8(np.stack([np.random.permutation(S) for _ in range(8)])),
        "p2": striped8(np.stack([np.random.permutation(S) for _ in range(8)])),
    }


def reference(x_words, x_scales, w1_words, w1_scales, w2_words, w2_scales, w3, w4_words, w4_scales, offs, p1, p2):
    xq = unpack_weight(x_words, x_scales)[:, unstriped(offs)]
    y = unpack_weight(w1_words, w1_scales).T @ xq
    e = unpack_weight(w2_words, w2_scales).T @ xq
    s1 = sigmoid(3.0 * (y + e[np.arange(H)[:, None], runs(p1, H)]))
    h = mxq(f64(w3), 0, "e4m3").T @ xq
    s2 = sigmoid(3.0 * (y + e[np.arange(H)[:, None], runs(p2, H)]))
    z = (s1 * (h[np.arange(H)[:, None], runs(p1, H)]) + s2 * (h[np.arange(H)[:, None], runs(p2, H)])) / (s1 + s2 + 0.1)
    out_0 = unpack_weight(w4_words, w4_scales).T @ mxq(z, 0, "e4m3")
    return (out_0,) + planes(out_0)

@@ -1,0 +1,278 @@
+from contextlib import ExitStack
+
+import concourse.mybir as mybir
+from concourse.masks import make_identity
+
+K, T, S, N, H = 512, 2048, 512, 512, 512
+FLOPS = 4 * 2 * 512 * 512 * 512
+
+F32 = mybir.dt.float32
+BF16 = mybir.dt.bfloat16
+I32 = mybir.dt.int32
+U32 = mybir.dt.uint32
+U16 = mybir.dt.uint16
+U8 = mybir.dt.uint8
+FP8X4 = mybir.dt.float8_e4m3fn_x4
+ACT = mybir.ActivationFunctionType
+ALU = mybir.AluOpType
+
+P = 128
+PACK = 4
+HALF = 256
+PIECES = (256, 128, 128)
+
+
+def tile_picked_ggnorm_none_po_kernel(
+    tc, x_words, x_scales, w1_words, w1_scales, w2_words, w2_scales, w3, w4_words, w4_scales, offs, p1, p2,
+    out_0, out_1, out_2,
+):
+    nc = tc.nc
+
+    def words_of(dram):
+        return dram[0].rearrange("p n t -> p (n t)").bitcast(I32)
+
+    def load_scale_rows(engine, plane, first, dram):
+        rows = dram[0].bitcast(I32)
+        for q in range(4):
+            engine.dma_start(out=plane[32 * q + first : 32 * q + first + 4, :].bitcast(I32), in_=rows[4 * q : 4 * q + 4, :])
+
+    def load_scale_quadrant(engine, plane, dram, q):
+        rows = dram[0].bitcast(I32)[4 * q : 4 * q + 4, :]
+        engine.dma_start(
+            out=plane[32 * q : 32 * q + 32, :].bitcast(I32),
+            in_=rows.unsqueeze(0).broadcast_to([8, 4, rows.shape[1]]),
+        )
+
+    def deal(out, in_, ts):
+        nc.vector.tensor_copy(
+            out=out.rearrange("p (t m) -> p t m", t=PACK)[:, ts, :],
+            in_=in_.rearrange("p (m t) -> p t m", t=PACK)[:, ts, :],
+        )
+
+    with ExitStack() as ctx:
+        keep = ctx.enter_context(tc.tile_pool(name="keep", bufs=1))
+        ring = ctx.enter_context(tc.tile_pool(name="ring", bufs=3))
+        psum = ctx.enter_context(tc.psum_pool(name="psum", bufs=1))
+
+        offs_sb = keep.tile([P, S // 16], U16)
+        p_sb = [keep.tile([P, S // 16], U16, name=f"p{i}_sb") for i in (1, 2)]
+        xw = keep.tile([P, T], U32, align_bytes=64, tag="big")
+        xs = keep.tile([P, T], U8, align_bytes=64)
+        w1s_raw = keep.tile([P, H], U8, align_bytes=64)
+        w2s_raw = keep.tile([P, H], U8, align_bytes=64, tag="sraw")
+        w1_raw = keep.tile([P, H], I32, align_bytes=64)
+        w2_raw = keep.tile([P, H], I32, align_bytes=64, tag="wraw")
+        warm = keep.tile([P, 8], F32)
+
+        nc.vector.memset(xs[:].bitcast(I32), 0)
+        nc.vector.memset(warm[:], 0.0)
+        nc.scalar.activation(out=warm[:], in_=warm[:], func=ACT.Sigmoid)
+
+        nc.sync.dma_start(offs_sb[:], offs)
+        load_scale_quadrant(nc.sync, w2s_raw, w2_scales, 0)
+        load_scale_quadrant(nc.sync, w2s_raw, w2_scales, 1)
+        load_scale_rows(nc.sync, xs, 0, x_scales)
+        nc.sync.dma_start(out=xw[:].bitcast(I32), in_=words_of(x_words))
+        load_scale_quadrant(nc.sync, w2s_raw, w2_scales, 2)
+        load_scale_quadrant(nc.sync, w2s_raw, w2_scales, 3)
+        for q in range(3):
+            load_scale_quadrant(nc.sync, w1s_raw, w1_scales, q)
+        nc.sync.dma_start(out=w2_raw[:], in_=words_of(w2_words))
+        nc.sync.dma_start(out=w1_raw[:], in_=words_of(w1_words))
+        load_scale_quadrant(nc.sync, w1s_raw, w1_scales, 3)
+        nc.sync.dma_start(p_sb[0][:], p1)
+        nc.sync.dma_start(p_sb[1][:], p2)
+
+        ident = keep.tile([P, P], F32)
+        make_identity(nc, ident[:])
+
+        xg_s = keep.tile([P, S], U8, align_bytes=64)
+        xg_w = keep.tile([P, S], U32, align_bytes=64)
+        nc.vector.tensor_copy(out=xg_s[:], in_=xs[:].indirect(offs_sb[:]))
+        nc.vector.tensor_copy(out=xg_w[:], in_=xw[:].indirect(offs_sb[:]))
+
+        w1s = keep.tile([P, H], U8, align_bytes=64)
+        w2s = keep.tile([P, H], U8, align_bytes=64)
+        w1d = keep.tile([P, H], I32, align_bytes=64)
+        w2d = keep.tile([P, H], I32, align_bytes=64)
+        for ts in (slice(0, 2), slice(2, 4)):
+            deal(w2s[:], w2s_raw[:], ts)
+            deal(w2d[:], w2_raw[:], ts)
+            deal(w1s[:], w1s_raw[:], ts)
+            deal(w1d[:], w1_raw[:], ts)
+
+        w3_raw = keep.tile([P, PACK, H], F32, align_bytes=64, tag="big")
+        nc.sync.dma_start(out=w3_raw[:], in_=w3.rearrange("(p j) c -> p j c", j=PACK))
+        w4_raw = keep.tile([P, N], I32, align_bytes=64, tag="wraw")
+        w4s_raw = keep.tile([P, N], U8, align_bytes=64, tag="sraw")
+        nc.sync.dma_start(out=w4_raw[:], in_=words_of(w4_words))
+        for q in range(4):
+            load_scale_quadrant(nc.sync, w4s_raw, w4_scales, q)
+
+        def product(codes, plane, t):
+            bank = psum.tile([P, S], F32, tag="mm", bufs=4, name="mm")
+            cols = slice(t * P, (t + 1) * P)
+            nc.tensor.matmul_mx(
+                out=bank[:], lhsT=codes[:, cols].bitcast(FP8X4), lhsT_scale=plane[:, cols],
+                rhs=xg_w[:].bitcast(FP8X4), rhs_scale=xg_s[:], start=True, stop=True,
+            )
+            return bank
+
+        def add_turned(bank_cols, a, b):
+            nc.tensor.matmul(bank_cols, lhsT=a, rhs=ident[:], start=True, stop=False, is_transpose=True)
+            nc.tensor.matmul(bank_cols, lhsT=b, rhs=ident[:], start=False, stop=True, is_transpose=True)
+
+        order = [0]
+
+        def slot(shape, dtype):
+            tile = keep.tile(shape, dtype, tag=f"slot{order[0] % 3}", name="slot", align_bytes=64)
+            order[0] = order[0] + 1
+            return tile
+
+        w3c = keep.tile([P, H], U32, align_bytes=64)
+        w3s = keep.tile([P, H], U8, align_bytes=64)
+        h_sb = [keep.tile([P, S], F32, name=f"h_sb{t}") for t in range(PACK)]
+
+        def values():
+            w3b = slot([P, PACK, P, PACK], BF16)
+            nc.vector.tensor_copy(
+                out=w3b[:].rearrange("p t m j -> p m j t"),
+                in_=w3_raw[:].rearrange("p j (m t) -> p m j t", t=PACK),
+            )
+            nc.vector.quantize_mx(out=w3c[:].bitcast(FP8X4), scales=w3s[:], in_=w3b[:].rearrange("p t m j -> p (t m j)"))
+
+        gate = [keep.tile([P, 2, S], F32, name=f"gate{t}") for t in range(PACK)]
+        den_sq = keep.tile([P, 4, PACK, P], F32)
+        for t in range(PACK):
+            if t == 3:
+                values()
+            e_sb = ring.tile([P, S], F32, name="e_sb")
+            y_sb = ring.tile([P, S], F32, name="y_sb")
+            e_ps = product(w2d, w2s, t)
+            y_ps = product(w1d, w1s, t)
+            nc.scalar.copy(out=e_sb[:], in_=e_ps[:])
+            if t == 0:
+                nc.vector.tensor_copy(out=y_sb[:], in_=y_ps[:])
+            else:
+                nc.scalar.copy(out=y_sb[:], in_=y_ps[:])
+            key = slot([P, 2, S], F32)
+            for i in range(2):
+                for c in range(0, S, HALF):
+                    nc.vector.tensor_tensor(
+                        key[:, i, c : c + HALF], e_sb[:].indirect(p_sb[i][:, c // 16 : (c + HALF) // 16]),
+                        y_sb[:, c : c + HALF], ALU.add,
+                    )
+                nc.scalar.activation(out=gate[t][:, i, :], in_=key[:, i, :], func=ACT.Sigmoid, scale=3.0)
+            den = psum.tile([P, 4, P], F32, tag=f"acc{t % 3}", name="den")
+            for b in range(4):
+                blk = slice(b * P, (b + 1) * P)
+                add_turned(den[:, b, :], gate[t][:, 0, blk], gate[t][:, 1, blk])
+            nc.scalar.activation(out=den_sq[:, :, t, :], in_=den[:], func=ACT.Square, bias=0.1)
+
+        for t in range(PACK):
+            h_ps = product(w3c, w3s, t)
+            nc.scalar.copy(out=h_sb[t][:], in_=h_ps[:])
+
+        inv = keep.tile([P, 4, 2, P, 2], F32)
+        for b in range(4):
+            nc.scalar.activation(
+                out=inv[:, b], in_=den_sq[:, b].rearrange("j (u e) p -> j u p e", e=2), func=ACT.Abs_reciprocal_sqrt
+            )
+
+        w4d = keep.tile([P, N], I32, align_bytes=64)
+        w4s = keep.tile([P, N], U8, align_bytes=64)
+        deal(w4d[:], w4_raw[:], slice(0, 4))
+        deal(w4s[:], w4s_raw[:], slice(0, 4))
+
+        oc = keep.tile([P, S], U32, align_bytes=64)
+        osc = keep.tile([P, S], U8, align_bytes=64)
+        out_rows = out_0.rearrange("(p t) j -> p t j", t=PACK)
+        out_words = out_1[0].rearrange("p n t -> p (n t)").bitcast(I32)
+        starts = [sum(PIECES[:i]) for i in range(len(PIECES))]
+        nums = {}
+        turned = {}
+        packed = {}
+        results = {}
+
+        def messages(k, t):
+            c0, n = starts[k], PIECES[k]
+            msg = slot([P, 2, n], F32)
+            for i in range(2):
+                nc.vector.tensor_tensor(
+                    msg[:, i, :], h_sb[t][:].indirect(p_sb[i][:, c0 // 16 : (c0 + n) // 16]),
+                    gate[t][:, i, c0 : c0 + n], ALU.mult,
+                )
+            for b in range(n // P):
+                g = c0 // P + b
+                if t == 0:
+                    nums[g] = psum.tile([P, PACK, P], F32, tag=f"acc{1 + g % 2}", name="num")
+                blk = slice(b * P, (b + 1) * P)
+                add_turned(nums[g][:, t, :], msg[:, 0, blk], msg[:, 1, blk])
+
+        def normalise(k):
+            c0, n = starts[k], PIECES[k]
+            zt = psum.tile([P, 2, n], F32, tag="zt", name="zt")
+            for b in range(n // P):
+                g = c0 // P + b
+                zb = ring.tile([P, 2, P, 2], BF16, name="zb")
+                nc.vector.tensor_tensor(zb[:], nums[g][:].rearrange("j (u e) p -> j u p e", e=2), inv[:, g], ALU.mult)
+                zwords = zb[:].rearrange("j u p e -> j (u p e)").bitcast(F32)
+                for u in range(2):
+                    nc.tensor.transpose(zt[:, u, b * P : (b + 1) * P], zwords[:, u * P : (u + 1) * P], ident[:])
+            turned[k] = zt
+
+        def last_layer(k):
+            c0, n = starts[k], PIECES[k]
+            zg = slot([P, n * PACK], BF16)
+            nc.scalar.copy(out=zg[:].bitcast(F32).rearrange("p (j u) -> p j u", u=2), in_=turned[k][:].rearrange("p u j -> p j u"))
+            zc = ring.tile([P, n], U32, name="zc", align_bytes=64)
+            zs = ring.tile([P, n], U8, name="zs", align_bytes=64)
+            nc.vector.quantize_mx(out=zc[:].bitcast(FP8X4), scales=zs[:], in_=zg[:])
+            o_sb = ring.tile([P, PACK, n], F32, name="o_sb")
+            per_bank = 512 // n
+            for t0 in range(0, PACK, per_bank):
+                bank = psum.tile([P, per_bank, n], F32, tag="mm", bufs=4, name="mm")
+                for t in range(t0, t0 + per_bank):
+                    wc = slice(t * P, (t + 1) * P)
+                    nc.tensor.matmul_mx(
+                        out=bank[:, t - t0, :], lhsT=w4d[:, wc].bitcast(FP8X4), lhsT_scale=w4s[:, wc],
+                        rhs=zc[:].bitcast(FP8X4), rhs_scale=zs[:], start=True, stop=True,
+                    )
+                nc.scalar.copy(out=o_sb[:, t0 : t0 + per_bank, :], in_=bank[:])
+            nc.sync.dma_start(out=out_rows[:, :, c0 : c0 + n], in_=o_sb[:])
+            results[k] = o_sb
+
+        def planes(k):
+            c0, n = starts[k], PIECES[k]
+            cols = slice(c0, c0 + n)
+            ob = ring.tile([P, n, PACK], BF16, name="ob", align_bytes=64)
+            if c0 + n < S:
+                nc.scalar.copy(out=ob[:], in_=results[k][:].rearrange("p t j -> p j t"))
+            else:
+                nc.vector.tensor_copy(out=ob[:], in_=results[k][:].rearrange("p t j -> p j t"))
+            nc.vector.quantize_mx(out=oc[:, cols].bitcast(FP8X4), scales=osc[:, cols], in_=ob[:].rearrange("p j t -> p (j t)"))
+            nc.sync.dma_start(out=out_words[:, cols], in_=oc[:, cols].bitcast(I32))
+
+        for t in range(PACK):
+            messages(0, t)
+        normalise(0)
+        messages(1, 0)
+        messages(1, 1)
+        last_layer(0)
+        messages(1, 2)
+        messages(1, 3)
+        normalise(1)
+        messages(2, 0)
+        messages(2, 1)
+        last_layer(1)
+        planes(0)
+        messages(2, 2)
+        messages(2, 3)
+        normalise(2)
+        planes(1)
+        last_layer(2)
+        planes(2)
+        out_planes = out_2[0].bitcast(I32)
+        for q in range(4):
+            engine = nc.sync if q % 2 == 0 else nc.scalar
+            engine.dma_start(out=out_planes[4 * q : 4 * q + 4, :], in_=osc[32 * q : 32 * q + 4, :].bitcast(I32))

@@ -43,10 +43,16 @@ def tile_picked_ggnorm_none_po_kernel(
             in_=rows.unsqueeze(0).broadcast_to([8, 4, rows.shape[1]]),
         )
 
-    def deal(out, in_, ts):
+    def deal_runs(out, in_, ts):
         nc.vector.tensor_copy(
-            out=out.rearrange("p (t m) -> p t m", t=PACK)[:, ts, :],
-            in_=in_.rearrange("p (m t) -> p t m", t=PACK)[:, ts, :],
+            out=out.bitcast(I32).rearrange("p (t g r) -> p t g r", t=PACK, g=8)[:, ts],
+            in_=in_.bitcast(I32).rearrange("p (g t r) -> p t g r", t=PACK, g=8)[:, ts],
+        )
+
+    def deal(out, in_):
+        nc.vector.tensor_copy(
+            out=out.rearrange("p (t m) -> p m t", t=PACK),
+            in_=in_.rearrange("p (m t) -> p m t", t=PACK),
         )
 
     with ExitStack() as ctx:
@@ -66,8 +72,12 @@ def tile_picked_ggnorm_none_po_kernel(
 
         nc.vector.memset(xs[:].bitcast(I32), 0)
         nc.vector.memset(warm[:], 0.0)
+        e_sb = [keep.tile([P, 2 * S], F32, name=f"e_sb{i}") for i in range(2)]
+        for i in range(2):
+            nc.vector.memset(e_sb[i][:, S : 2 * S], 0.0)
         nc.scalar.activation(out=warm[:], in_=warm[:], func=ACT.Sigmoid)
 
+        load_scale_quadrant(nc.gpsimd, w1s_raw, w1_scales, 3)
         nc.sync.dma_start(offs_sb[:], offs)
         load_scale_quadrant(nc.sync, w2s_raw, w2_scales, 0)
         load_scale_quadrant(nc.sync, w2s_raw, w2_scales, 1)
@@ -79,7 +89,6 @@ def tile_picked_ggnorm_none_po_kernel(
             load_scale_quadrant(nc.sync, w1s_raw, w1_scales, q)
         nc.sync.dma_start(out=w2_raw[:], in_=words_of(w2_words))
         nc.sync.dma_start(out=w1_raw[:], in_=words_of(w1_words))
-        load_scale_quadrant(nc.sync, w1s_raw, w1_scales, 3)
         nc.sync.dma_start(p_sb[0][:], p1)
         nc.sync.dma_start(p_sb[1][:], p2)
 
@@ -89,17 +98,17 @@ def tile_picked_ggnorm_none_po_kernel(
         xg_s = keep.tile([P, S], U8, align_bytes=64)
         xg_w = keep.tile([P, S], U32, align_bytes=64)
         nc.vector.tensor_copy(out=xg_s[:], in_=xs[:].indirect(offs_sb[:]))
-        nc.vector.tensor_copy(out=xg_w[:], in_=xw[:].indirect(offs_sb[:]))
-
         w1s = keep.tile([P, H], U8, align_bytes=64)
         w2s = keep.tile([P, H], U8, align_bytes=64)
         w1d = keep.tile([P, H], I32, align_bytes=64)
         w2d = keep.tile([P, H], I32, align_bytes=64)
-        for ts in (slice(0, 2), slice(2, 4)):
-            deal(w2s[:], w2s_raw[:], ts)
-            deal(w2d[:], w2_raw[:], ts)
-            deal(w1s[:], w1s_raw[:], ts)
-            deal(w1d[:], w1_raw[:], ts)
+        for c in range(0, S, HALF):
+            nc.vector.tensor_copy(out=xg_w[:, c : c + HALF], in_=xw[:].indirect(offs_sb[:, c // 16 : (c + HALF) // 16]))
+        for ts in (slice(0, 1), slice(1, 4)):
+            deal_runs(w2s[:], w2s_raw[:], ts)
+            deal_runs(w2d[:], w2_raw[:], ts)
+            deal_runs(w1s[:], w1s_raw[:], ts)
+            deal_runs(w1d[:], w1_raw[:], ts)
 
         w3_raw = keep.tile([P, PACK, H], F32, align_bytes=64, tag="big")
         nc.sync.dma_start(out=w3_raw[:], in_=w3.rearrange("(p j) c -> p j c", j=PACK))
@@ -109,12 +118,12 @@ def tile_picked_ggnorm_none_po_kernel(
         for q in range(4):
             load_scale_quadrant(nc.sync, w4s_raw, w4_scales, q)
 
-        def product(codes, plane, t):
-            bank = psum.tile([P, S], F32, tag="mm", bufs=4, name="mm")
+        def product(codes, plane, t, c0=0, n=S, tag="mm"):
+            bank = psum.tile([P, n], F32, tag=tag, bufs=4 if tag == "mm" else 1, name="mm")
             cols = slice(t * P, (t + 1) * P)
             nc.tensor.matmul_mx(
                 out=bank[:], lhsT=codes[:, cols].bitcast(FP8X4), lhsT_scale=plane[:, cols],
-                rhs=xg_w[:].bitcast(FP8X4), rhs_scale=xg_s[:], start=True, stop=True,
+                rhs=xg_w[:, c0 : c0 + n].bitcast(FP8X4), rhs_scale=xg_s[:, c0 : c0 + n], start=True, stop=True,
             )
             return bank
 
@@ -134,55 +143,60 @@ def tile_picked_ggnorm_none_po_kernel(
         h_sb = [keep.tile([P, S], F32, name=f"h_sb{t}") for t in range(PACK)]
 
         def values():
-            w3b = slot([P, PACK, P, PACK], BF16)
-            nc.vector.tensor_copy(
-                out=w3b[:].rearrange("p t m j -> p m j t"),
-                in_=w3_raw[:].rearrange("p j (m t) -> p m j t", t=PACK),
-            )
-            nc.vector.quantize_mx(out=w3c[:].bitcast(FP8X4), scales=w3s[:], in_=w3b[:].rearrange("p t m j -> p (t m j)"))
+            w3b = slot([P, PACK, 8, 16, PACK], BF16)
+            raw = w3_raw[:].rearrange("p j (g t r) -> p t g r j", t=PACK, g=8)
+            nc.scalar.copy(out=w3b[:, 0:2], in_=raw[:, 0:2])
+            nc.vector.tensor_copy(out=w3b[:, 2:4], in_=raw[:, 2:4])
+            nc.vector.quantize_mx(out=w3c[:].bitcast(FP8X4), scales=w3s[:], in_=w3b[:].rearrange("p t g r j -> p (t g r j)"))
 
         gate = [keep.tile([P, 2, S], F32, name=f"gate{t}") for t in range(PACK)]
-        den_sq = keep.tile([P, 4, PACK, P], F32)
+        den_sq = keep.tile([P, 4, 8, PACK, 16], F32)
         for t in range(PACK):
             if t == 3:
                 values()
-            e_sb = ring.tile([P, S], F32, name="e_sb")
+            e_win = e_sb[t % 2]
             y_sb = ring.tile([P, S], F32, name="y_sb")
-            e_ps = product(w2d, w2s, t)
-            y_ps = product(w1d, w1s, t)
-            nc.scalar.copy(out=e_sb[:], in_=e_ps[:])
             if t == 0:
-                nc.vector.tensor_copy(out=y_sb[:], in_=y_ps[:])
+                for c, tag in ((0, "acc0"), (HALF, "acc1")):
+                    e_ps = product(w2d, w2s, t, c, HALF, tag)
+                    nc.scalar.copy(out=e_win[:, c : c + HALF], in_=e_ps[:])
+                y_ps = product(w1d, w1s, t, 0, HALF, "acc2")
+                nc.vector.tensor_copy(out=y_sb[:, 0:HALF], in_=y_ps[:])
+                y_ps = product(w1d, w1s, t, HALF, HALF, "zt")
+                nc.scalar.copy(out=y_sb[:, HALF:S], in_=y_ps[:])
             else:
+                e_ps = product(w2d, w2s, t)
+                y_ps = product(w1d, w1s, t)
+                nc.scalar.copy(out=e_win[:, 0:S], in_=e_ps[:])
                 nc.scalar.copy(out=y_sb[:], in_=y_ps[:])
             key = slot([P, 2, S], F32)
             for i in range(2):
-                for c in range(0, S, HALF):
+                n = HALF if t == 0 and i == 0 else S
+                for c in range(0, S, n):
                     nc.vector.tensor_tensor(
-                        key[:, i, c : c + HALF], e_sb[:].indirect(p_sb[i][:, c // 16 : (c + HALF) // 16]),
-                        y_sb[:, c : c + HALF], ALU.add,
+                        key[:, i, c : c + n], e_win[:].indirect(p_sb[i][:, c // 16 : (c + n) // 16]), y_sb[:, c : c + n], ALU.add
                     )
                 nc.scalar.activation(out=gate[t][:, i, :], in_=key[:, i, :], func=ACT.Sigmoid, scale=3.0)
             den = psum.tile([P, 4, P], F32, tag=f"acc{t % 3}", name="den")
             for b in range(4):
                 blk = slice(b * P, (b + 1) * P)
                 add_turned(den[:, b, :], gate[t][:, 0, blk], gate[t][:, 1, blk])
-            nc.scalar.activation(out=den_sq[:, :, t, :], in_=den[:], func=ACT.Square, bias=0.1)
+            nc.scalar.activation(
+                out=den_sq[:, :, :, t, :], in_=den[:].rearrange("j b (g r) -> j b g r", g=8), func=ACT.Square, bias=0.1
+            )
 
         for t in range(PACK):
             h_ps = product(w3c, w3s, t)
             nc.scalar.copy(out=h_sb[t][:], in_=h_ps[:])
 
-        inv = keep.tile([P, 4, 2, P, 2], F32)
+        inv = keep.tile([P, 4, 8, PACK, 16], F32)
         for b in range(4):
-            nc.scalar.activation(
-                out=inv[:, b], in_=den_sq[:, b].rearrange("j (u e) p -> j u p e", e=2), func=ACT.Abs_reciprocal_sqrt
-            )
+            nc.scalar.activation(out=inv[:, b], in_=den_sq[:, b], func=ACT.Abs_reciprocal_sqrt)
 
         w4d = keep.tile([P, N], I32, align_bytes=64)
         w4s = keep.tile([P, N], U8, align_bytes=64)
-        deal(w4d[:], w4_raw[:], slice(0, 4))
-        deal(w4s[:], w4s_raw[:], slice(0, 4))
+        deal(w4d[:], w4_raw[:])
+        deal(w4s[:], w4s_raw[:])
 
         oc = keep.tile([P, S], U32, align_bytes=64)
         osc = keep.tile([P, S], U8, align_bytes=64)
@@ -214,11 +228,11 @@ def tile_picked_ggnorm_none_po_kernel(
             zt = psum.tile([P, 2, n], F32, tag="zt", name="zt")
             for b in range(n // P):
                 g = c0 // P + b
-                zb = ring.tile([P, 2, P, 2], BF16, name="zb")
-                nc.vector.tensor_tensor(zb[:], nums[g][:].rearrange("j (u e) p -> j u p e", e=2), inv[:, g], ALU.mult)
-                zwords = zb[:].rearrange("j u p e -> j (u p e)").bitcast(F32)
+                zb = ring.tile([P, 8, PACK, 16], BF16, name="zb")
+                nc.vector.tensor_tensor(zb[:], nums[g][:].rearrange("j t (g r) -> j g t r", g=8), inv[:, g], ALU.mult)
+                zwords = zb[:].rearrange("j g t r -> j (g t r)").bitcast(F32)
                 for u in range(2):
-                    nc.tensor.transpose(zt[:, u, b * P : (b + 1) * P], zwords[:, u * P : (u + 1) * P], ident[:])
+                    nc.tensor.transpose(zt[:, u, b * P : (b + 1) * P], zwords[:, u : 2 * P : 2], ident[:])
             turned[k] = zt
 
         def last_layer(k):
@@ -229,7 +243,7 @@ def tile_picked_ggnorm_none_po_kernel(
             zs = ring.tile([P, n], U8, name="zs", align_bytes=64)
             nc.vector.quantize_mx(out=zc[:].bitcast(FP8X4), scales=zs[:], in_=zg[:])
             o_sb = ring.tile([P, PACK, n], F32, name="o_sb")
-            per_bank = 512 // n
+            per_bank = 2
             for t0 in range(0, PACK, per_bank):
                 bank = psum.tile([P, per_bank, n], F32, tag="mm", bufs=4, name="mm")
                 for t in range(t0, t0 + per_bank):

@@ -72,8 +72,8 @@ def tile_picked_ggnorm_none_po_kernel(
 
         nc.vector.memset(xs[:].bitcast(I32), 0)
         nc.vector.memset(warm[:], 0.0)
-        e_sb = [keep.tile([P, 2 * S], F32, name=f"e_sb{i}") for i in range(2)]
-        for i in range(2):
+        e_sb = [keep.tile([P, 2 * S], F32, name=f"e_sb{i}") for i in range(PACK)]
+        for i in range(PACK):
             nc.vector.memset(e_sb[i][:, S : 2 * S], 0.0)
         nc.scalar.activation(out=warm[:], in_=warm[:], func=ACT.Sigmoid)
 
@@ -119,7 +119,7 @@ def tile_picked_ggnorm_none_po_kernel(
             load_scale_quadrant(nc.sync, w4s_raw, w4_scales, q)
 
         def product(codes, plane, t, c0=0, n=S, tag="mm"):
-            bank = psum.tile([P, n], F32, tag=tag, bufs=4 if tag == "mm" else 1, name="mm")
+            bank = psum.tile([P, n], F32, tag=tag, bufs=3 if tag == "mm" else 1, name="mm")
             cols = slice(t * P, (t + 1) * P)
             nc.tensor.matmul_mx(
                 out=bank[:], lhsT=codes[:, cols].bitcast(FP8X4), lhsT_scale=plane[:, cols],
@@ -131,74 +131,104 @@ def tile_picked_ggnorm_none_po_kernel(
             nc.tensor.matmul(bank_cols, lhsT=a, rhs=ident[:], start=True, stop=False, is_transpose=True)
             nc.tensor.matmul(bank_cols, lhsT=b, rhs=ident[:], start=False, stop=True, is_transpose=True)
 
-        order = [0]
-
-        def slot(shape, dtype):
-            tile = keep.tile(shape, dtype, tag=f"slot{order[0] % 3}", name="slot", align_bytes=64)
-            order[0] = order[0] + 1
-            return tile
+        def after(tag, shape, dtype):
+            return keep.tile(shape, dtype, tag=tag, name=tag, align_bytes=64)
 
         w3c = keep.tile([P, H], U32, align_bytes=64)
         w3s = keep.tile([P, H], U8, align_bytes=64)
         h_sb = [keep.tile([P, S], F32, name=f"h_sb{t}") for t in range(PACK)]
 
-        def values():
-            w3b = slot([P, PACK, 8, 16, PACK], BF16)
-            raw = w3_raw[:].rearrange("p j (g t r) -> p t g r j", t=PACK, g=8)
-            nc.scalar.copy(out=w3b[:, 0:2], in_=raw[:, 0:2])
-            nc.vector.tensor_copy(out=w3b[:, 2:4], in_=raw[:, 2:4])
-            nc.vector.quantize_mx(out=w3c[:].bitcast(FP8X4), scales=w3s[:], in_=w3b[:].rearrange("p t g r j -> p (t g r j)"))
-
-        gate = [keep.tile([P, 2, S], F32, name=f"gate{t}") for t in range(PACK)]
-        den_sq = keep.tile([P, 4, 8, PACK, 16], F32)
-        for t in range(PACK):
-            if t == 3:
-                values()
-            e_win = e_sb[t % 2]
-            y_sb = ring.tile([P, S], F32, name="y_sb")
-            if t == 0:
-                for c, tag in ((0, "acc0"), (HALF, "acc1")):
-                    e_ps = product(w2d, w2s, t, c, HALF, tag)
-                    nc.scalar.copy(out=e_win[:, c : c + HALF], in_=e_ps[:])
-                y_ps = product(w1d, w1s, t, 0, HALF, "acc2")
-                nc.vector.tensor_copy(out=y_sb[:, 0:HALF], in_=y_ps[:])
-                y_ps = product(w1d, w1s, t, HALF, HALF, "zt")
-                nc.scalar.copy(out=y_sb[:, HALF:S], in_=y_ps[:])
-            else:
-                e_ps = product(w2d, w2s, t)
-                y_ps = product(w1d, w1s, t)
-                nc.scalar.copy(out=e_win[:, 0:S], in_=e_ps[:])
-                nc.scalar.copy(out=y_sb[:], in_=y_ps[:])
-            key = slot([P, 2, S], F32)
-            for i in range(2):
-                n = HALF if t == 0 and i == 0 else S
-                for c in range(0, S, n):
-                    nc.vector.tensor_tensor(
-                        key[:, i, c : c + n], e_win[:].indirect(p_sb[i][:, c // 16 : (c + n) // 16]), y_sb[:, c : c + n], ALU.add
-                    )
-                nc.scalar.activation(out=gate[t][:, i, :], in_=key[:, i, :], func=ACT.Sigmoid, scale=3.0)
-            den = psum.tile([P, 4, P], F32, tag=f"acc{t % 3}", name="den")
-            for b in range(4):
-                blk = slice(b * P, (b + 1) * P)
-                add_turned(den[:, b, :], gate[t][:, 0, blk], gate[t][:, 1, blk])
-            nc.scalar.activation(
-                out=den_sq[:, :, :, t, :], in_=den[:].rearrange("j b (g r) -> j b g r", g=8), func=ACT.Square, bias=0.1
+        def quantise_values(half, copy, tag):
+            cols = slice(half * HALF, (half + 1) * HALF)
+            w3b = after(tag, [P, 2, 8, 16, PACK], BF16)
+            copy(out=w3b[:], in_=w3_raw[:].rearrange("p j (g t r) -> p t g r j", t=PACK, g=8)[:, 2 * half : 2 * half + 2])
+            nc.vector.quantize_mx(
+                out=w3c[:, cols].bitcast(FP8X4), scales=w3s[:, cols], in_=w3b[:].rearrange("p t g r j -> p (t g r j)")
             )
 
-        for t in range(PACK):
+        def values(t):
             h_ps = product(w3c, w3s, t)
             nc.scalar.copy(out=h_sb[t][:], in_=h_ps[:])
 
-        inv = keep.tile([P, 4, 8, PACK, 16], F32)
-        for b in range(4):
-            nc.scalar.activation(out=inv[:, b], in_=den_sq[:, b], func=ACT.Abs_reciprocal_sqrt)
+        gate = [after(f"gate{t}", [P, 2, S], F32) for t in range(PACK)]
+        y_sb = [keep.tile([P, S], F32, name=f"y_sb{t}") for t in range(PACK)]
+        dens = {}
+        den_sq = {}
+
+        def square(t):
+            den_sq[t] = keep.tile([P, 4, P], F32, name=f"den_sq{t}")
+            nc.scalar.activation(out=den_sq[t][:], in_=dens[t][:], func=ACT.Square, bias=0.1)
+
+        def gates(t, i, tag):
+            key = after(tag, [P, S], F32)
+            n = HALF if t == 0 and i == 0 else S
+            for c in range(0, S, n):
+                nc.vector.tensor_tensor(
+                    key[:, c : c + n], e_sb[t][:].indirect(p_sb[i][:, c // 16 : (c + n) // 16]), y_sb[t][:, c : c + n], ALU.add
+                )
+            nc.scalar.activation(out=gate[t][:, i, :], in_=key[:], func=ACT.Sigmoid, scale=3.0)
+
+        def gate_sums(t):
+            dens[t] = psum.tile([P, 4, P], F32, tag=f"acc{t}", name="den")
+            for b in range(4):
+                blk = slice(b * P, (b + 1) * P)
+                add_turned(dens[t][:, b, :], gate[t][:, 0, blk], gate[t][:, 1, blk])
+
+        for c, tag in ((0, "acc0"), (HALF, "acc1")):
+            e_ps = product(w2d, w2s, 0, c, HALF, tag)
+            nc.scalar.copy(out=e_sb[0][:, c : c + HALF], in_=e_ps[:])
+        y_ps = product(w1d, w1s, 0, 0, HALF, "acc2")
+        nc.vector.tensor_copy(out=y_sb[0][:, 0:HALF], in_=y_ps[:])
+        y_ps = product(w1d, w1s, 0, HALF, HALF, "acc3")
+        nc.scalar.copy(out=y_sb[0][:, HALF:S], in_=y_ps[:])
+        def keys(codes, plane, t, out, tag="mm"):
+            nc.scalar.copy(out=out, in_=product(codes, plane, t, 0, S, tag)[:])
+
+        for t in (1, 2):
+            keys(w2d, w2s, t, e_sb[t][:, 0:S], f"acc{t + 1}")
+            keys(w1d, w1s, t, y_sb[t][:])
+        gates(0, 0, "k00")
+        keys(w2d, w2s, 3, e_sb[3][:, 0:S], "acc2")
+        gates(0, 1, "k10")
+        keys(w1d, w1s, 3, y_sb[3][:])
+        gate_sums(0)
+        quantise_values(1, nc.scalar.copy, "g")
+        gates(1, 0, "k01")
+        quantise_values(0, nc.vector.tensor_copy, "k00")
+        gates(1, 1, "k11")
+        square(0)
+        gate_sums(1)
+        values(0)
+        values(1)
+        gates(2, 0, "k02")
+        gates(2, 1, "k12")
+        gate_sums(2)
+        gates(3, 0, "c")
+        square(1)
+        gates(3, 1, "g")
+        values(2)
+        values(3)
+        gate_sums(3)
+
+        inv = {}
+
+        def inverses(half, tag):
+            inv[half] = after(tag, [P, 2, 8, PACK, 16], F32)
+            for t in range(PACK):
+                if t == 2 and half == 0:
+                    square(2)
+                    square(3)
+                nc.scalar.activation(
+                    out=inv[half][:, :, :, t, :],
+                    in_=den_sq[t][:, 2 * half : 2 * half + 2].rearrange("j b (g r) -> j b g r", g=8),
+                    func=ACT.Abs_reciprocal_sqrt,
+                )
 
         w4d = keep.tile([P, N], I32, align_bytes=64)
         w4s = keep.tile([P, N], U8, align_bytes=64)
         deal(w4d[:], w4_raw[:])
         deal(w4s[:], w4s_raw[:])
 
-        oc = keep.tile([P, S], U32, align_bytes=64)
         osc = keep.tile([P, S], U8, align_bytes=64)
         out_rows = out_0.rearrange("(p t) j -> p t j", t=PACK)
         out_words = out_1[0].rearrange("p n t -> p (n t)").bitcast(I32)
@@ -208,9 +238,14 @@ def tile_picked_ggnorm_none_po_kernel(
         packed = {}
         results = {}
 
-        def messages(k, t):
+        def sum_banks(g):
+            if g < 3:
+                return [(slice(0, PACK), f"acc{g % 2}")]
+            return [(slice(0, 3), "acc1"), (slice(3, PACK), "acc2")]
+
+        def messages(k, t, tag):
             c0, n = starts[k], PIECES[k]
-            msg = slot([P, 2, n], F32)
+            msg = after(tag, [P, 2, n], F32)
             for i in range(2):
                 nc.vector.tensor_tensor(
                     msg[:, i, :], h_sb[t][:].indirect(p_sb[i][:, c0 // 16 : (c0 + n) // 16]),
@@ -218,34 +253,40 @@ def tile_picked_ggnorm_none_po_kernel(
                 )
             for b in range(n // P):
                 g = c0 // P + b
-                if t == 0:
-                    nums[g] = psum.tile([P, PACK, P], F32, tag=f"acc{1 + g % 2}", name="num")
-                blk = slice(b * P, (b + 1) * P)
-                add_turned(nums[g][:, t, :], msg[:, 0, blk], msg[:, 1, blk])
+                for ts, bank in sum_banks(g):
+                    if t == ts.start:
+                        nums[g, t] = psum.tile([P, ts.stop - ts.start, P], F32, tag=bank, name="num")
+                    if ts.start <= t < ts.stop:
+                        blk = slice(b * P, (b + 1) * P)
+                        add_turned(nums[g, ts.start][:, t - ts.start, :], msg[:, 0, blk], msg[:, 1, blk])
 
-        def normalise(k):
+        def normalise(k, tags):
             c0, n = starts[k], PIECES[k]
             zt = psum.tile([P, 2, n], F32, tag="zt", name="zt")
             for b in range(n // P):
                 g = c0 // P + b
-                zb = ring.tile([P, 8, PACK, 16], BF16, name="zb")
-                nc.vector.tensor_tensor(zb[:], nums[g][:].rearrange("j t (g r) -> j g t r", g=8), inv[:, g], ALU.mult)
+                zb = after(tags[b], [P, 8, PACK, 16], BF16)
+                for ts, bank in sum_banks(g):
+                    nc.vector.tensor_tensor(
+                        zb[:, :, ts, :], nums[g, ts.start][:].rearrange("j t (g r) -> j g t r", g=8),
+                        inv[g // 2][:, g % 2, :, ts, :], ALU.mult,
+                    )
                 zwords = zb[:].rearrange("j g t r -> j (g t r)").bitcast(F32)
                 for u in range(2):
                     nc.tensor.transpose(zt[:, u, b * P : (b + 1) * P], zwords[:, u : 2 * P : 2], ident[:])
             turned[k] = zt
 
-        def last_layer(k):
+        def last_layer(k, tag, code_tag):
             c0, n = starts[k], PIECES[k]
-            zg = slot([P, n * PACK], BF16)
+            zg = after(tag, [P, n * PACK], BF16)
             nc.scalar.copy(out=zg[:].bitcast(F32).rearrange("p (j u) -> p j u", u=2), in_=turned[k][:].rearrange("p u j -> p j u"))
-            zc = ring.tile([P, n], U32, name="zc", align_bytes=64)
+            zc = after(code_tag, [P, n], U32)
             zs = ring.tile([P, n], U8, name="zs", align_bytes=64)
             nc.vector.quantize_mx(out=zc[:].bitcast(FP8X4), scales=zs[:], in_=zg[:])
             o_sb = ring.tile([P, PACK, n], F32, name="o_sb")
             per_bank = 2
             for t0 in range(0, PACK, per_bank):
-                bank = psum.tile([P, per_bank, n], F32, tag="mm", bufs=4, name="mm")
+                bank = psum.tile([P, per_bank, n], F32, tag="mm", bufs=3, name="mm")
                 for t in range(t0, t0 + per_bank):
                     wc = slice(t * P, (t + 1) * P)
                     nc.tensor.matmul_mx(
@@ -256,36 +297,38 @@ def tile_picked_ggnorm_none_po_kernel(
             nc.sync.dma_start(out=out_rows[:, :, c0 : c0 + n], in_=o_sb[:])
             results[k] = o_sb
 
-        def planes(k):
+        def planes(k, copy):
             c0, n = starts[k], PIECES[k]
             cols = slice(c0, c0 + n)
-            ob = ring.tile([P, n, PACK], BF16, name="ob", align_bytes=64)
-            if c0 + n < S:
-                nc.scalar.copy(out=ob[:], in_=results[k][:].rearrange("p t j -> p j t"))
-            else:
-                nc.vector.tensor_copy(out=ob[:], in_=results[k][:].rearrange("p t j -> p j t"))
+            ob = keep.tile([P, n, PACK], BF16, name=f"ob{k}", align_bytes=64)
+            copy(out=ob[:], in_=results[k][:].rearrange("p t j -> p j t"))
             nc.vector.quantize_mx(out=oc[:, cols].bitcast(FP8X4), scales=osc[:, cols], in_=ob[:].rearrange("p j t -> p (j t)"))
             nc.sync.dma_start(out=out_words[:, cols], in_=oc[:, cols].bitcast(I32))
 
-        for t in range(PACK):
-            messages(0, t)
-        normalise(0)
-        messages(1, 0)
-        messages(1, 1)
-        last_layer(0)
-        messages(1, 2)
-        messages(1, 3)
-        normalise(1)
-        messages(2, 0)
-        messages(2, 1)
-        last_layer(1)
-        planes(0)
-        messages(2, 2)
-        messages(2, 3)
-        normalise(2)
-        planes(1)
-        last_layer(2)
-        planes(2)
+        inverses(0, "g")
+        messages(0, 0, "k02")
+        messages(0, 1, "k12")
+        messages(0, 2, "c")
+        messages(0, 3, "m3")
+        inverses(1, "m3")
+        messages(1, 0, "k02")
+        messages(1, 1, "k12")
+        normalise(0, ("z0", "z1"))
+        messages(1, 2, "g")
+        messages(1, 3, "k02")
+        last_layer(0, "q0", "zc0")
+        normalise(1, ("z2",))
+        messages(2, 0, "k12")
+        messages(2, 1, "g")
+        messages(2, 2, "k02")
+        messages(2, 3, "k12")
+        normalise(2, ("z3",))
+        last_layer(1, "q1", "m3")
+        last_layer(2, "q2", "zc2")
+        oc = after("z3", [P, S], U32)
+        planes(0, nc.scalar.copy)
+        planes(1, nc.vector.tensor_copy)
+        planes(2, nc.vector.tensor_copy)
         out_planes = out_2[0].bitcast(I32)
         for q in range(4):
             engine = nc.sync if q % 2 == 0 else nc.scalar

@@ -20,6 +20,7 @@ P = 128
 PACK = 4
 HALF = 256
 PIECES = (256, 128, 128)
+ROW = 4 * S
 
 
 def tile_picked_ggnorm_none_po_kernel(
@@ -31,11 +32,6 @@ def tile_picked_ggnorm_none_po_kernel(
     def words_of(dram):
         return dram[0].rearrange("p n t -> p (n t)").bitcast(I32)
 
-    def load_scale_rows(engine, plane, first, dram):
-        rows = dram[0].bitcast(I32)
-        for q in range(4):
-            engine.dma_start(out=plane[32 * q + first : 32 * q + first + 4, :].bitcast(I32), in_=rows[4 * q : 4 * q + 4, :])
-
     def load_scale_quadrant(engine, plane, dram, q):
         rows = dram[0].bitcast(I32)[4 * q : 4 * q + 4, :]
         engine.dma_start(
@@ -45,7 +41,7 @@ def tile_picked_ggnorm_none_po_kernel(
 
     def deal_runs(out, in_, ts):
         nc.vector.tensor_copy(
-            out=out.bitcast(I32).rearrange("p (t g r) -> p t g r", t=PACK, g=8)[:, ts],
+            out=out.bitcast(I32).rearrange("p (t g r) -> p t g r", t=ts.stop - ts.start, g=8),
             in_=in_.bitcast(I32).rearrange("p (g t r) -> p t g r", t=PACK, g=8)[:, ts],
         )
 
@@ -57,40 +53,44 @@ def tile_picked_ggnorm_none_po_kernel(
 
     with ExitStack() as ctx:
         keep = ctx.enter_context(tc.tile_pool(name="keep", bufs=1))
-        ring = ctx.enter_context(tc.tile_pool(name="ring", bufs=3))
+        turns = ctx.enter_context(tc.tile_pool(name="turns", bufs=1))
         psum = ctx.enter_context(tc.psum_pool(name="psum", bufs=1))
 
         offs_sb = keep.tile([P, S // 16], U16)
         p_sb = [keep.tile([P, S // 16], U16, name=f"p{i}_sb") for i in (1, 2)]
-        xw = keep.tile([P, T], U32, align_bytes=64, tag="big")
+        xw = keep.tile([P, T], U32, align_bytes=64)
         xs = keep.tile([P, T], U8, align_bytes=64)
-        w1s_raw = keep.tile([P, H], U8, align_bytes=64)
-        w2s_raw = keep.tile([P, H], U8, align_bytes=64, tag="sraw")
+        w1s_raw = turns.tile([P, H], U8, offset=15 * ROW, align_bytes=64)
+        w2s_raw = keep.tile([P, H], U8, align_bytes=64)
         w1_raw = keep.tile([P, H], I32, align_bytes=64)
-        w2_raw = keep.tile([P, H], I32, align_bytes=64, tag="wraw")
+        w2_raw = keep.tile([P, H], I32, align_bytes=64)
         warm = keep.tile([P, 8], F32)
 
-        nc.vector.memset(xs[:].bitcast(I32), 0)
         nc.vector.memset(warm[:], 0.0)
-        e_sb = [keep.tile([P, 2 * S], F32, name=f"e_sb{i}") for i in range(PACK)]
-        for i in range(PACK):
-            nc.vector.memset(e_sb[i][:, S : 2 * S], 0.0)
+        e_sb = [turns.tile([P, S], F32, name="e_sb0", offset=14 * ROW, align_bytes=64)]
+        e_sb.extend(keep.tile([P, 2 * S], F32, name=f"e_sb{t}") for t in range(1, PACK))
+        y_last = keep.tile([P, S], F32)
         nc.scalar.activation(out=warm[:], in_=warm[:], func=ACT.Sigmoid)
 
-        load_scale_quadrant(nc.gpsimd, w1s_raw, w1_scales, 3)
         nc.sync.dma_start(offs_sb[:], offs)
-        load_scale_quadrant(nc.sync, w2s_raw, w2_scales, 0)
-        load_scale_quadrant(nc.sync, w2s_raw, w2_scales, 1)
-        load_scale_rows(nc.sync, xs, 0, x_scales)
+        for q in range(4):
+            load_scale_quadrant(nc.sync, xs, x_scales, q)
         nc.sync.dma_start(out=xw[:].bitcast(I32), in_=words_of(x_words))
-        load_scale_quadrant(nc.sync, w2s_raw, w2_scales, 2)
-        load_scale_quadrant(nc.sync, w2s_raw, w2_scales, 3)
-        for q in range(3):
-            load_scale_quadrant(nc.sync, w1s_raw, w1_scales, q)
+        for q in range(4):
+            load_scale_quadrant(nc.sync, w2s_raw, w2_scales, q)
         nc.sync.dma_start(out=w2_raw[:], in_=words_of(w2_words))
         nc.sync.dma_start(out=w1_raw[:], in_=words_of(w1_words))
+        for q in range(4):
+            load_scale_quadrant(nc.sync, w1s_raw, w1_scales, q)
         nc.sync.dma_start(p_sb[0][:], p1)
         nc.sync.dma_start(p_sb[1][:], p2)
+        w3_raw = turns.tile([P, PACK, H], F32, offset=7 * ROW, align_bytes=64)
+        nc.sync.dma_start(out=w3_raw[:], in_=w3.rearrange("(p j) c -> p j c", j=PACK))
+        w4_raw = keep.tile([P, N], I32, align_bytes=64)
+        w4s_raw = keep.tile([P, N], U8, align_bytes=64)
+        nc.sync.dma_start(out=w4_raw[:], in_=words_of(w4_words))
+        for q in range(4):
+            load_scale_quadrant(nc.sync, w4s_raw, w4_scales, q)
 
         ident = keep.tile([P, P], F32)
         make_identity(nc, ident[:])
@@ -101,28 +101,30 @@ def tile_picked_ggnorm_none_po_kernel(
         w1s = keep.tile([P, H], U8, align_bytes=64)
         w2s = keep.tile([P, H], U8, align_bytes=64)
         w1d = keep.tile([P, H], I32, align_bytes=64)
-        w2d = keep.tile([P, H], I32, align_bytes=64)
+        w2d_first = keep.tile([P, P], I32, align_bytes=64)
         for c in range(0, S, HALF):
             nc.vector.tensor_copy(out=xg_w[:, c : c + HALF], in_=xw[:].indirect(offs_sb[:, c // 16 : (c + HALF) // 16]))
-        for ts in (slice(0, 1), slice(1, 4)):
-            deal_runs(w2s[:], w2s_raw[:], ts)
-            deal_runs(w2d[:], w2_raw[:], ts)
-            deal_runs(w1s[:], w1s_raw[:], ts)
-            deal_runs(w1d[:], w1_raw[:], ts)
+        first, rest = slice(0, 1), slice(1, PACK)
+        deal_runs(w2s[:, 0:P], w2s_raw[:], first)
+        deal_runs(w2d_first[:], w2_raw[:], first)
+        deal_runs(w1d[:, 0:P], w1_raw[:], first)
+        deal_runs(w1s[:, 0:P], w1s_raw[:], first)
+        deal_runs(w1s[:, P:H], w1s_raw[:], rest)
+        deal_runs(w2s[:, P:H], w2s_raw[:], rest)
+        deal_runs(w1d[:, P:H], w1_raw[:], rest)
+        w2d_rest = turns.tile([P, H - P], I32, offset=15 * ROW, align_bytes=64)
+        deal_runs(w2d_rest[:], w2_raw[:], rest)
+        w2d = [w2d_first[:]] + [w2d_rest[:, (t - 1) * P : t * P] for t in range(1, PACK)]
+        w1d = [w1d[:, t * P : (t + 1) * P] for t in range(PACK)]
 
-        w3_raw = keep.tile([P, PACK, H], F32, align_bytes=64, tag="big")
-        nc.sync.dma_start(out=w3_raw[:], in_=w3.rearrange("(p j) c -> p j c", j=PACK))
-        w4_raw = keep.tile([P, N], I32, align_bytes=64, tag="wraw")
-        w4s_raw = keep.tile([P, N], U8, align_bytes=64, tag="sraw")
-        nc.sync.dma_start(out=w4_raw[:], in_=words_of(w4_words))
-        for q in range(4):
-            load_scale_quadrant(nc.sync, w4s_raw, w4_scales, q)
+        def bank_tile(b, shape):
+            return psum.tile(shape, F32, tag=f"bank{b}", name=f"bank{b}")
 
-        def product(codes, plane, t, c0=0, n=S, tag="mm"):
-            bank = psum.tile([P, n], F32, tag=tag, bufs=3 if tag == "mm" else 1, name="mm")
+        def product(codes, plane, t, b, c0=0, n=S):
+            bank = bank_tile(b, [P, n])
             cols = slice(t * P, (t + 1) * P)
             nc.tensor.matmul_mx(
-                out=bank[:], lhsT=codes[:, cols].bitcast(FP8X4), lhsT_scale=plane[:, cols],
+                out=bank[:], lhsT=codes[t].bitcast(FP8X4), lhsT_scale=plane[:, cols],
                 rhs=xg_w[:, c0 : c0 + n].bitcast(FP8X4), rhs_scale=xg_s[:, c0 : c0 + n], start=True, stop=True,
             )
             return bank
@@ -131,121 +133,133 @@ def tile_picked_ggnorm_none_po_kernel(
             nc.tensor.matmul(bank_cols, lhsT=a, rhs=ident[:], start=True, stop=False, is_transpose=True)
             nc.tensor.matmul(bank_cols, lhsT=b, rhs=ident[:], start=False, stop=True, is_transpose=True)
 
-        def after(tag, shape, dtype):
-            return keep.tile(shape, dtype, tag=tag, name=tag, align_bytes=64)
+        def placed(name, row, shape, dtype):
+            return turns.tile(shape, dtype, name=name, offset=row * ROW, align_bytes=64)
+
+        key_place = {(0, 0): (0, 1), (1, 0): (2, 2), (3, 1): (4, 5), (0, 1): (1, 1), (1, 1): (12, 1), (2, 0): (13, 1), (2, 1): (10, 1), (3, 0): (9, 1)}
 
         w3c = keep.tile([P, H], U32, align_bytes=64)
         w3s = keep.tile([P, H], U8, align_bytes=64)
+        w3d = [w3c[:, t * P : (t + 1) * P] for t in range(PACK)]
         h_sb = [keep.tile([P, S], F32, name=f"h_sb{t}") for t in range(PACK)]
+        gate = [keep.tile([P, 2, S], F32, name=f"gate{t}") for t in range(PACK)]
+        y_sb = [e_sb[t + 1][:, S : 2 * S] for t in range(PACK - 1)] + [y_last[:]]
+        den_sq = keep.tile([P, 4, 8, PACK, 16], F32)
+        w3b = {}
+        key = {}
+        dens = {}
+        inv = {}
 
-        def quantise_values(half, copy, tag):
+        def round_values(half, copy):
+            w3b[half] = placed(f"w3b{half}", 14 if half == 0 else 0, [P, 2, 8, 16, PACK], BF16)
+            copy(out=w3b[half][:], in_=w3_raw[:].rearrange("p j (g t r) -> p t g r j", t=PACK, g=8)[:, 2 * half : 2 * half + 2])
+
+        def quantise_values(half):
             cols = slice(half * HALF, (half + 1) * HALF)
-            w3b = after(tag, [P, 2, 8, 16, PACK], BF16)
-            copy(out=w3b[:], in_=w3_raw[:].rearrange("p j (g t r) -> p t g r j", t=PACK, g=8)[:, 2 * half : 2 * half + 2])
             nc.vector.quantize_mx(
-                out=w3c[:, cols].bitcast(FP8X4), scales=w3s[:, cols], in_=w3b[:].rearrange("p t g r j -> p (t g r j)")
+                out=w3c[:, cols].bitcast(FP8X4), scales=w3s[:, cols], in_=w3b[half][:].rearrange("p t g r j -> p (t g r j)")
             )
 
-        def values(t):
-            h_ps = product(w3c, w3s, t)
-            nc.scalar.copy(out=h_sb[t][:], in_=h_ps[:])
+        def emptied(codes, plane, t, out, b):
+            nc.scalar.copy(out=out, in_=product(codes, plane, t, b)[:])
 
-        gate = [after(f"gate{t}", [P, 2, S], F32) for t in range(PACK)]
-        y_sb = [keep.tile([P, S], F32, name=f"y_sb{t}") for t in range(PACK)]
-        dens = {}
-        den_sq = {}
-
-        def square(t):
-            den_sq[t] = keep.tile([P, 4, P], F32, name=f"den_sq{t}")
-            nc.scalar.activation(out=den_sq[t][:], in_=dens[t][:], func=ACT.Square, bias=0.1)
-
-        def gates(t, i, tag):
-            key = after(tag, [P, S], F32)
-            n = HALF if t == 0 and i == 0 else S
+        def keys(t, i):
+            row, rows = key_place[t, i]
+            key[t, i] = placed(f"key{t}{i}", row, [P, rows * S], F32)
+            n = HALF if t == 0 else S
             for c in range(0, S, n):
                 nc.vector.tensor_tensor(
-                    key[:, c : c + n], e_sb[t][:].indirect(p_sb[i][:, c // 16 : (c + n) // 16]), y_sb[t][:, c : c + n], ALU.add
+                    key[t, i][:, c : c + n], e_sb[t][:].indirect(p_sb[i][:, c // 16 : (c + n) // 16]), y_sb[t][:, c : c + n], ALU.add
                 )
-            nc.scalar.activation(out=gate[t][:, i, :], in_=key[:], func=ACT.Sigmoid, scale=3.0)
+
+        def gates(t, i):
+            nc.scalar.activation(out=gate[t][:, i, :], in_=key[t, i][:, 0:S], func=ACT.Sigmoid, scale=3.0)
 
         def gate_sums(t):
-            dens[t] = psum.tile([P, 4, P], F32, tag=f"acc{t}", name="den")
+            dens[t] = bank_tile(t, [P, 4, P])
             for b in range(4):
                 blk = slice(b * P, (b + 1) * P)
                 add_turned(dens[t][:, b, :], gate[t][:, 0, blk], gate[t][:, 1, blk])
 
-        for c, tag in ((0, "acc0"), (HALF, "acc1")):
-            e_ps = product(w2d, w2s, 0, c, HALF, tag)
-            nc.scalar.copy(out=e_sb[0][:, c : c + HALF], in_=e_ps[:])
-        y_ps = product(w1d, w1s, 0, 0, HALF, "acc2")
-        nc.vector.tensor_copy(out=y_sb[0][:, 0:HALF], in_=y_ps[:])
-        y_ps = product(w1d, w1s, 0, HALF, HALF, "acc3")
-        nc.scalar.copy(out=y_sb[0][:, HALF:S], in_=y_ps[:])
-        def keys(codes, plane, t, out, tag="mm"):
-            nc.scalar.copy(out=out, in_=product(codes, plane, t, 0, S, tag)[:])
+        def square(t):
+            nc.scalar.activation(
+                out=den_sq[:, :, :, t, :], in_=dens[t][:].rearrange("j b (g r) -> j b g r", g=8), func=ACT.Square, bias=0.1
+            )
 
-        for t in (1, 2):
-            keys(w2d, w2s, t, e_sb[t][:, 0:S], f"acc{t + 1}")
-            keys(w1d, w1s, t, y_sb[t][:])
-        gates(0, 0, "k00")
-        keys(w2d, w2s, 3, e_sb[3][:, 0:S], "acc2")
-        gates(0, 1, "k10")
-        keys(w1d, w1s, 3, y_sb[3][:])
+        def inverse(b, ts=slice(0, PACK)):
+            if ts.start == 0:
+                inv[b] = placed(f"inv{b}", 4 + b, [P, 8, PACK, 16], F32)
+            nc.scalar.activation(out=inv[b][:, :, ts, :], in_=den_sq[:, b, :, ts, :], func=ACT.Abs_reciprocal_sqrt)
+
+        for c, b in ((0, 0), (HALF, 1)):
+            nc.scalar.copy(out=e_sb[0][:, c : c + HALF], in_=product(w2d, w2s, 0, b, c, HALF)[:])
+        nc.vector.tensor_copy(out=y_sb[0][:, 0:HALF], in_=product(w1d, w1s, 0, 2, 0, HALF)[:])
+        nc.scalar.copy(out=y_sb[0][:, HALF:S], in_=product(w1d, w1s, 0, 3, HALF, HALF)[:])
+        emptied(w1d, w1s, 1, y_sb[1], 4)
+        emptied(w1d, w1s, 2, y_sb[2], 5)
+        emptied(w2d, w2s, 1, e_sb[1][:, 0:S], 6)
+        emptied(w2d, w2s, 2, e_sb[2][:, 0:S], 7)
+        keys(0, 0)
+        keys(0, 1)
+        round_values(0, nc.vector.tensor_copy)
+        keys(1, 0)
+        keys(1, 1)
+        quantise_values(0)
+        gates(0, 0)
+        gates(0, 1)
         gate_sums(0)
-        quantise_values(1, nc.scalar.copy, "g")
-        gates(1, 0, "k01")
-        quantise_values(0, nc.vector.tensor_copy, "k00")
-        gates(1, 1, "k11")
-        square(0)
+        emptied(w2d, w2s, 3, e_sb[3][:, 0:S], 4)
+        emptied(w1d, w1s, 3, y_sb[3], 5)
+        round_values(1, nc.scalar.copy)
+        gates(1, 0)
+        gates(1, 1)
         gate_sums(1)
-        values(0)
-        values(1)
-        gates(2, 0, "k02")
-        gates(2, 1, "k12")
-        gate_sums(2)
-        gates(3, 0, "c")
-        square(1)
-        gates(3, 1, "g")
-        values(2)
-        values(3)
-        gate_sums(3)
-
-        inv = {}
-
-        def inverses(half, tag):
-            inv[half] = after(tag, [P, 2, 8, PACK, 16], F32)
-            for t in range(PACK):
-                if t == 2 and half == 0:
-                    square(2)
-                    square(3)
-                nc.scalar.activation(
-                    out=inv[half][:, :, :, t, :],
-                    in_=den_sq[t][:, 2 * half : 2 * half + 2].rearrange("j b (g r) -> j b g r", g=8),
-                    func=ACT.Abs_reciprocal_sqrt,
-                )
-
-        w4d = keep.tile([P, N], I32, align_bytes=64)
-        w4s = keep.tile([P, N], U8, align_bytes=64)
+        keys(2, 0)
+        quantise_values(1)
+        keys(2, 1)
+        keys(3, 0)
+        w4d = placed("w4d", 2, [P, N], I32)
+        w4s = placed("w4s", 3, [P, N], U8)
         deal(w4d[:], w4_raw[:])
         deal(w4s[:], w4s_raw[:])
+        keys(3, 1)
+        emptied(w3d, w3s, 0, h_sb[0][:], 6)
+        gates(2, 0)
+        square(0)
+        gates(2, 1)
+        gate_sums(2)
+        emptied(w3d, w3s, 1, h_sb[1][:], 7)
+        square(1)
+        gates(3, 0)
+        square(2)
+        gates(3, 1)
+        gate_sums(3)
+        emptied(w3d, w3s, 2, h_sb[2][:], 4)
+        emptied(w3d, w3s, 3, h_sb[3][:], 5)
+        inverse(0, slice(0, 3))
+        square(3)
+        inverse(0, slice(3, PACK))
+        for b in range(1, 4):
+            inverse(b)
 
         osc = keep.tile([P, S], U8, align_bytes=64)
+        oc = keep.tile([P, S], U32, align_bytes=64)
         out_rows = out_0.rearrange("(p t) j -> p t j", t=PACK)
         out_words = out_1[0].rearrange("p n t -> p (n t)").bitcast(I32)
         starts = [sum(PIECES[:i]) for i in range(len(PIECES))]
         nums = {}
-        turned = {}
-        packed = {}
+        rounded = {}
+        grouped = {}
+        codes_z = {}
         results = {}
 
         def sum_banks(g):
             if g < 3:
-                return [(slice(0, PACK), f"acc{g % 2}")]
-            return [(slice(0, 3), "acc1"), (slice(3, PACK), "acc2")]
+                return [(slice(0, PACK), 4 + g)]
+            return [(slice(0, 3), 7), (slice(3, PACK), 0)]
 
-        def messages(k, t, tag):
+        def messages(k, t, msg):
             c0, n = starts[k], PIECES[k]
-            msg = after(tag, [P, 2, n], F32)
             for i in range(2):
                 nc.vector.tensor_tensor(
                     msg[:, i, :], h_sb[t][:].indirect(p_sb[i][:, c0 // 16 : (c0 + n) // 16]),
@@ -255,38 +269,46 @@ def tile_picked_ggnorm_none_po_kernel(
                 g = c0 // P + b
                 for ts, bank in sum_banks(g):
                     if t == ts.start:
-                        nums[g, t] = psum.tile([P, ts.stop - ts.start, P], F32, tag=bank, name="num")
+                        nums[g, t] = bank_tile(bank, [P, ts.stop - ts.start, P])
                     if ts.start <= t < ts.stop:
                         blk = slice(b * P, (b + 1) * P)
                         add_turned(nums[g, ts.start][:, t - ts.start, :], msg[:, 0, blk], msg[:, 1, blk])
 
-        def normalise(k, tags):
+        def message_pair(k, t0, row):
+            msg = placed(f"msg{k}{t0}", row, [P, 2, 2, P], F32)
+            for t in (t0, t0 + 1):
+                messages(k, t, msg[:, t - t0])
+
+        def normalise(k):
             c0, n = starts[k], PIECES[k]
-            zt = psum.tile([P, 2, n], F32, tag="zt", name="zt")
             for b in range(n // P):
                 g = c0 // P + b
-                zb = after(tags[b], [P, 8, PACK, 16], BF16)
+                rounded[g] = keep.tile([P, 8, PACK, 16], BF16, name=f"zb{g}", align_bytes=64)
                 for ts, bank in sum_banks(g):
                     nc.vector.tensor_tensor(
-                        zb[:, :, ts, :], nums[g, ts.start][:].rearrange("j t (g r) -> j g t r", g=8),
-                        inv[g // 2][:, g % 2, :, ts, :], ALU.mult,
+                        rounded[g][:, :, ts, :], nums[g, ts.start][:].rearrange("j t (g r) -> j g t r", g=8),
+                        inv[g][:, :, ts, :], ALU.mult,
                     )
-                zwords = zb[:].rearrange("j g t r -> j (g t r)").bitcast(F32)
+
+        def turn_back(k):
+            c0, n = starts[k], PIECES[k]
+            zt = bank_tile(1 + k, [P, 2, n])
+            for b in range(n // P):
+                zwords = rounded[c0 // P + b][:].rearrange("j g t r -> j (g t r)").bitcast(F32)
                 for u in range(2):
                     nc.tensor.transpose(zt[:, u, b * P : (b + 1) * P], zwords[:, u : 2 * P : 2], ident[:])
-            turned[k] = zt
+            grouped[k] = keep.tile([P, n * PACK], BF16, name=f"zg{k}", align_bytes=64)
+            nc.scalar.copy(out=grouped[k][:].bitcast(F32).rearrange("p (j u) -> p j u", u=2), in_=zt[:].rearrange("p u j -> p j u"))
 
-        def last_layer(k, tag, code_tag):
+        def last_layer(k):
             c0, n = starts[k], PIECES[k]
-            zg = after(tag, [P, n * PACK], BF16)
-            nc.scalar.copy(out=zg[:].bitcast(F32).rearrange("p (j u) -> p j u", u=2), in_=turned[k][:].rearrange("p u j -> p j u"))
-            zc = after(code_tag, [P, n], U32)
-            zs = ring.tile([P, n], U8, name="zs", align_bytes=64)
-            nc.vector.quantize_mx(out=zc[:].bitcast(FP8X4), scales=zs[:], in_=zg[:])
-            o_sb = ring.tile([P, PACK, n], F32, name="o_sb")
+            zc = keep.tile([P, n], U32, name=f"zc{k}", align_bytes=64)
+            zs = keep.tile([P, n], U8, name=f"zs{k}", align_bytes=64)
+            nc.vector.quantize_mx(out=zc[:].bitcast(FP8X4), scales=zs[:], in_=grouped[k][:])
+            o_sb = keep.tile([P, PACK, n], F32, name=f"o_sb{k}")
             per_bank = 2
             for t0 in range(0, PACK, per_bank):
-                bank = psum.tile([P, per_bank, n], F32, tag="mm", bufs=3, name="mm")
+                bank = bank_tile(((4, 5), (6, 1), (2, 4))[k][t0 // per_bank], [P, per_bank, n])
                 for t in range(t0, t0 + per_bank):
                     wc = slice(t * P, (t + 1) * P)
                     nc.tensor.matmul_mx(
@@ -305,28 +327,22 @@ def tile_picked_ggnorm_none_po_kernel(
             nc.vector.quantize_mx(out=oc[:, cols].bitcast(FP8X4), scales=osc[:, cols], in_=ob[:].rearrange("p j t -> p (j t)"))
             nc.sync.dma_start(out=out_words[:, cols], in_=oc[:, cols].bitcast(I32))
 
-        inverses(0, "g")
-        messages(0, 0, "k02")
-        messages(0, 1, "k12")
-        messages(0, 2, "c")
-        messages(0, 3, "m3")
-        inverses(1, "m3")
-        messages(1, 0, "k02")
-        messages(1, 1, "k12")
-        normalise(0, ("z0", "z1"))
-        messages(1, 2, "g")
-        messages(1, 3, "k02")
-        last_layer(0, "q0", "zc0")
-        normalise(1, ("z2",))
-        messages(2, 0, "k12")
-        messages(2, 1, "g")
-        messages(2, 2, "k02")
-        messages(2, 3, "k12")
-        normalise(2, ("z3",))
-        last_layer(1, "q1", "m3")
-        last_layer(2, "q2", "zc2")
-        oc = after("z3", [P, S], U32)
-        planes(0, nc.scalar.copy)
+        for t in range(PACK):
+            messages(0, t, keep.tile([P, 2, HALF], F32, name=f"msg0{t}")[:])
+        message_pair(1, 0, 8)
+        normalise(0)
+        turn_back(0)
+        message_pair(1, 2, 4)
+        message_pair(2, 0, 5)
+        normalise(1)
+        last_layer(0)
+        turn_back(1)
+        message_pair(2, 2, 6)
+        last_layer(1)
+        normalise(2)
+        turn_back(2)
+        last_layer(2)
+        planes(0, nc.vector.tensor_copy)
         planes(1, nc.vector.tensor_copy)
         planes(2, nc.vector.tensor_copy)
         out_planes = out_2[0].bitcast(I32)

@@ -39,17 +39,22 @@ def tile_picked_ggnorm_none_po_kernel(
             in_=rows.unsqueeze(0).broadcast_to([8, 4, rows.shape[1]]),
         )
 
-    def deal_runs(out, in_, ts):
+    def load_scale_rows(plane, dram):
+        rows = dram[0].bitcast(I32)
+        for q in range(4):
+            nc.sync.dma_start(out=plane[32 * q : 32 * q + 4, :].bitcast(I32), in_=rows[4 * q : 4 * q + 4, :])
+
+    def deal(out, in_, ts=slice(0, PACK)):
         nc.vector.tensor_copy(
-            out=out.bitcast(I32).rearrange("p (t g r) -> p t g r", t=ts.stop - ts.start, g=8),
-            in_=in_.bitcast(I32).rearrange("p (g t r) -> p t g r", t=PACK, g=8)[:, ts],
+            out=out.rearrange("p (t m) -> p m t", t=ts.stop - ts.start),
+            in_=in_.rearrange("p (m t) -> p m t", t=PACK)[:, :, ts],
         )
 
-    def deal(out, in_):
-        nc.vector.tensor_copy(
-            out=out.rearrange("p (t m) -> p m t", t=PACK),
-            in_=in_.rearrange("p (m t) -> p m t", t=PACK),
-        )
+    def by_lines(ap):
+        return ap.rearrange("p t (a c) -> p a t c", c=4)
+
+    def woven(ap):
+        return ap.rearrange("p (a c t) -> p a t c", c=4, t=PACK)
 
     with ExitStack() as ctx:
         keep = ctx.enter_context(tc.tile_pool(name="keep", bufs=1))
@@ -66,6 +71,9 @@ def tile_picked_ggnorm_none_po_kernel(
         w2_raw = keep.tile([P, H], I32, align_bytes=64)
         warm = keep.tile([P, 8], F32)
 
+        w4s_raw = keep.tile([P, N], U8, align_bytes=64)
+        for plane in (w2s_raw, w1s_raw, w4s_raw):
+            nc.gpsimd.memset(plane[:].bitcast(I32), 0)
         nc.vector.memset(warm[:], 0.0)
         e_sb = [turns.tile([P, S], F32, name="e_sb0", offset=14 * ROW, align_bytes=64)]
         e_sb.extend(keep.tile([P, 2 * S], F32, name=f"e_sb{t}") for t in range(1, PACK))
@@ -76,21 +84,17 @@ def tile_picked_ggnorm_none_po_kernel(
         for q in range(4):
             load_scale_quadrant(nc.sync, xs, x_scales, q)
         nc.sync.dma_start(out=xw[:].bitcast(I32), in_=words_of(x_words))
-        for q in range(4):
-            load_scale_quadrant(nc.sync, w2s_raw, w2_scales, q)
+        load_scale_rows(w2s_raw, w2_scales)
         nc.sync.dma_start(out=w2_raw[:], in_=words_of(w2_words))
         nc.sync.dma_start(out=w1_raw[:], in_=words_of(w1_words))
-        for q in range(4):
-            load_scale_quadrant(nc.sync, w1s_raw, w1_scales, q)
+        load_scale_rows(w1s_raw, w1_scales)
         nc.sync.dma_start(p_sb[0][:], p1)
         nc.sync.dma_start(p_sb[1][:], p2)
         w3_raw = turns.tile([P, PACK, H], F32, offset=7 * ROW, align_bytes=64)
         nc.sync.dma_start(out=w3_raw[:], in_=w3.rearrange("(p j) c -> p j c", j=PACK))
         w4_raw = keep.tile([P, N], I32, align_bytes=64)
-        w4s_raw = keep.tile([P, N], U8, align_bytes=64)
         nc.sync.dma_start(out=w4_raw[:], in_=words_of(w4_words))
-        for q in range(4):
-            load_scale_quadrant(nc.sync, w4s_raw, w4_scales, q)
+        load_scale_rows(w4s_raw, w4_scales)
 
         ident = keep.tile([P, P], F32)
         make_identity(nc, ident[:])
@@ -105,15 +109,15 @@ def tile_picked_ggnorm_none_po_kernel(
         for c in range(0, S, HALF):
             nc.vector.tensor_copy(out=xg_w[:, c : c + HALF], in_=xw[:].indirect(offs_sb[:, c // 16 : (c + HALF) // 16]))
         first, rest = slice(0, 1), slice(1, PACK)
-        deal_runs(w2s[:, 0:P], w2s_raw[:], first)
-        deal_runs(w2d_first[:], w2_raw[:], first)
-        deal_runs(w1d[:, 0:P], w1_raw[:], first)
-        deal_runs(w1s[:, 0:P], w1s_raw[:], first)
-        deal_runs(w1s[:, P:H], w1s_raw[:], rest)
-        deal_runs(w2s[:, P:H], w2s_raw[:], rest)
-        deal_runs(w1d[:, P:H], w1_raw[:], rest)
+        deal(w2s[:, 0:P], w2s_raw[:], first)
+        deal(w2d_first[:], w2_raw[:], first)
+        deal(w1d[:, 0:P], w1_raw[:], first)
+        deal(w1s[:, 0:P], w1s_raw[:], first)
+        deal(w1s[:, P:H], w1s_raw[:], rest)
+        deal(w2s[:, P:H], w2s_raw[:], rest)
+        deal(w1d[:, P:H], w1_raw[:], rest)
         w2d_rest = turns.tile([P, H - P], I32, offset=15 * ROW, align_bytes=64)
-        deal_runs(w2d_rest[:], w2_raw[:], rest)
+        deal(w2d_rest[:], w2_raw[:], rest)
         w2d = [w2d_first[:]] + [w2d_rest[:, (t - 1) * P : t * P] for t in range(1, PACK)]
         w1d = [w1d[:, t * P : (t + 1) * P] for t in range(PACK)]
 
@@ -144,20 +148,15 @@ def tile_picked_ggnorm_none_po_kernel(
         h_sb = [keep.tile([P, S], F32, name=f"h_sb{t}") for t in range(PACK)]
         gate = [keep.tile([P, 2, S], F32, name=f"gate{t}") for t in range(PACK)]
         y_sb = [e_sb[t + 1][:, S : 2 * S] for t in range(PACK - 1)] + [y_last[:]]
-        den_sq = keep.tile([P, 4, 8, PACK, 16], F32)
-        w3b = {}
+        den_sq = keep.tile([P, 4, PACK, P], F32)
         key = {}
         dens = {}
         inv = {}
 
-        def round_values(half, copy):
-            w3b[half] = placed(f"w3b{half}", 14 if half == 0 else 0, [P, 2, 8, 16, PACK], BF16)
-            copy(out=w3b[half][:], in_=w3_raw[:].rearrange("p j (g t r) -> p t g r j", t=PACK, g=8)[:, 2 * half : 2 * half + 2])
-
-        def quantise_values(half):
-            cols = slice(half * HALF, (half + 1) * HALF)
-            nc.vector.quantize_mx(
-                out=w3c[:, cols].bitcast(FP8X4), scales=w3s[:, cols], in_=w3b[half][:].rearrange("p t g r j -> p (t g r j)")
+        def round_values(half):
+            ms = slice(half * P // 2, (half + 1) * P // 2)
+            nc.scalar.copy(
+                out=w3b[:].rearrange("p t m j -> p m t j")[:, ms], in_=w3_raw[:].rearrange("p j (m t) -> p m t j", t=PACK)[:, ms]
             )
 
         def emptied(codes, plane, t, out, b):
@@ -182,14 +181,12 @@ def tile_picked_ggnorm_none_po_kernel(
                 add_turned(dens[t][:, b, :], gate[t][:, 0, blk], gate[t][:, 1, blk])
 
         def square(t):
-            nc.scalar.activation(
-                out=den_sq[:, :, :, t, :], in_=dens[t][:].rearrange("j b (g r) -> j b g r", g=8), func=ACT.Square, bias=0.1
-            )
+            nc.scalar.activation(out=den_sq[:, :, t, :], in_=dens[t][:], func=ACT.Square, bias=0.1)
 
         def inverse(b, ts=slice(0, PACK)):
             if ts.start == 0:
-                inv[b] = placed(f"inv{b}", 4 + b, [P, 8, PACK, 16], F32)
-            nc.scalar.activation(out=inv[b][:, :, ts, :], in_=den_sq[:, b, :, ts, :], func=ACT.Abs_reciprocal_sqrt)
+                inv[b] = placed(f"inv{b}", 4 + b, [P, PACK, P], F32)
+            nc.scalar.activation(out=inv[b][:, ts, :], in_=den_sq[:, b, ts, :], func=ACT.Abs_reciprocal_sqrt)
 
         for c, b in ((0, 0), (HALF, 1)):
             nc.scalar.copy(out=e_sb[0][:, c : c + HALF], in_=product(w2d, w2s, 0, b, c, HALF)[:])
@@ -201,21 +198,21 @@ def tile_picked_ggnorm_none_po_kernel(
         emptied(w2d, w2s, 2, e_sb[2][:, 0:S], 7)
         keys(0, 0)
         keys(0, 1)
-        round_values(0, nc.vector.tensor_copy)
         keys(1, 0)
         keys(1, 1)
-        quantise_values(0)
+        keys(2, 0)
         gates(0, 0)
         gates(0, 1)
         gate_sums(0)
+        w3b = placed("w3b", 0, [P, PACK, P, PACK], BF16)
+        round_values(0)
+        round_values(1)
         emptied(w2d, w2s, 3, e_sb[3][:, 0:S], 4)
         emptied(w1d, w1s, 3, y_sb[3], 5)
-        round_values(1, nc.scalar.copy)
         gates(1, 0)
         gates(1, 1)
         gate_sums(1)
-        keys(2, 0)
-        quantise_values(1)
+        nc.vector.quantize_mx(out=w3c[:].bitcast(FP8X4), scales=w3s[:], in_=w3b[:].rearrange("p t m j -> p (t m j)"))
         keys(2, 1)
         keys(3, 0)
         w4d = placed("w4d", 2, [P, N], I32)
@@ -229,16 +226,16 @@ def tile_picked_ggnorm_none_po_kernel(
         gates(2, 1)
         gate_sums(2)
         emptied(w3d, w3s, 1, h_sb[1][:], 7)
-        square(1)
         gates(3, 0)
-        square(2)
-        gates(3, 1)
-        gate_sums(3)
         emptied(w3d, w3s, 2, h_sb[2][:], 4)
         emptied(w3d, w3s, 3, h_sb[3][:], 5)
-        inverse(0, slice(0, 3))
+        gates(3, 1)
+        gate_sums(3)
+        square(1)
+        square(2)
+        inverse(0, slice(0, 2))
         square(3)
-        inverse(0, slice(3, PACK))
+        inverse(0, slice(2, PACK))
         for b in range(1, 4):
             inverse(b)
 
@@ -250,13 +247,7 @@ def tile_picked_ggnorm_none_po_kernel(
         nums = {}
         rounded = {}
         grouped = {}
-        codes_z = {}
         results = {}
-
-        def sum_banks(g):
-            if g < 3:
-                return [(slice(0, PACK), 4 + g)]
-            return [(slice(0, 3), 7), (slice(3, PACK), 0)]
 
         def messages(k, t, msg):
             c0, n = starts[k], PIECES[k]
@@ -265,39 +256,38 @@ def tile_picked_ggnorm_none_po_kernel(
                     msg[:, i, :], h_sb[t][:].indirect(p_sb[i][:, c0 // 16 : (c0 + n) // 16]),
                     gate[t][:, i, c0 : c0 + n], ALU.mult,
                 )
-            for b in range(n // P):
-                g = c0 // P + b
-                for ts, bank in sum_banks(g):
-                    if t == ts.start:
-                        nums[g, t] = bank_tile(bank, [P, ts.stop - ts.start, P])
-                    if ts.start <= t < ts.stop:
-                        blk = slice(b * P, (b + 1) * P)
-                        add_turned(nums[g, ts.start][:, t - ts.start, :], msg[:, 0, blk], msg[:, 1, blk])
 
-        def message_pair(k, t0, row):
+        def summed_messages(k, t, msg):
+            messages(k, t, msg)
+            for b in range(PIECES[k] // P):
+                g = starts[k] // P + b
+                if t == 0:
+                    nums[g] = bank_tile((1, 2, 6)[g], [P, PACK, P])
+                blk = slice(b * P, (b + 1) * P)
+                add_turned(nums[g][:, t, :], msg[:, 0, blk], msg[:, 1, blk])
+
+        def message_pair(k, t0, row, make):
             msg = placed(f"msg{k}{t0}", row, [P, 2, 2, P], F32)
             for t in (t0, t0 + 1):
-                messages(k, t, msg[:, t - t0])
+                make(k, t, msg[:, t - t0])
+            return msg
 
-        def normalise(k):
-            c0, n = starts[k], PIECES[k]
-            for b in range(n // P):
-                g = c0 // P + b
-                rounded[g] = keep.tile([P, 8, PACK, 16], BF16, name=f"zb{g}", align_bytes=64)
-                for ts, bank in sum_banks(g):
-                    nc.vector.tensor_tensor(
-                        rounded[g][:, :, ts, :], nums[g, ts.start][:].rearrange("j t (g r) -> j g t r", g=8),
-                        inv[g][:, :, ts, :], ALU.mult,
-                    )
+        def normalise(g):
+            rounded[g] = keep.tile([P, 2, 2 * P], BF16, name=f"zb{g}", align_bytes=64)
+            for u in range(2):
+                ts = slice(2 * u, 2 * u + 2)
+                nc.vector.tensor_tensor(
+                    rounded[g][:, u, :].rearrange("j (a c e) -> j a e c", c=4, e=2),
+                    by_lines(nums[g][:, ts, :]), by_lines(inv[g][:, ts, :]), ALU.mult,
+                )
 
         def turn_back(k):
             c0, n = starts[k], PIECES[k]
-            zt = bank_tile(1 + k, [P, 2, n])
+            zt = bank_tile((0, 4)[k], [P, 2, n])
             for b in range(n // P):
-                zwords = rounded[c0 // P + b][:].rearrange("j g t r -> j (g t r)").bitcast(F32)
                 for u in range(2):
-                    nc.tensor.transpose(zt[:, u, b * P : (b + 1) * P], zwords[:, u : 2 * P : 2], ident[:])
-            grouped[k] = keep.tile([P, n * PACK], BF16, name=f"zg{k}", align_bytes=64)
+                    nc.tensor.transpose(zt[:, u, b * P : (b + 1) * P], rounded[c0 // P + b][:, u, :].bitcast(F32), ident[:])
+            grouped[k] = placed(f"zg{k}", 11 + 2 * k, [P, n * PACK], BF16)
             nc.scalar.copy(out=grouped[k][:].bitcast(F32).rearrange("p (j u) -> p j u", u=2), in_=zt[:].rearrange("p u j -> p j u"))
 
         def last_layer(k):
@@ -308,7 +298,7 @@ def tile_picked_ggnorm_none_po_kernel(
             o_sb = keep.tile([P, PACK, n], F32, name=f"o_sb{k}")
             per_bank = 2
             for t0 in range(0, PACK, per_bank):
-                bank = bank_tile(((4, 5), (6, 1), (2, 4))[k][t0 // per_bank], [P, per_bank, n])
+                bank = bank_tile(((1, 2), (6, 5), (3, 0))[k][t0 // per_bank], [P, per_bank, n])
                 for t in range(t0, t0 + per_bank):
                     wc = slice(t * P, (t + 1) * P)
                     nc.tensor.matmul_mx(
@@ -322,27 +312,37 @@ def tile_picked_ggnorm_none_po_kernel(
         def planes(k, copy):
             c0, n = starts[k], PIECES[k]
             cols = slice(c0, c0 + n)
-            ob = keep.tile([P, n, PACK], BF16, name=f"ob{k}", align_bytes=64)
-            copy(out=ob[:], in_=results[k][:].rearrange("p t j -> p j t"))
-            nc.vector.quantize_mx(out=oc[:, cols].bitcast(FP8X4), scales=osc[:, cols], in_=ob[:].rearrange("p j t -> p (j t)"))
+            ob = keep.tile([P, n * PACK], BF16, name=f"ob{k}", align_bytes=64)
+            copy(out=woven(ob[:]), in_=by_lines(results[k][:]))
+            nc.vector.quantize_mx(out=oc[:, cols].bitcast(FP8X4), scales=osc[:, cols], in_=ob[:])
             nc.sync.dma_start(out=out_words[:, cols], in_=oc[:, cols].bitcast(I32))
 
+        inv_last = bank_tile(7, [P, PACK, P])
         for t in range(PACK):
-            messages(0, t, keep.tile([P, 2, HALF], F32, name=f"msg0{t}")[:])
-        message_pair(1, 0, 8)
+            nc.tensor.transpose(inv_last[:, t, :], inv[3][:, t, :], ident[:])
+        for t in range(PACK):
+            summed_messages(0, t, keep.tile([P, 2, HALF], F32, name=f"msg0{t}")[:])
+        message_pair(1, 0, 8, summed_messages)
         normalise(0)
-        turn_back(0)
-        message_pair(1, 2, 4)
-        message_pair(2, 0, 5)
         normalise(1)
+        turn_back(0)
+        message_pair(1, 2, 4, summed_messages)
+        msg_first = placed("msg_first", 5, [P, 1, 2, P], F32)
+        messages(2, 0, msg_first[:, 0])
         last_layer(0)
-        turn_back(1)
-        message_pair(2, 2, 6)
-        last_layer(1)
         normalise(2)
-        turn_back(2)
+        turn_back(1)
+        msg_rest = placed("msg_rest", 11, [P, 3, 2, P], F32)
+        for t in range(1, PACK):
+            messages(2, t, msg_rest[:, t - 1])
+        num_last = keep.tile([P, PACK, P], F32)
+        for ts, msg in ((slice(0, 1), msg_first), (slice(1, PACK), msg_rest)):
+            nc.vector.tensor_tensor(num_last[:, ts, :], msg[:, :, 0, :], msg[:, :, 1, :], ALU.add)
+        last_layer(1)
+        grouped[2] = keep.tile([P, P * PACK], BF16, name="zg2", align_bytes=64)
+        nc.vector.tensor_tensor(woven(grouped[2][:]), by_lines(num_last[:]), by_lines(inv_last[:]), ALU.mult)
         last_layer(2)
-        planes(0, nc.vector.tensor_copy)
+        planes(0, nc.scalar.copy)
         planes(1, nc.vector.tensor_copy)
         planes(2, nc.vector.tensor_copy)
         out_planes = out_2[0].bitcast(I32)

@@ -50,11 +50,11 @@ def tile_picked_ggnorm_none_po_kernel(
             in_=in_.rearrange("p (m t) -> p m t", t=PACK)[:, :, ts],
         )
 
-    def by_lines(ap):
-        return ap.rearrange("p t (a c) -> p a t c", c=4)
-
-    def woven(ap):
-        return ap.rearrange("p (a c t) -> p a t c", c=4, t=PACK)
+    def deal_bytes(out, in_, ts=slice(0, PACK)):
+        nc.vector.tensor_copy(
+            out=out.rearrange("p (t m) -> p t m", t=ts.stop - ts.start),
+            in_=in_.rearrange("p (m t) -> p t m", t=PACK)[:, ts],
+        )
 
     with ExitStack() as ctx:
         keep = ctx.enter_context(tc.tile_pool(name="keep", bufs=1))
@@ -109,12 +109,12 @@ def tile_picked_ggnorm_none_po_kernel(
         for c in range(0, S, HALF):
             nc.vector.tensor_copy(out=xg_w[:, c : c + HALF], in_=xw[:].indirect(offs_sb[:, c // 16 : (c + HALF) // 16]))
         first, rest = slice(0, 1), slice(1, PACK)
-        deal(w2s[:, 0:P], w2s_raw[:], first)
+        deal_bytes(w2s[:, 0:P], w2s_raw[:], first)
         deal(w2d_first[:], w2_raw[:], first)
         deal(w1d[:, 0:P], w1_raw[:], first)
-        deal(w1s[:, 0:P], w1s_raw[:], first)
-        deal(w1s[:, P:H], w1s_raw[:], rest)
-        deal(w2s[:, P:H], w2s_raw[:], rest)
+        deal_bytes(w1s[:, 0:P], w1s_raw[:], first)
+        deal_bytes(w1s[:, P:H], w1s_raw[:], rest)
+        deal_bytes(w2s[:, P:H], w2s_raw[:], rest)
         deal(w1d[:, P:H], w1_raw[:], rest)
         w2d_rest = turns.tile([P, H - P], I32, offset=15 * ROW, align_bytes=64)
         deal(w2d_rest[:], w2_raw[:], rest)
@@ -138,9 +138,9 @@ def tile_picked_ggnorm_none_po_kernel(
             nc.tensor.matmul(bank_cols, lhsT=b, rhs=ident[:], start=False, stop=True, is_transpose=True)
 
         def placed(name, row, shape, dtype):
-            return turns.tile(shape, dtype, name=name, offset=row * ROW, align_bytes=64)
+            return turns.tile(shape, dtype, name=name, offset=int(row * ROW), align_bytes=64)
 
-        key_place = {(0, 0): (0, 1), (1, 0): (2, 2), (3, 1): (4, 5), (0, 1): (1, 1), (1, 1): (12, 1), (2, 0): (13, 1), (2, 1): (10, 1), (3, 0): (9, 1)}
+        key_place = {(0, 0): (0, 1), (1, 0): (2, 2), (3, 1): (4, 5), (0, 1): (1, 1), (1, 1): (12, 1), (2, 0): (13, 1), (2, 1): (26, 1), (3, 0): (9, 1)}
 
         w3c = keep.tile([P, H], U32, align_bytes=64)
         w3s = keep.tile([P, H], U8, align_bytes=64)
@@ -148,7 +148,8 @@ def tile_picked_ggnorm_none_po_kernel(
         h_sb = [keep.tile([P, S], F32, name=f"h_sb{t}") for t in range(PACK)]
         gate = [keep.tile([P, 2, S], F32, name=f"gate{t}") for t in range(PACK)]
         y_sb = [e_sb[t + 1][:, S : 2 * S] for t in range(PACK - 1)] + [y_last[:]]
-        den_sq = keep.tile([P, 4, PACK, P], F32)
+        den_late = keep.tile([P, 2, PACK, P], F32)
+        den_early = [placed(f"den_early{u}", 22 + 2 * u, [P, 2, 2, P], F32) for u in range(2)]
         key = {}
         dens = {}
         inv = {}
@@ -181,12 +182,13 @@ def tile_picked_ggnorm_none_po_kernel(
                 add_turned(dens[t][:, b, :], gate[t][:, 0, blk], gate[t][:, 1, blk])
 
         def square(t):
-            nc.scalar.activation(out=den_sq[:, :, t, :], in_=dens[t][:], func=ACT.Square, bias=0.1)
+            for out, blocks in ((den_early[t // 2][:, :, t % 2, :], slice(0, 2)), (den_late[:, :, t, :], slice(2, 4))):
+                nc.scalar.activation(out=out, in_=dens[t][:, blocks], func=ACT.Square, bias=0.1)
 
-        def inverse(b, ts=slice(0, PACK)):
-            if ts.start == 0:
-                inv[b] = placed(f"inv{b}", 4 + b, [P, PACK, P], F32)
-            nc.scalar.activation(out=inv[b][:, ts, :], in_=den_sq[:, b, ts, :], func=ACT.Abs_reciprocal_sqrt)
+        def inverse(name, row, den):
+            tile = placed(name, row, [P, *den.shape[1:]], F32)
+            nc.scalar.activation(out=tile[:], in_=den, func=ACT.Abs_reciprocal_sqrt)
+            return tile
 
         for c, b in ((0, 0), (HALF, 1)):
             nc.scalar.copy(out=e_sb[0][:, c : c + HALF], in_=product(w2d, w2s, 0, b, c, HALF)[:])
@@ -201,6 +203,7 @@ def tile_picked_ggnorm_none_po_kernel(
         keys(1, 0)
         keys(1, 1)
         keys(2, 0)
+        keys(2, 1)
         gates(0, 0)
         gates(0, 1)
         gate_sums(0)
@@ -213,18 +216,17 @@ def tile_picked_ggnorm_none_po_kernel(
         gates(1, 1)
         gate_sums(1)
         nc.vector.quantize_mx(out=w3c[:].bitcast(FP8X4), scales=w3s[:], in_=w3b[:].rearrange("p t m j -> p (t m j)"))
-        keys(2, 1)
         keys(3, 0)
         w4d = placed("w4d", 2, [P, N], I32)
         w4s = placed("w4s", 3, [P, N], U8)
         deal(w4d[:], w4_raw[:])
-        deal(w4s[:], w4s_raw[:])
+        deal_bytes(w4s[:], w4s_raw[:])
         keys(3, 1)
-        emptied(w3d, w3s, 0, h_sb[0][:], 6)
         gates(2, 0)
         square(0)
         gates(2, 1)
         gate_sums(2)
+        emptied(w3d, w3s, 0, h_sb[0][:], 6)
         emptied(w3d, w3s, 1, h_sb[1][:], 7)
         gates(3, 0)
         emptied(w3d, w3s, 2, h_sb[2][:], 4)
@@ -233,14 +235,15 @@ def tile_picked_ggnorm_none_po_kernel(
         gate_sums(3)
         square(1)
         square(2)
-        inverse(0, slice(0, 2))
+        inv_low = inverse("inv_low", 4, den_early[0][:])
         square(3)
-        inverse(0, slice(2, PACK))
-        for b in range(1, 4):
-            inverse(b)
+        inv_high = inverse("inv_high", 5, den_early[1][:])
+        inv_third = inverse("inv_third", 6, den_late[:, 0:1])
+        inv_fourth = inverse("inv_fourth", 7, den_late[:, 1])
+        inv[0, 0], inv[0, 1] = inv_low[:], inv_high[:]
+        inv[1, 0], inv[1, 1] = inv_third[:, :, 0:2, :], inv_third[:, :, 2:PACK, :]
 
         osc = keep.tile([P, S], U8, align_bytes=64)
-        oc = keep.tile([P, S], U32, align_bytes=64)
         out_rows = out_0.rearrange("(p t) j -> p t j", t=PACK)
         out_words = out_1[0].rearrange("p n t -> p (n t)").bitcast(I32)
         starts = [sum(PIECES[:i]) for i in range(len(PIECES))]
@@ -248,6 +251,7 @@ def tile_picked_ggnorm_none_po_kernel(
         rounded = {}
         grouped = {}
         results = {}
+        woven_out = {}
 
         def messages(k, t, msg):
             c0, n = starts[k], PIECES[k]
@@ -259,12 +263,13 @@ def tile_picked_ggnorm_none_po_kernel(
 
         def summed_messages(k, t, msg):
             messages(k, t, msg)
-            for b in range(PIECES[k] // P):
-                g = starts[k] // P + b
-                if t == 0:
-                    nums[g] = bank_tile((1, 2, 6)[g], [P, PACK, P])
+            blocks = PIECES[k] // P
+            u, e = divmod(t, 2)
+            if e == 0:
+                nums[k, u] = bank_tile(((1, 2), (3, 5))[k][u], [P, blocks, 2, P])
+            for b in range(blocks):
                 blk = slice(b * P, (b + 1) * P)
-                add_turned(nums[g][:, t, :], msg[:, 0, blk], msg[:, 1, blk])
+                add_turned(nums[k, u][:, b, e, :], msg[:, 0, blk], msg[:, 1, blk])
 
         def message_pair(k, t0, row, make):
             msg = placed(f"msg{k}{t0}", row, [P, 2, 2, P], F32)
@@ -272,21 +277,19 @@ def tile_picked_ggnorm_none_po_kernel(
                 make(k, t, msg[:, t - t0])
             return msg
 
-        def normalise(g):
-            rounded[g] = keep.tile([P, 2, 2 * P], BF16, name=f"zb{g}", align_bytes=64)
-            for u in range(2):
-                ts = slice(2 * u, 2 * u + 2)
-                nc.vector.tensor_tensor(
-                    rounded[g][:, u, :].rearrange("j (a c e) -> j a e c", c=4, e=2),
-                    by_lines(nums[g][:, ts, :]), by_lines(inv[g][:, ts, :]), ALU.mult,
-                )
+        def normalise(k, u):
+            blocks = PIECES[k] // P
+            rounded[k, u] = keep.tile([P, blocks, P, 2], BF16, name=f"zb{k}{u}", align_bytes=64)
+            nc.vector.tensor_tensor(
+                rounded[k, u][:], nums[k, u][:].rearrange("j b e p -> j b p e"), inv[k, u].rearrange("j b e p -> j b p e"), ALU.mult,
+            )
 
         def turn_back(k):
             c0, n = starts[k], PIECES[k]
             zt = bank_tile((0, 4)[k], [P, 2, n])
-            for b in range(n // P):
-                for u in range(2):
-                    nc.tensor.transpose(zt[:, u, b * P : (b + 1) * P], rounded[c0 // P + b][:, u, :].bitcast(F32), ident[:])
+            for u in range(2):
+                for b in range(n // P):
+                    nc.tensor.transpose(zt[:, u, b * P : (b + 1) * P], rounded[k, u][:, b].rearrange("j p e -> j (p e)").bitcast(F32), ident[:])
             grouped[k] = placed(f"zg{k}", 11 + 2 * k, [P, n * PACK], BF16)
             nc.scalar.copy(out=grouped[k][:].bitcast(F32).rearrange("p (j u) -> p j u", u=2), in_=zt[:].rearrange("p u j -> p j u"))
 
@@ -298,7 +301,7 @@ def tile_picked_ggnorm_none_po_kernel(
             o_sb = keep.tile([P, PACK, n], F32, name=f"o_sb{k}")
             per_bank = 2
             for t0 in range(0, PACK, per_bank):
-                bank = bank_tile(((1, 2), (6, 5), (3, 0))[k][t0 // per_bank], [P, per_bank, n])
+                bank = bank_tile(((1, 2), (6, 5), (7, 0))[k][t0 // per_bank], [P, per_bank, n])
                 for t in range(t0, t0 + per_bank):
                     wc = slice(t * P, (t + 1) * P)
                     nc.tensor.matmul_mx(
@@ -306,45 +309,60 @@ def tile_picked_ggnorm_none_po_kernel(
                         rhs=zc[:].bitcast(FP8X4), rhs_scale=zs[:], start=True, stop=True,
                     )
                 nc.scalar.copy(out=o_sb[:, t0 : t0 + per_bank, :], in_=bank[:])
-            nc.sync.dma_start(out=out_rows[:, :, c0 : c0 + n], in_=o_sb[:])
+                if k == 0:
+                    nc.sync.dma_start(out=out_rows[:, t0 : t0 + per_bank, c0 : c0 + n], in_=o_sb[:, t0 : t0 + per_bank, :])
+            if k > 0:
+                (nc.sync if k == 1 else nc.scalar).dma_start(out=out_rows[:, :, c0 : c0 + n], in_=o_sb[:])
             results[k] = o_sb
 
-        def planes(k, copy):
-            c0, n = starts[k], PIECES[k]
-            cols = slice(c0, c0 + n)
-            ob = keep.tile([P, n * PACK], BF16, name=f"ob{k}", align_bytes=64)
-            copy(out=woven(ob[:]), in_=by_lines(results[k][:]))
-            nc.vector.quantize_mx(out=oc[:, cols].bitcast(FP8X4), scales=osc[:, cols], in_=ob[:])
-            nc.sync.dma_start(out=out_words[:, cols], in_=oc[:, cols].bitcast(I32))
+        def round_result(k, copy):
+            woven_out[k] = placed(f"ob{k}", (27, 16.25, 28)[k], [P, PIECES[k] * PACK], BF16)
+            copy(out=woven_out[k][:].rearrange("p (j t) -> p j t", t=PACK), in_=results[k][:].rearrange("p t j -> p j t"))
 
-        inv_last = bank_tile(7, [P, PACK, P])
+        def planes(k):
+            cols = slice(starts[k], starts[k] + PIECES[k])
+            nc.vector.quantize_mx(out=oc[:, cols].bitcast(FP8X4), scales=osc[:, cols], in_=woven_out[k][:])
+
         for t in range(PACK):
-            nc.tensor.transpose(inv_last[:, t, :], inv[3][:, t, :], ident[:])
-        for t in range(PACK):
-            summed_messages(0, t, keep.tile([P, 2, HALF], F32, name=f"msg0{t}")[:])
+            summed_messages(0, t, placed(f"msg0{t}", (18, 21, 19, 23)[t], [P, 2, HALF], F32)[:])
         message_pair(1, 0, 8, summed_messages)
-        normalise(0)
-        normalise(1)
+        normalise(0, 0)
+        summed_messages(1, 2, placed("msg12", 21.75, [P, 2, P], F32)[:])
+        normalise(0, 1)
         turn_back(0)
-        message_pair(1, 2, 4, summed_messages)
-        msg_first = placed("msg_first", 5, [P, 1, 2, P], F32)
+        summed_messages(1, 3, placed("msg13", 23.75, [P, 2, P], F32)[:])
+        msg_first = placed("msg_first", 23, [P, 1, 2, P], F32)
         messages(2, 0, msg_first[:, 0])
-        last_layer(0)
-        normalise(2)
+        for u in range(2):
+            normalise(1, u)
         turn_back(1)
-        msg_rest = placed("msg_rest", 11, [P, 3, 2, P], F32)
-        for t in range(1, PACK):
+        last_layer(0)
+        inv_last = bank_tile(3, [P, PACK, P])
+        for t in range(PACK):
+            nc.tensor.transpose(inv_last[:, t, :], inv_fourth[:, t, :], ident[:])
+        msg_rest = placed("msg_rest", 24, [P, 3, 2, P], F32)
+        for t in (1, 2):
             messages(2, t, msg_rest[:, t - 1])
-        num_last = keep.tile([P, PACK, P], F32)
-        for ts, msg in ((slice(0, 1), msg_first), (slice(1, PACK), msg_rest)):
-            nc.vector.tensor_tensor(num_last[:, ts, :], msg[:, :, 0, :], msg[:, :, 1, :], ALU.add)
         last_layer(1)
-        grouped[2] = keep.tile([P, P * PACK], BF16, name="zg2", align_bytes=64)
-        nc.vector.tensor_tensor(woven(grouped[2][:]), by_lines(num_last[:]), by_lines(inv_last[:]), ALU.mult)
+        round_result(0, nc.scalar.copy)
+        messages(2, 3, msg_rest[:, 2])
+        num_last = placed("num_last", 11.5, [P, PACK, P], F32)
+        for ts, msg in ((slice(0, 1), msg_first[:]), (slice(1, 3), msg_rest[:, 0:2]), (slice(3, PACK), msg_rest[:, 2:3])):
+            nc.vector.tensor_tensor(num_last[:, ts, :], msg[:, :, 0, :], msg[:, :, 1, :], ALU.add)
+        grouped[2] = placed("zg2", 16, [P, P * PACK], BF16)
+        nc.vector.tensor_tensor(
+            grouped[2][:].rearrange("p (j t) -> p j t", t=PACK),
+            num_last[:].rearrange("p t j -> p j t"), inv_last[:].rearrange("p t j -> p j t"), ALU.mult,
+        )
         last_layer(2)
-        planes(0, nc.scalar.copy)
-        planes(1, nc.vector.tensor_copy)
-        planes(2, nc.vector.tensor_copy)
+        oc = placed("oc", 15.25, [P, S], U32)
+        round_result(1, nc.vector.tensor_copy)
+        planes(1)
+        planes(0)
+        nc.sync.dma_start(out=out_words[:, 0 : S - P], in_=oc[:, 0 : S - P].bitcast(I32))
+        round_result(2, nc.vector.tensor_copy)
+        planes(2)
+        nc.sync.dma_start(out=out_words[:, S - P : S], in_=oc[:, S - P : S].bitcast(I32))
         out_planes = out_2[0].bitcast(I32)
         for q in range(4):
             engine = nc.sync if q % 2 == 0 else nc.scalar

@@ -190,6 +190,9 @@ def tile_picked_ggnorm_none_po_kernel(
             nc.scalar.activation(out=tile[:], in_=den, func=ACT.Abs_reciprocal_sqrt)
             return tile
 
+        def paired(den):
+            return den.rearrange("j b e p -> j b p e")
+
         for c, b in ((0, 0), (HALF, 1)):
             nc.scalar.copy(out=e_sb[0][:, c : c + HALF], in_=product(w2d, w2s, 0, b, c, HALF)[:])
         nc.vector.tensor_copy(out=y_sb[0][:, 0:HALF], in_=product(w1d, w1s, 0, 2, 0, HALF)[:])
@@ -235,13 +238,13 @@ def tile_picked_ggnorm_none_po_kernel(
         gate_sums(3)
         square(1)
         square(2)
-        inv_low = inverse("inv_low", 4, den_early[0][:])
+        inv_low = inverse("inv_low", 4, paired(den_early[0][:]))
         square(3)
-        inv_high = inverse("inv_high", 5, den_early[1][:])
-        inv_third = inverse("inv_third", 6, den_late[:, 0:1])
+        inv_high = inverse("inv_high", 5, paired(den_early[1][:]))
+        inv_third = inverse("inv_third", 6, paired(den_late[:, 0].rearrange("j (u e) p -> j u e p", e=2)))
         inv_fourth = inverse("inv_fourth", 7, den_late[:, 1])
         inv[0, 0], inv[0, 1] = inv_low[:], inv_high[:]
-        inv[1, 0], inv[1, 1] = inv_third[:, :, 0:2, :], inv_third[:, :, 2:PACK, :]
+        inv[1, 0], inv[1, 1] = inv_third[:, 0:1], inv_third[:, 1:2]
 
         osc = keep.tile([P, S], U8, align_bytes=64)
         out_rows = out_0.rearrange("(p t) j -> p t j", t=PACK)
@@ -281,7 +284,7 @@ def tile_picked_ggnorm_none_po_kernel(
             blocks = PIECES[k] // P
             rounded[k, u] = keep.tile([P, blocks, P, 2], BF16, name=f"zb{k}{u}", align_bytes=64)
             nc.vector.tensor_tensor(
-                rounded[k, u][:], nums[k, u][:].rearrange("j b e p -> j b p e"), inv[k, u].rearrange("j b e p -> j b p e"), ALU.mult,
+                rounded[k, u][:], paired(nums[k, u][:]), inv[k, u], ALU.mult,
             )
 
         def turn_back(k):
@@ -351,8 +354,8 @@ def tile_picked_ggnorm_none_po_kernel(
             nc.vector.tensor_tensor(num_last[:, ts, :], msg[:, :, 0, :], msg[:, :, 1, :], ALU.add)
         grouped[2] = placed("zg2", 16, [P, P * PACK], BF16)
         nc.vector.tensor_tensor(
-            grouped[2][:].rearrange("p (j t) -> p j t", t=PACK),
-            num_last[:].rearrange("p t j -> p j t"), inv_last[:].rearrange("p t j -> p j t"), ALU.mult,
+            grouped[2][:].rearrange("p (a c t) -> p a t c", c=2, t=PACK),
+            num_last[:].rearrange("p t (a c) -> p a t c", c=2), inv_last[:].rearrange("p t (a c) -> p a t c", c=2), ALU.mult,
         )
         last_layer(2)
         oc = placed("oc", 15.25, [P, S], U32)

@@ -39,11 +39,6 @@ def tile_picked_ggnorm_none_po_kernel(
             in_=rows.unsqueeze(0).broadcast_to([8, 4, rows.shape[1]]),
         )
 
-    def load_scale_rows(plane, dram):
-        rows = dram[0].bitcast(I32)
-        for q in range(4):
-            nc.sync.dma_start(out=plane[32 * q : 32 * q + 4, :].bitcast(I32), in_=rows[4 * q : 4 * q + 4, :])
-
     def deal(out, in_, ts=slice(0, PACK)):
         nc.vector.tensor_copy(
             out=out.rearrange("p (t m) -> p m t", t=ts.stop - ts.start),
@@ -72,8 +67,6 @@ def tile_picked_ggnorm_none_po_kernel(
         warm = keep.tile([P, 8], F32)
 
         w4s_raw = keep.tile([P, N], U8, align_bytes=64)
-        for plane in (w2s_raw, w1s_raw, w4s_raw):
-            nc.gpsimd.memset(plane[:].bitcast(I32), 0)
         nc.vector.memset(warm[:], 0.0)
         e_sb = [turns.tile([P, S], F32, name="e_sb0", offset=14 * ROW, align_bytes=64)]
         e_sb.extend(keep.tile([P, 2 * S], F32, name=f"e_sb{t}") for t in range(1, PACK))
@@ -84,17 +77,20 @@ def tile_picked_ggnorm_none_po_kernel(
         for q in range(4):
             load_scale_quadrant(nc.sync, xs, x_scales, q)
         nc.sync.dma_start(out=xw[:].bitcast(I32), in_=words_of(x_words))
-        load_scale_rows(w2s_raw, w2_scales)
+        for q in range(4):
+            load_scale_quadrant(nc.sync, w2s_raw, w2_scales, q)
         nc.sync.dma_start(out=w2_raw[:], in_=words_of(w2_words))
         nc.sync.dma_start(out=w1_raw[:], in_=words_of(w1_words))
-        load_scale_rows(w1s_raw, w1_scales)
+        for q in range(4):
+            load_scale_quadrant(nc.sync, w1s_raw, w1_scales, q)
         nc.sync.dma_start(p_sb[0][:], p1)
         nc.sync.dma_start(p_sb[1][:], p2)
         w3_raw = turns.tile([P, PACK, H], F32, offset=7 * ROW, align_bytes=64)
         nc.sync.dma_start(out=w3_raw[:], in_=w3.rearrange("(p j) c -> p j c", j=PACK))
         w4_raw = keep.tile([P, N], I32, align_bytes=64)
         nc.sync.dma_start(out=w4_raw[:], in_=words_of(w4_words))
-        load_scale_rows(w4s_raw, w4_scales)
+        for q in range(4):
+            load_scale_quadrant(nc.sync, w4s_raw, w4_scales, q)
 
         ident = keep.tile([P, P], F32)
         make_identity(nc, ident[:])
@@ -231,12 +227,12 @@ def tile_picked_ggnorm_none_po_kernel(
         gate_sums(2)
         emptied(w3d, w3s, 0, h_sb[0][:], 6)
         emptied(w3d, w3s, 1, h_sb[1][:], 7)
+        square(1)
         gates(3, 0)
         emptied(w3d, w3s, 2, h_sb[2][:], 4)
         emptied(w3d, w3s, 3, h_sb[3][:], 5)
         gates(3, 1)
         gate_sums(3)
-        square(1)
         square(2)
         inv_low = inverse("inv_low", 4, paired(den_early[0][:]))
         square(3)
@@ -334,7 +330,7 @@ def tile_picked_ggnorm_none_po_kernel(
         normalise(0, 1)
         turn_back(0)
         summed_messages(1, 3, placed("msg13", 23.75, [P, 2, P], F32)[:])
-        msg_first = placed("msg_first", 23, [P, 1, 2, P], F32)
+        msg_first = placed("msg_first", 24.25, [P, 1, 2, P], F32)
         messages(2, 0, msg_first[:, 0])
         for u in range(2):
             normalise(1, u)
@@ -343,7 +339,7 @@ def tile_picked_ggnorm_none_po_kernel(
         inv_last = bank_tile(3, [P, PACK, P])
         for t in range(PACK):
             nc.tensor.transpose(inv_last[:, t, :], inv_fourth[:, t, :], ident[:])
-        msg_rest = placed("msg_rest", 24, [P, 3, 2, P], F32)
+        msg_rest = placed("msg_rest", 22.5, [P, 3, 2, P], F32)
         for t in (1, 2):
             messages(2, t, msg_rest[:, t - 1])
         last_layer(1)

@@ -18,9 +18,11 @@ ALU = mybir.AluOpType
 
 P = 128
 PACK = 4
-HALF = 256
-PIECES = (256, 128, 128)
+HALF = S // 2
 ROW = 4 * S
+EARLY = slice(0, 2 * P)
+MIDDLE = slice(2 * P, 3 * P)
+LAST = slice(3 * P, 4 * P)
 
 
 def tile_picked_ggnorm_none_po_kernel(
@@ -32,336 +34,333 @@ def tile_picked_ggnorm_none_po_kernel(
     def words_of(dram):
         return dram[0].rearrange("p n t -> p (n t)").bitcast(I32)
 
-    def load_scale_quadrant(engine, plane, dram, q):
-        rows = dram[0].bitcast(I32)[4 * q : 4 * q + 4, :]
-        engine.dma_start(
-            out=plane[32 * q : 32 * q + 32, :].bitcast(I32),
-            in_=rows.unsqueeze(0).broadcast_to([8, 4, rows.shape[1]]),
-        )
+    def load_scale_rows(plane, dram):
+        rows = dram[0].bitcast(I32)
+        for q in range(4):
+            nc.sync.dma_start(
+                out=plane[32 * q : 32 * q + 32, :].bitcast(I32),
+                in_=rows[4 * q : 4 * q + 4, :].unsqueeze(0).broadcast_to([8, 4, rows.shape[1]]),
+            )
 
-    def deal(out, in_, ts=slice(0, PACK)):
+    def deal_words(out, in_, ts):
         nc.vector.tensor_copy(
             out=out.rearrange("p (t m) -> p m t", t=ts.stop - ts.start),
             in_=in_.rearrange("p (m t) -> p m t", t=PACK)[:, :, ts],
         )
 
-    def deal_bytes(out, in_, ts=slice(0, PACK)):
+    def deal_bytes(out, in_, ts):
         nc.vector.tensor_copy(
             out=out.rearrange("p (t m) -> p t m", t=ts.stop - ts.start),
             in_=in_.rearrange("p (m t) -> p t m", t=PACK)[:, ts],
         )
 
+    def entries(offsets, nodes):
+        return offsets[:, nodes.start // 16 : nodes.stop // 16]
+
+    def part(t):
+        return slice(t * P, (t + 1) * P)
+
     with ExitStack() as ctx:
         keep = ctx.enter_context(tc.tile_pool(name="keep", bufs=1))
         turns = ctx.enter_context(tc.tile_pool(name="turns", bufs=1))
+        reuse = ctx.enter_context(tc.tile_pool(name="reuse", bufs=1))
         psum = ctx.enter_context(tc.psum_pool(name="psum", bufs=1))
 
+        def shared(tag, name, shape, dtype):
+            return turns.tile(shape, dtype, tag=tag, name=name, align_bytes=64)
+
+        def bank(b, name, shape):
+            return psum.tile(shape, F32, tag=f"bank{b}", name=name)
+
         offs_sb = keep.tile([P, S // 16], U16)
-        p_sb = [keep.tile([P, S // 16], U16, name=f"p{i}_sb") for i in (1, 2)]
+        lists = [keep.tile([P, S // 16], U16, name=f"p{i}_sb") for i in (1, 2)]
         xw = keep.tile([P, T], U32, align_bytes=64)
         xs = keep.tile([P, T], U8, align_bytes=64)
-        w1s_raw = turns.tile([P, H], U8, offset=15 * ROW, align_bytes=64)
+        w1s_raw = shared("w1s", "w1s_raw", [P, H], U8)
         w2s_raw = keep.tile([P, H], U8, align_bytes=64)
+        w4s_raw = keep.tile([P, N], U8, align_bytes=64)
         w1_raw = keep.tile([P, H], I32, align_bytes=64)
         w2_raw = keep.tile([P, H], I32, align_bytes=64)
+        w4_raw = keep.tile([P, N], I32, align_bytes=64)
+        w3_raw = reuse.tile([P, PACK, H], F32, offset=0, align_bytes=64)
         warm = keep.tile([P, 8], F32)
 
-        w4s_raw = keep.tile([P, N], U8, align_bytes=64)
         nc.vector.memset(warm[:], 0.0)
-        e_sb = [turns.tile([P, S], F32, name="e_sb0", offset=14 * ROW, align_bytes=64)]
-        e_sb.extend(keep.tile([P, 2 * S], F32, name=f"e_sb{t}") for t in range(1, PACK))
-        y_last = keep.tile([P, S], F32)
         nc.scalar.activation(out=warm[:], in_=warm[:], func=ACT.Sigmoid)
 
         nc.sync.dma_start(offs_sb[:], offs)
-        for q in range(4):
-            load_scale_quadrant(nc.sync, xs, x_scales, q)
+        load_scale_rows(xs, x_scales)
         nc.sync.dma_start(out=xw[:].bitcast(I32), in_=words_of(x_words))
-        for q in range(4):
-            load_scale_quadrant(nc.sync, w2s_raw, w2_scales, q)
+        load_scale_rows(w2s_raw, w2_scales)
         nc.sync.dma_start(out=w2_raw[:], in_=words_of(w2_words))
         nc.sync.dma_start(out=w1_raw[:], in_=words_of(w1_words))
-        for q in range(4):
-            load_scale_quadrant(nc.sync, w1s_raw, w1_scales, q)
-        nc.sync.dma_start(p_sb[0][:], p1)
-        nc.sync.dma_start(p_sb[1][:], p2)
-        w3_raw = turns.tile([P, PACK, H], F32, offset=7 * ROW, align_bytes=64)
-        nc.sync.dma_start(out=w3_raw[:], in_=w3.rearrange("(p j) c -> p j c", j=PACK))
-        w4_raw = keep.tile([P, N], I32, align_bytes=64)
         nc.sync.dma_start(out=w4_raw[:], in_=words_of(w4_words))
-        for q in range(4):
-            load_scale_quadrant(nc.sync, w4s_raw, w4_scales, q)
+        load_scale_rows(w1s_raw, w1_scales)
+        nc.sync.dma_start(lists[0][:], p1)
+        nc.sync.dma_start(lists[1][:], p2)
+        nc.sync.dma_start(out=w3_raw[:], in_=w3.rearrange("(p j) c -> p j c", j=PACK))
+        load_scale_rows(w4s_raw, w4_scales)
 
         ident = keep.tile([P, P], F32)
         make_identity(nc, ident[:])
 
         xg_s = keep.tile([P, S], U8, align_bytes=64)
         xg_w = keep.tile([P, S], U32, align_bytes=64)
-        nc.vector.tensor_copy(out=xg_s[:], in_=xs[:].indirect(offs_sb[:]))
-        w1s = keep.tile([P, H], U8, align_bytes=64)
-        w2s = keep.tile([P, H], U8, align_bytes=64)
         w1d = keep.tile([P, H], I32, align_bytes=64)
         w2d_first = keep.tile([P, P], I32, align_bytes=64)
-        for c in range(0, S, HALF):
-            nc.vector.tensor_copy(out=xg_w[:, c : c + HALF], in_=xw[:].indirect(offs_sb[:, c // 16 : (c + HALF) // 16]))
-        first, rest = slice(0, 1), slice(1, PACK)
+        first, rest, whole = slice(0, 1), slice(1, PACK), slice(0, PACK)
+        halves = (slice(0, HALF), slice(HALF, S))
+
+        nc.vector.tensor_copy(out=xg_s[:], in_=xs[:].indirect(offs_sb[:]))
+        for nodes in halves:
+            nc.vector.tensor_copy(out=xg_w[:, nodes], in_=xw[:].indirect(entries(offs_sb, nodes)))
+        w1s = keep.tile([P, H], U8, align_bytes=64)
+        w2s = keep.tile([P, H], U8, align_bytes=64)
         deal_bytes(w2s[:, 0:P], w2s_raw[:], first)
-        deal(w2d_first[:], w2_raw[:], first)
-        deal(w1d[:, 0:P], w1_raw[:], first)
+        deal_words(w2d_first[:], w2_raw[:], first)
+        deal_words(w1d[:, 0:P], w1_raw[:], first)
         deal_bytes(w1s[:, 0:P], w1s_raw[:], first)
         deal_bytes(w1s[:, P:H], w1s_raw[:], rest)
         deal_bytes(w2s[:, P:H], w2s_raw[:], rest)
-        deal(w1d[:, P:H], w1_raw[:], rest)
-        w2d_rest = turns.tile([P, H - P], I32, offset=15 * ROW, align_bytes=64)
-        deal(w2d_rest[:], w2_raw[:], rest)
-        w2d = [w2d_first[:]] + [w2d_rest[:, (t - 1) * P : t * P] for t in range(1, PACK)]
-        w1d = [w1d[:, t * P : (t + 1) * P] for t in range(PACK)]
+        deal_words(w1d[:, P:H], w1_raw[:], rest)
+        w2d_rest = shared("w1s", "w2d_rest", [P, H - P], I32)
+        deal_words(w2d_rest[:], w2_raw[:], rest)
+        w4d = keep.tile([P, N], I32, align_bytes=64)
+        deal_words(w4d[:], w4_raw[:], whole)
+        w1_parts = [w1d[:, part(t)] for t in range(PACK)]
+        w2_parts = [w2d_first[:]] + [w2d_rest[:, part(t)] for t in range(PACK - 1)]
 
-        def bank_tile(b, shape):
-            return psum.tile(shape, F32, tag=f"bank{b}", name=f"bank{b}")
-
-        def product(codes, plane, t, b, c0=0, n=S):
-            bank = bank_tile(b, [P, n])
-            cols = slice(t * P, (t + 1) * P)
+        def product(b, name, codes, plane, t, nodes=slice(0, S)):
+            acc = bank(b, name, [P, nodes.stop - nodes.start])
             nc.tensor.matmul_mx(
-                out=bank[:], lhsT=codes[t].bitcast(FP8X4), lhsT_scale=plane[:, cols],
-                rhs=xg_w[:, c0 : c0 + n].bitcast(FP8X4), rhs_scale=xg_s[:, c0 : c0 + n], start=True, stop=True,
+                out=acc[:], lhsT=codes[t].bitcast(FP8X4), lhsT_scale=plane[:, part(t)],
+                rhs=xg_w[:, nodes].bitcast(FP8X4), rhs_scale=xg_s[:, nodes], start=True, stop=True,
             )
-            return bank
+            return acc
 
-        def add_turned(bank_cols, a, b):
-            nc.tensor.matmul(bank_cols, lhsT=a, rhs=ident[:], start=True, stop=False, is_transpose=True)
-            nc.tensor.matmul(bank_cols, lhsT=b, rhs=ident[:], start=False, stop=True, is_transpose=True)
+        def add_turned(cols, a, b):
+            nc.tensor.matmul(cols, lhsT=a, rhs=ident[:], start=True, stop=False, is_transpose=True)
+            nc.tensor.matmul(cols, lhsT=b, rhs=ident[:], start=False, stop=True, is_transpose=True)
 
-        def placed(name, row, shape, dtype):
-            return turns.tile(shape, dtype, name=name, offset=int(row * ROW), align_bytes=64)
+        e_win = [keep.tile([P, S if t == 0 else 2 * S], F32, name=f"e_win{t}") for t in range(PACK)]
+        h_win = [keep.tile([P, 2 * S if t < 2 else S], F32, name=f"h_win{t}") for t in range(PACK)]
+        y_sb = [e_win[1][:, S:], e_win[2][:, S:], e_win[3][:, S:], h_win[0][:, S:]]
+        key = {(t, i): shared(f"key{t}{i}", f"key{t}{i}", [P, S], F32)[:] for t in range(PACK - 1) for i in range(2) if (t, i) != (2, 1)}
+        key[2, 1] = h_win[1][:, S:]
+        gate = {t: keep.tile([P, 2, S], F32, name=f"gate{t}") for t in (0, 2, 3)}
 
-        key_place = {(0, 0): (0, 1), (1, 0): (2, 2), (3, 1): (4, 5), (0, 1): (1, 1), (1, 1): (12, 1), (2, 0): (13, 1), (2, 1): (26, 1), (3, 0): (9, 1)}
+        e0 = [product(b, f"e0{b}", w2_parts, w2s, 0, nodes) for b, nodes in enumerate(halves)]
+        y0 = [product(2 + b, f"y0{b}", w1_parts, w1s, 0, nodes) for b, nodes in enumerate(halves)]
+        nc.scalar.copy(out=e_win[0][:, halves[0]], in_=e0[0][:])
+        nc.scalar.copy(out=e_win[0][:, halves[1]], in_=e0[1][:])
+        nc.scalar.copy(out=y_sb[0][:, halves[0]], in_=y0[0][:])
+        nc.scalar.copy(out=y_sb[0][:, halves[1]], in_=y0[1][:])
 
-        w3c = keep.tile([P, H], U32, align_bytes=64)
-        w3s = keep.tile([P, H], U8, align_bytes=64)
-        w3d = [w3c[:, t * P : (t + 1) * P] for t in range(PACK)]
-        h_sb = [keep.tile([P, S], F32, name=f"h_sb{t}") for t in range(PACK)]
-        gate = [keep.tile([P, 2, S], F32, name=f"gate{t}") for t in range(PACK)]
-        y_sb = [e_sb[t + 1][:, S : 2 * S] for t in range(PACK - 1)] + [y_last[:]]
-        den_late = keep.tile([P, 2, PACK, P], F32)
-        den_early = [placed(f"den_early{u}", 22 + 2 * u, [P, 2, 2, P], F32) for u in range(2)]
-        key = {}
-        dens = {}
-        inv = {}
-
-        def round_values(half):
-            ms = slice(half * P // 2, (half + 1) * P // 2)
-            nc.scalar.copy(
-                out=w3b[:].rearrange("p t m j -> p m t j")[:, ms], in_=w3_raw[:].rearrange("p j (m t) -> p m t j", t=PACK)[:, ms]
-            )
-
-        def emptied(codes, plane, t, out, b):
-            nc.scalar.copy(out=out, in_=product(codes, plane, t, b)[:])
+        def key_products(t, banks):
+            nc.scalar.copy(out=e_win[t][:, 0:S], in_=product(banks[0], f"e{t}", w2_parts, w2s, t)[:])
+            nc.scalar.copy(out=y_sb[t], in_=product(banks[1], f"y{t}", w1_parts, w1s, t)[:])
 
         def keys(t, i):
-            row, rows = key_place[t, i]
-            key[t, i] = placed(f"key{t}{i}", row, [P, rows * S], F32)
-            n = HALF if t == 0 else S
-            for c in range(0, S, n):
+            for nodes in halves if t == 0 else (slice(0, S),):
                 nc.vector.tensor_tensor(
-                    key[t, i][:, c : c + n], e_sb[t][:].indirect(p_sb[i][:, c // 16 : (c + n) // 16]), y_sb[t][:, c : c + n], ALU.add
+                    key[t, i][:, nodes], e_win[t][:].indirect(entries(lists[i], nodes)), y_sb[t][:, nodes], ALU.add
                 )
 
         def gates(t, i):
-            nc.scalar.activation(out=gate[t][:, i, :], in_=key[t, i][:, 0:S], func=ACT.Sigmoid, scale=3.0)
+            nc.scalar.activation(out=gate[t][:, i, :], in_=key[t, i], func=ACT.Sigmoid, scale=3.0)
+
+        den = {}
 
         def gate_sums(t):
-            dens[t] = bank_tile(t, [P, 4, P])
-            for b in range(4):
-                blk = slice(b * P, (b + 1) * P)
-                add_turned(dens[t][:, b, :], gate[t][:, 0, blk], gate[t][:, 1, blk])
+            u, e = divmod(t, 2)
+            for b in range(PACK):
+                cols = den["early", u][:, b, e, :] if b < 2 else den[("middle", "last")[b - 2]][:, t, :]
+                add_turned(cols, gate[t][:, 0, part(b)], gate[t][:, 1, part(b)])
 
-        def square(t):
-            for out, blocks in ((den_early[t // 2][:, :, t % 2, :], slice(0, 2)), (den_late[:, :, t, :], slice(2, 4))):
-                nc.scalar.activation(out=out, in_=dens[t][:, blocks], func=ACT.Square, bias=0.1)
+        def square(which):
+            if which == ("early", 1):
+                sq = reuse.tile([P, 2, 2, P], F32, name="sq_early1", offset=6 * ROW + ROW // 2, align_bytes=64)
+            elif which == ("early", 0):
+                sq = shared("sq0", "sq_early0", [P, 2, 2, P], F32)
+            elif which == "middle":
+                sq = reuse.tile([P, PACK, P], F32, name="sq_middle", offset=9 * ROW, align_bytes=64)
+            else:
+                sq = keep.tile(list(den[which].shape), F32, name=f"sq{len(squares)}")
+            nc.scalar.activation(out=sq[:], in_=den[which][:], func=ACT.Square, bias=0.1)
+            squares[which] = sq
 
-        def inverse(name, row, den):
-            tile = placed(name, row, [P, *den.shape[1:]], F32)
-            nc.scalar.activation(out=tile[:], in_=den, func=ACT.Abs_reciprocal_sqrt)
-            return tile
+        def inverse(out, in_):
+            nc.scalar.activation(out=out, in_=in_, func=ACT.Abs_reciprocal_sqrt)
 
-        def paired(den):
-            return den.rearrange("j b e p -> j b p e")
-
-        for c, b in ((0, 0), (HALF, 1)):
-            nc.scalar.copy(out=e_sb[0][:, c : c + HALF], in_=product(w2d, w2s, 0, b, c, HALF)[:])
-        nc.vector.tensor_copy(out=y_sb[0][:, 0:HALF], in_=product(w1d, w1s, 0, 2, 0, HALF)[:])
-        nc.scalar.copy(out=y_sb[0][:, HALF:S], in_=product(w1d, w1s, 0, 3, HALF, HALF)[:])
-        emptied(w1d, w1s, 1, y_sb[1], 4)
-        emptied(w1d, w1s, 2, y_sb[2], 5)
-        emptied(w2d, w2s, 1, e_sb[1][:, 0:S], 6)
-        emptied(w2d, w2s, 2, e_sb[2][:, 0:S], 7)
-        keys(0, 0)
-        keys(0, 1)
-        keys(1, 0)
-        keys(1, 1)
-        keys(2, 0)
-        keys(2, 1)
+        squares = {}
+        key_products(1, (4, 5))
+        key_products(2, (6, 7))
+        for t in range(PACK - 1):
+            keys(t, 0)
+            keys(t, 1)
         gates(0, 0)
         gates(0, 1)
+        w3b = keep.tile([P, PACK, P, PACK], BF16, align_bytes=64)
+        for ms in (slice(0, P // 2), slice(P // 2, P)):
+            nc.scalar.copy(
+                out=w3b[:].rearrange("p t m j -> p m t j")[:, ms], in_=w3_raw[:].rearrange("p j (m t) -> p m t j", t=PACK)[:, ms]
+            )
+        w3c = keep.tile([P, H], U32, align_bytes=64)
+        w3s = keep.tile([P, H], U8, align_bytes=64)
+        nc.vector.quantize_mx(out=w3c[:].bitcast(FP8X4), scales=w3s[:], in_=w3b[:].rearrange("p t m j -> p (t m j)"))
+        gate[1] = reuse.tile([P, 2, S], F32, name="gate1", offset=0, align_bytes=64)
+        key[3, 0] = reuse.tile([P, S], F32, name="key30", offset=2 * ROW, align_bytes=64)[:]
+        key[3, 1] = reuse.tile([P, S], F32, name="key31", offset=3 * ROW, align_bytes=64)[:]
+        key_products(3, (0, 1))
+        keys(3, 0)
+        keys(3, 1)
+        w3_parts = [w3c[:, part(t)] for t in range(PACK)]
+        h_acc = [product(2 + t, f"h{t}", w3_parts, w3s, t) for t in range(PACK)]
+
+        def values(t):
+            nc.scalar.copy(out=h_win[t][:, 0:S], in_=h_acc[t][:])
+
+        den["early", 0] = bank(6, "den_early0", [P, 2, 2, P])
+        den["middle"] = bank(7, "den_middle", [P, PACK, P])
+        den["last"] = bank(0, "den_last", [P, PACK, P])
+        den["early", 1] = bank(1, "den_early1", [P, 2, 2, P])
         gate_sums(0)
-        w3b = placed("w3b", 0, [P, PACK, P, PACK], BF16)
-        round_values(0)
-        round_values(1)
-        emptied(w2d, w2s, 3, e_sb[3][:, 0:S], 4)
-        emptied(w1d, w1s, 3, y_sb[3], 5)
         gates(1, 0)
         gates(1, 1)
         gate_sums(1)
-        nc.vector.quantize_mx(out=w3c[:].bitcast(FP8X4), scales=w3s[:], in_=w3b[:].rearrange("p t m j -> p (t m j)"))
-        keys(3, 0)
-        w4d = placed("w4d", 2, [P, N], I32)
-        w4s = placed("w4s", 3, [P, N], U8)
-        deal(w4d[:], w4_raw[:])
-        deal_bytes(w4s[:], w4s_raw[:])
-        keys(3, 1)
+        values(0)
         gates(2, 0)
-        square(0)
         gates(2, 1)
         gate_sums(2)
-        emptied(w3d, w3s, 0, h_sb[0][:], 6)
-        emptied(w3d, w3s, 1, h_sb[1][:], 7)
-        square(1)
         gates(3, 0)
-        emptied(w3d, w3s, 2, h_sb[2][:], 4)
-        emptied(w3d, w3s, 3, h_sb[3][:], 5)
+        values(1)
         gates(3, 1)
         gate_sums(3)
-        square(2)
-        inv_low = inverse("inv_low", 4, paired(den_early[0][:]))
-        square(3)
-        inv_high = inverse("inv_high", 5, paired(den_early[1][:]))
-        inv_third = inverse("inv_third", 6, paired(den_late[:, 0].rearrange("j (u e) p -> j u e p", e=2)))
-        inv_fourth = inverse("inv_fourth", 7, den_late[:, 1])
-        inv[0, 0], inv[0, 1] = inv_low[:], inv_high[:]
-        inv[1, 0], inv[1, 1] = inv_third[:, 0:1], inv_third[:, 1:2]
+        square(("early", 0))
+        values(2)
+        values(3)
+        square(("early", 1))
+        inv_early = [
+            reuse.tile([P, 2, P, 2], F32, name="inv_early0", offset=3 * ROW, align_bytes=64),
+            keep.tile([P, 2, P, 2], F32, name="inv_early1"),
+        ]
+        for u in range(2):
+            inverse(inv_early[u][:], squares["early", u][:].rearrange("j b e p -> j b p e"))
+        square("middle")
+        square("last")
+        inv_turned = keep.tile([P, PACK, P], F32)
+        inverse(inv_turned[:], squares["last"][:])
+
+        def messages(msg, t, nodes):
+            for i in range(2):
+                nc.vector.tensor_tensor(
+                    msg[:, i, :], h_win[t][:].indirect(entries(lists[i], nodes)), gate[t][:, i, nodes], ALU.mult
+                )
+
+        num_early = [bank(2 + u, f"num_early{u}", [P, 2, 2, P]) for u in range(2)]
+        num_middle = bank(4, "num_middle", [P, 2, 2, P])
+        wide = keep.tile([P, 2, 2, S], F32)
+        for t in range(2):
+            messages(wide[:, t], t, slice(0, S))
+            for b in range(2):
+                add_turned(num_early[0][:, b, t, :], wide[:, t, 0, part(b)], wide[:, t, 1, part(b)])
+            add_turned(num_middle[:, 0, t, :], wide[:, t, 0, MIDDLE], wide[:, t, 1, MIDDLE])
+        early = keep.tile([P, 2, 2, HALF], F32)
+        for e in range(2):
+            messages(early[:, e], 2 + e, EARLY)
+            for b in range(2):
+                add_turned(num_early[1][:, b, e, :], early[:, e, 0, part(b)], early[:, e, 1, part(b)])
+
+
+        def normalise(name, num, inv):
+            z = shared(name, name, [P, 2, P, 2], BF16)
+            nc.vector.tensor_tensor(z[:], num[:].rearrange("j a e p -> j a p e"), inv[:], ALU.mult)
+            return z
+
+        def turn_back(b, name, pairs, n, grouped):
+            zt = bank(b, name, [P, 2, n])
+            for (u, blk), z in pairs.items():
+                nc.tensor.transpose(zt[:, u, part(blk)], z.rearrange("j p e -> j (p e)").bitcast(F32), ident[:])
+            nc.scalar.copy(out=grouped[:].bitcast(F32).rearrange("p (j u) -> p j u", u=2), in_=zt[:].rearrange("p u j -> p j u"))
 
         osc = keep.tile([P, S], U8, align_bytes=64)
         out_rows = out_0.rearrange("(p t) j -> p t j", t=PACK)
         out_words = out_1[0].rearrange("p n t -> p (n t)").bitcast(I32)
-        starts = [sum(PIECES[:i]) for i in range(len(PIECES))]
-        nums = {}
-        rounded = {}
-        grouped = {}
         results = {}
-        woven_out = {}
 
-        def messages(k, t, msg):
-            c0, n = starts[k], PIECES[k]
-            for i in range(2):
-                nc.vector.tensor_tensor(
-                    msg[:, i, :], h_sb[t][:].indirect(p_sb[i][:, c0 // 16 : (c0 + n) // 16]),
-                    gate[t][:, i, c0 : c0 + n], ALU.mult,
-                )
-
-        def summed_messages(k, t, msg):
-            messages(k, t, msg)
-            blocks = PIECES[k] // P
-            u, e = divmod(t, 2)
-            if e == 0:
-                nums[k, u] = bank_tile(((1, 2), (3, 5))[k][u], [P, blocks, 2, P])
-            for b in range(blocks):
-                blk = slice(b * P, (b + 1) * P)
-                add_turned(nums[k, u][:, b, e, :], msg[:, 0, blk], msg[:, 1, blk])
-
-        def message_pair(k, t0, row, make):
-            msg = placed(f"msg{k}{t0}", row, [P, 2, 2, P], F32)
-            for t in (t0, t0 + 1):
-                make(k, t, msg[:, t - t0])
-            return msg
-
-        def normalise(k, u):
-            blocks = PIECES[k] // P
-            rounded[k, u] = keep.tile([P, blocks, P, 2], BF16, name=f"zb{k}{u}", align_bytes=64)
-            nc.vector.tensor_tensor(
-                rounded[k, u][:], paired(nums[k, u][:]), inv[k, u], ALU.mult,
-            )
-
-        def turn_back(k):
-            c0, n = starts[k], PIECES[k]
-            zt = bank_tile((0, 4)[k], [P, 2, n])
+        def last_layer(name, nodes, grouped, zs, banks, store):
+            n = nodes.stop - nodes.start
+            zc = keep.tile([P, n], U32, name=f"zc_{name}", align_bytes=64)
+            nc.vector.quantize_mx(out=zc[:].bitcast(FP8X4), scales=zs[:], in_=grouped[:])
+            o_sb = keep.tile([P, PACK, n], F32, name=f"o_{name}")
             for u in range(2):
-                for b in range(n // P):
-                    nc.tensor.transpose(zt[:, u, b * P : (b + 1) * P], rounded[k, u][:, b].rearrange("j p e -> j (p e)").bitcast(F32), ident[:])
-            grouped[k] = placed(f"zg{k}", 11 + 2 * k, [P, n * PACK], BF16)
-            nc.scalar.copy(out=grouped[k][:].bitcast(F32).rearrange("p (j u) -> p j u", u=2), in_=zt[:].rearrange("p u j -> p j u"))
-
-        def last_layer(k):
-            c0, n = starts[k], PIECES[k]
-            zc = keep.tile([P, n], U32, name=f"zc{k}", align_bytes=64)
-            zs = keep.tile([P, n], U8, name=f"zs{k}", align_bytes=64)
-            nc.vector.quantize_mx(out=zc[:].bitcast(FP8X4), scales=zs[:], in_=grouped[k][:])
-            o_sb = keep.tile([P, PACK, n], F32, name=f"o_sb{k}")
-            per_bank = 2
-            for t0 in range(0, PACK, per_bank):
-                bank = bank_tile(((1, 2), (6, 5), (7, 0))[k][t0 // per_bank], [P, per_bank, n])
-                for t in range(t0, t0 + per_bank):
-                    wc = slice(t * P, (t + 1) * P)
+                acc = bank(banks[u], f"out_{name}{u}", [P, 2, n])
+                for e in range(2):
+                    wc = part(2 * u + e)
                     nc.tensor.matmul_mx(
-                        out=bank[:, t - t0, :], lhsT=w4d[:, wc].bitcast(FP8X4), lhsT_scale=w4s[:, wc],
+                        out=acc[:, e, :], lhsT=w4d[:, wc].bitcast(FP8X4), lhsT_scale=w4s[:, wc],
                         rhs=zc[:].bitcast(FP8X4), rhs_scale=zs[:], start=True, stop=True,
                     )
-                nc.scalar.copy(out=o_sb[:, t0 : t0 + per_bank, :], in_=bank[:])
-                if k == 0:
-                    nc.sync.dma_start(out=out_rows[:, t0 : t0 + per_bank, c0 : c0 + n], in_=o_sb[:, t0 : t0 + per_bank, :])
-            if k > 0:
-                (nc.sync if k == 1 else nc.scalar).dma_start(out=out_rows[:, :, c0 : c0 + n], in_=o_sb[:])
-            results[k] = o_sb
+                nc.scalar.copy(out=o_sb[:, 2 * u : 2 * u + 2, :], in_=acc[:])
+                if n > P:
+                    store.dma_start(out=out_rows[:, 2 * u : 2 * u + 2, nodes], in_=o_sb[:, 2 * u : 2 * u + 2, :])
+            if n == P:
+                store.dma_start(out=out_rows[:, :, nodes], in_=o_sb[:])
+            results[name] = o_sb
 
-        def round_result(k, copy):
-            woven_out[k] = placed(f"ob{k}", (27, 16.25, 28)[k], [P, PIECES[k] * PACK], BF16)
-            copy(out=woven_out[k][:].rearrange("p (j t) -> p j t", t=PACK), in_=results[k][:].rearrange("p t j -> p j t"))
+        def rounded(copy, tile, name):
+            copy(out=tile.rearrange("p (j t) -> p j t", t=PACK), in_=results[name][:].rearrange("p t j -> p j t"))
 
-        def planes(k):
-            cols = slice(starts[k], starts[k] + PIECES[k])
-            nc.vector.quantize_mx(out=oc[:, cols].bitcast(FP8X4), scales=osc[:, cols], in_=woven_out[k][:])
+        def planes(nodes, woven):
+            nc.vector.quantize_mx(out=oc[:, nodes].bitcast(FP8X4), scales=osc[:, nodes], in_=woven)
 
+        z_early = [normalise("z_early0", num_early[0], inv_early[0])]
+        w4s = shared("sq0", "w4s", [P, N], U8)
+        deal_bytes(w4s[:], w4s_raw[:], whole)
+        z_early.append(normalise("z_early1", num_early[1], inv_early[1]))
+        zg_early = keep.tile([P, HALF * PACK], BF16, align_bytes=64)
+        turn_back(6, "zt_early", {(u, b): z_early[u][:, b] for u in range(2) for b in range(2)}, HALF, zg_early)
+        inv_middle = shared("z_early1", "inv_middle", [P, 2, P, 2], F32)
+        inverse(inv_middle[:], squares["middle"][:].rearrange("j (u e) p -> j u p e", e=2))
+        middle = reuse.tile([P, 2, 2, P], F32, offset=7 * ROW, align_bytes=64)
+        for e in range(2):
+            messages(middle[:, e], 2 + e, MIDDLE)
+            add_turned(num_middle[:, 1, e, :], middle[:, e, 0, :], middle[:, e, 1, :])
+        last_a = reuse.tile([P, 2, P], F32, offset=6 * ROW + ROW // 2, align_bytes=64)
+        messages(last_a[:], 2, LAST)
+        zs_early = keep.tile([P, HALF], U8, align_bytes=64)
+        last_layer("early", EARLY, zg_early, zs_early, (2, 3), nc.sync)
+        inv_last = bank(5, "inv_last", [P, PACK, P])
         for t in range(PACK):
-            summed_messages(0, t, placed(f"msg0{t}", (18, 21, 19, 23)[t], [P, 2, HALF], F32)[:])
-        message_pair(1, 0, 8, summed_messages)
-        normalise(0, 0)
-        summed_messages(1, 2, placed("msg12", 21.75, [P, 2, P], F32)[:])
-        normalise(0, 1)
-        turn_back(0)
-        summed_messages(1, 3, placed("msg13", 23.75, [P, 2, P], F32)[:])
-        msg_first = placed("msg_first", 24.25, [P, 1, 2, P], F32)
-        messages(2, 0, msg_first[:, 0])
-        for u in range(2):
-            normalise(1, u)
-        turn_back(1)
-        last_layer(0)
-        inv_last = bank_tile(3, [P, PACK, P])
-        for t in range(PACK):
-            nc.tensor.transpose(inv_last[:, t, :], inv_fourth[:, t, :], ident[:])
-        msg_rest = placed("msg_rest", 22.5, [P, 3, 2, P], F32)
-        for t in (1, 2):
-            messages(2, t, msg_rest[:, t - 1])
-        last_layer(1)
-        round_result(0, nc.scalar.copy)
-        messages(2, 3, msg_rest[:, 2])
-        num_last = placed("num_last", 11.5, [P, PACK, P], F32)
-        for ts, msg in ((slice(0, 1), msg_first[:]), (slice(1, 3), msg_rest[:, 0:2]), (slice(3, PACK), msg_rest[:, 2:3])):
-            nc.vector.tensor_tensor(num_last[:, ts, :], msg[:, :, 0, :], msg[:, :, 1, :], ALU.add)
-        grouped[2] = placed("zg2", 16, [P, P * PACK], BF16)
+            nc.tensor.transpose(inv_last[:, t, :], inv_turned[:, t, :], ident[:])
+        last_b = reuse.tile([P, 2, P], F32, offset=9 * ROW, align_bytes=64)
+        messages(last_b[:], 3, LAST)
+        z_middle = normalise("z_middle", num_middle, inv_middle)
+        zg_middle = keep.tile([P, P * PACK], BF16, align_bytes=64)
+        turn_back(1, "zt_middle", {(u, 0): z_middle[:, u] for u in range(2)}, P, zg_middle)
+        num_last = reuse.tile([P, PACK, P], F32, offset=9 * ROW + ROW // 2, align_bytes=64)
+        nc.vector.tensor_tensor(num_last[:, 0:2, :], wide[:, :, 0, LAST], wide[:, :, 1, LAST], ALU.add)
+        nc.vector.tensor_tensor(num_last[:, 2, :], last_a[:, 0, :], last_a[:, 1, :], ALU.add)
+        nc.vector.tensor_tensor(num_last[:, 3, :], last_b[:, 0, :], last_b[:, 1, :], ALU.add)
+        zs_middle = keep.tile([P, P], U8, align_bytes=64)
+        last_layer("middle", MIDDLE, zg_middle, zs_middle, (6, 7), nc.sync)
+        zg_last = reuse.tile([P, P * PACK], BF16, offset=4 * ROW, align_bytes=64)
         nc.vector.tensor_tensor(
-            grouped[2][:].rearrange("p (a c t) -> p a t c", c=2, t=PACK),
+            zg_last[:].rearrange("p (a c t) -> p a t c", c=2, t=PACK),
             num_last[:].rearrange("p t (a c) -> p a t c", c=2), inv_last[:].rearrange("p t (a c) -> p a t c", c=2), ALU.mult,
         )
-        last_layer(2)
-        oc = placed("oc", 15.25, [P, S], U32)
-        round_result(1, nc.vector.tensor_copy)
-        planes(1)
-        planes(0)
-        nc.sync.dma_start(out=out_words[:, 0 : S - P], in_=oc[:, 0 : S - P].bitcast(I32))
-        round_result(2, nc.vector.tensor_copy)
-        planes(2)
-        nc.sync.dma_start(out=out_words[:, S - P : S], in_=oc[:, S - P : S].bitcast(I32))
+        zs_last = keep.tile([P, P], U8, align_bytes=64)
+        last_layer("last", LAST, zg_last, zs_last, (0, 4), nc.scalar)
+        oc = keep.tile([P, S], U32, align_bytes=64)
+        woven_early = reuse.tile([P, HALF * PACK], BF16, offset=4 * ROW, align_bytes=64)
+        rounded(nc.vector.tensor_copy, woven_early[:], "early")
+        planes(EARLY, woven_early[:])
+        nc.sync.dma_start(out=out_words[:, EARLY], in_=oc[:, EARLY].bitcast(I32))
+        woven_late = keep.tile([P, 2, P * PACK], BF16, align_bytes=64)
+        rounded(nc.vector.tensor_copy, woven_late[:, 0, :], "middle")
+        rounded(nc.vector.tensor_copy, woven_late[:, 1, :], "last")
+        planes(slice(HALF, S), woven_late[:].rearrange("p b c -> p (b c)"))
+        nc.sync.dma_start(out=out_words[:, HALF:S], in_=oc[:, HALF:S].bitcast(I32))
         out_planes = out_2[0].bitcast(I32)
         for q in range(4):
             engine = nc.sync if q % 2 == 0 else nc.scalar

@@ -21,8 +21,7 @@ PACK = 4
 HALF = S // 2
 ROW = 4 * S
 EARLY = slice(0, 2 * P)
-MIDDLE = slice(2 * P, 3 * P)
-LAST = slice(3 * P, 4 * P)
+LATE = (slice(2 * P, 3 * P), slice(3 * P, 4 * P))
 
 
 def tile_picked_ggnorm_none_po_kernel(
@@ -34,9 +33,9 @@ def tile_picked_ggnorm_none_po_kernel(
     def words_of(dram):
         return dram[0].rearrange("p n t -> p (n t)").bitcast(I32)
 
-    def load_scale_rows(plane, dram):
+    def load_scale_rows(plane, dram, quadrants=range(4)):
         rows = dram[0].bitcast(I32)
-        for q in range(4):
+        for q in quadrants:
             nc.sync.dma_start(
                 out=plane[32 * q : 32 * q + 32, :].bitcast(I32),
                 in_=rows[4 * q : 4 * q + 4, :].unsqueeze(0).broadcast_to([8, 4, rows.shape[1]]),
@@ -82,7 +81,7 @@ def tile_picked_ggnorm_none_po_kernel(
         w1_raw = keep.tile([P, H], I32, align_bytes=64)
         w2_raw = keep.tile([P, H], I32, align_bytes=64)
         w4_raw = keep.tile([P, N], I32, align_bytes=64)
-        w3_raw = reuse.tile([P, PACK, H], F32, offset=0, align_bytes=64)
+        w3_raw = reuse.tile([P, PACK, H], F32, offset=2 * ROW, align_bytes=64)
         warm = keep.tile([P, 8], F32)
 
         nc.vector.memset(warm[:], 0.0)
@@ -90,15 +89,16 @@ def tile_picked_ggnorm_none_po_kernel(
 
         nc.sync.dma_start(offs_sb[:], offs)
         load_scale_rows(xs, x_scales)
+        load_scale_rows(w2s_raw, w2_scales, range(2))
         nc.sync.dma_start(out=xw[:].bitcast(I32), in_=words_of(x_words))
-        load_scale_rows(w2s_raw, w2_scales)
+        load_scale_rows(w2s_raw, w2_scales, range(2, 4))
         nc.sync.dma_start(out=w2_raw[:], in_=words_of(w2_words))
         nc.sync.dma_start(out=w1_raw[:], in_=words_of(w1_words))
-        nc.sync.dma_start(out=w4_raw[:], in_=words_of(w4_words))
         load_scale_rows(w1s_raw, w1_scales)
         nc.sync.dma_start(lists[0][:], p1)
         nc.sync.dma_start(lists[1][:], p2)
         nc.sync.dma_start(out=w3_raw[:], in_=w3.rearrange("(p j) c -> p j c", j=PACK))
+        nc.sync.dma_start(out=w4_raw[:], in_=words_of(w4_words))
         load_scale_rows(w4s_raw, w4_scales)
 
         ident = keep.tile([P, P], F32)
@@ -106,7 +106,7 @@ def tile_picked_ggnorm_none_po_kernel(
 
         xg_s = keep.tile([P, S], U8, align_bytes=64)
         xg_w = keep.tile([P, S], U32, align_bytes=64)
-        w1d = keep.tile([P, H], I32, align_bytes=64)
+        w1d = shared("w1d", "w1d", [P, H], I32)
         w2d_first = keep.tile([P, P], I32, align_bytes=64)
         first, rest, whole = slice(0, 1), slice(1, PACK), slice(0, PACK)
         halves = (slice(0, HALF), slice(HALF, S))
@@ -116,17 +116,13 @@ def tile_picked_ggnorm_none_po_kernel(
             nc.vector.tensor_copy(out=xg_w[:, nodes], in_=xw[:].indirect(entries(offs_sb, nodes)))
         w1s = keep.tile([P, H], U8, align_bytes=64)
         w2s = keep.tile([P, H], U8, align_bytes=64)
-        deal_bytes(w2s[:, 0:P], w2s_raw[:], first)
+        deal_bytes(w2s[:], w2s_raw[:], whole)
         deal_words(w2d_first[:], w2_raw[:], first)
-        deal_words(w1d[:, 0:P], w1_raw[:], first)
+        deal_words(w1d[:], w1_raw[:], whole)
         deal_bytes(w1s[:, 0:P], w1s_raw[:], first)
         deal_bytes(w1s[:, P:H], w1s_raw[:], rest)
-        deal_bytes(w2s[:, P:H], w2s_raw[:], rest)
-        deal_words(w1d[:, P:H], w1_raw[:], rest)
         w2d_rest = shared("w1s", "w2d_rest", [P, H - P], I32)
         deal_words(w2d_rest[:], w2_raw[:], rest)
-        w4d = keep.tile([P, N], I32, align_bytes=64)
-        deal_words(w4d[:], w4_raw[:], whole)
         w1_parts = [w1d[:, part(t)] for t in range(PACK)]
         w2_parts = [w2d_first[:]] + [w2d_rest[:, part(t)] for t in range(PACK - 1)]
 
@@ -145,15 +141,15 @@ def tile_picked_ggnorm_none_po_kernel(
         e_win = [keep.tile([P, S if t == 0 else 2 * S], F32, name=f"e_win{t}") for t in range(PACK)]
         h_win = [keep.tile([P, 2 * S if t < 2 else S], F32, name=f"h_win{t}") for t in range(PACK)]
         y_sb = [e_win[1][:, S:], e_win[2][:, S:], e_win[3][:, S:], h_win[0][:, S:]]
-        key = {(t, i): shared(f"key{t}{i}", f"key{t}{i}", [P, S], F32)[:] for t in range(PACK - 1) for i in range(2) if (t, i) != (2, 1)}
-        key[2, 1] = h_win[1][:, S:]
-        gate = {t: keep.tile([P, 2, S], F32, name=f"gate{t}") for t in (0, 2, 3)}
+        key = {(t, i): keep.tile([P, S], F32, name=f"key{t}{i}")[:] for t in range(2) for i in range(2)}
+        key[2, 0] = h_win[1][:, S:]
+        gate = {t: keep.tile([P, 2, S], F32, name=f"gate{t}") for t in (2, 3)}
 
         e0 = [product(b, f"e0{b}", w2_parts, w2s, 0, nodes) for b, nodes in enumerate(halves)]
         y0 = [product(2 + b, f"y0{b}", w1_parts, w1s, 0, nodes) for b, nodes in enumerate(halves)]
         nc.scalar.copy(out=e_win[0][:, halves[0]], in_=e0[0][:])
         nc.scalar.copy(out=e_win[0][:, halves[1]], in_=e0[1][:])
-        nc.scalar.copy(out=y_sb[0][:, halves[0]], in_=y0[0][:])
+        nc.vector.tensor_copy(out=y_sb[0][:, halves[0]], in_=y0[0][:])
         nc.scalar.copy(out=y_sb[0][:, halves[1]], in_=y0[1][:])
 
         def key_products(t, banks):
@@ -174,124 +170,113 @@ def tile_picked_ggnorm_none_po_kernel(
         def gate_sums(t):
             u, e = divmod(t, 2)
             for b in range(PACK):
-                cols = den["early", u][:, b, e, :] if b < 2 else den[("middle", "last")[b - 2]][:, t, :]
-                add_turned(cols, gate[t][:, 0, part(b)], gate[t][:, 1, part(b)])
+                add_turned(den[u, b // 2][:, b % 2, e, :], gate[t][:, 0, part(b)], gate[t][:, 1, part(b)])
 
-        def square(which):
-            if which == ("early", 1):
-                sq = reuse.tile([P, 2, 2, P], F32, name="sq_early1", offset=6 * ROW + ROW // 2, align_bytes=64)
-            elif which == ("early", 0):
-                sq = shared("sq0", "sq_early0", [P, 2, 2, P], F32)
-            elif which == "middle":
-                sq = reuse.tile([P, PACK, P], F32, name="sq_middle", offset=9 * ROW, align_bytes=64)
-            else:
-                sq = keep.tile(list(den[which].shape), F32, name=f"sq{len(squares)}")
-            nc.scalar.activation(out=sq[:], in_=den[which][:], func=ACT.Square, bias=0.1)
-            squares[which] = sq
+        def square(u, c):
+            sq = reuse.tile([P, 2, 2, P], F32, name=f"sq{u}{c}", offset=(8 + u + 4 * c) * ROW, align_bytes=64)
+            nc.scalar.activation(out=sq[:], in_=den[u, c][:], func=ACT.Square, bias=0.1)
+            return sq[:]
 
-        def inverse(out, in_):
-            nc.scalar.activation(out=out, in_=in_, func=ACT.Abs_reciprocal_sqrt)
+        def inverse(out, sq):
+            nc.scalar.activation(out=out, in_=sq, func=ACT.Abs_reciprocal_sqrt)
 
-        squares = {}
         key_products(1, (4, 5))
-        key_products(2, (6, 7))
-        for t in range(PACK - 1):
+        key_products(2, (0, 2))
+        for t in range(2):
             keys(t, 0)
             keys(t, 1)
-        gates(0, 0)
-        gates(0, 1)
-        w3b = keep.tile([P, PACK, P, PACK], BF16, align_bytes=64)
-        for ms in (slice(0, P // 2), slice(P // 2, P)):
+        keys(2, 0)
+        w3b = keep.tile([P, 2, 2, P, PACK], BF16, align_bytes=64)
+        for u in range(2):
             nc.scalar.copy(
-                out=w3b[:].rearrange("p t m j -> p m t j")[:, ms], in_=w3_raw[:].rearrange("p j (m t) -> p m t j", t=PACK)[:, ms]
+                out=w3b[:, u].rearrange("p e m j -> p m j e"),
+                in_=w3_raw[:].rearrange("p j (m u e) -> p u m j e", u=2, e=2)[:, u],
             )
         w3c = keep.tile([P, H], U32, align_bytes=64)
         w3s = keep.tile([P, H], U8, align_bytes=64)
-        nc.vector.quantize_mx(out=w3c[:].bitcast(FP8X4), scales=w3s[:], in_=w3b[:].rearrange("p t m j -> p (t m j)"))
-        gate[1] = reuse.tile([P, 2, S], F32, name="gate1", offset=0, align_bytes=64)
-        key[3, 0] = reuse.tile([P, S], F32, name="key30", offset=2 * ROW, align_bytes=64)[:]
-        key[3, 1] = reuse.tile([P, S], F32, name="key31", offset=3 * ROW, align_bytes=64)[:]
-        key_products(3, (0, 1))
+        nc.vector.quantize_mx(out=w3c[:].bitcast(FP8X4), scales=w3s[:], in_=w3b[:].rearrange("p u e m j -> p (u e m j)"))
+        for t in range(2):
+            gate[t] = reuse.tile([P, 2, S], F32, name=f"gate{t}", offset=5 * t * ROW + ROW // 2, align_bytes=64)
+        for row, (t, i) in enumerate(((2, 1), (3, 0), (3, 1))):
+            key[t, i] = reuse.tile([P, S], F32, name=f"key{t}{i}", offset=(2 + row) * ROW + ROW // 2, align_bytes=64)[:]
+        keys(2, 1)
+        key_products(3, (1, 3))
         keys(3, 0)
         keys(3, 1)
         w3_parts = [w3c[:, part(t)] for t in range(PACK)]
-        h_acc = [product(2 + t, f"h{t}", w3_parts, w3s, t) for t in range(PACK)]
+        h_acc = [product(b, f"h{t}", w3_parts, w3s, t) for t, b in enumerate((4, 5, 0, 2))]
 
         def values(t):
             nc.scalar.copy(out=h_win[t][:, 0:S], in_=h_acc[t][:])
 
-        den["early", 0] = bank(6, "den_early0", [P, 2, 2, P])
-        den["middle"] = bank(7, "den_middle", [P, PACK, P])
-        den["last"] = bank(0, "den_last", [P, PACK, P])
-        den["early", 1] = bank(1, "den_early1", [P, 2, 2, P])
+        for (u, c), b in (((0, 0), 6), ((0, 1), 7), ((1, 0), 1), ((1, 1), 3)):
+            den[u, c] = bank(b, f"den{u}{c}", [P, 2, 2, P])
+        gates(0, 0)
+        gates(0, 1)
         gate_sums(0)
+        values(0)
         gates(1, 0)
         gates(1, 1)
         gate_sums(1)
-        values(0)
+        values(1)
         gates(2, 0)
         gates(2, 1)
         gate_sums(2)
         gates(3, 0)
-        values(1)
         gates(3, 1)
         gate_sums(3)
-        square(("early", 0))
+        paired = "j b e p -> j b p e"
+        inv = {(0, 0): reuse.tile([P, 2, P, 2], F32, name="inv00", offset=4 * ROW + ROW // 2, align_bytes=64)}
+        sq_first = square(0, 0)
         values(2)
         values(3)
-        square(("early", 1))
-        inv_early = [
-            reuse.tile([P, 2, P, 2], F32, name="inv_early0", offset=3 * ROW, align_bytes=64),
-            keep.tile([P, 2, P, 2], F32, name="inv_early1"),
-        ]
-        for u in range(2):
-            inverse(inv_early[u][:], squares["early", u][:].rearrange("j b e p -> j b p e"))
-        square("middle")
-        square("last")
-        inv_turned = keep.tile([P, PACK, P], F32)
-        inverse(inv_turned[:], squares["last"][:])
+        inverse(inv[0, 0][:], sq_first.rearrange(paired))
+        for u, c in ((1, 0), (0, 1)):
+            inv[u, c] = keep.tile([P, 2, P, 2], F32, name=f"inv{u}{c}")
+            inverse(inv[u, c][:], square(u, c).rearrange(paired))
+        sq_last = square(1, 1)
+
+        def message(msg, t, i, nodes):
+            nc.vector.tensor_tensor(msg, h_win[t][:].indirect(entries(lists[i], nodes)), gate[t][:, i, nodes], ALU.mult)
 
         def messages(msg, t, nodes):
             for i in range(2):
-                nc.vector.tensor_tensor(
-                    msg[:, i, :], h_win[t][:].indirect(entries(lists[i], nodes)), gate[t][:, i, nodes], ALU.mult
-                )
+                message(msg[:, i, :], t, i, nodes)
 
-        num_early = [bank(2 + u, f"num_early{u}", [P, 2, 2, P]) for u in range(2)]
-        num_middle = bank(4, "num_middle", [P, 2, 2, P])
+        num = {(0, 0): bank(4, "num00", [P, 2, 2, P]), (1, 0): bank(0, "num10", [P, 2, 2, P])}
         wide = keep.tile([P, 2, 2, S], F32)
-        for t in range(2):
-            messages(wide[:, t], t, slice(0, S))
+        early = reuse.tile([P, 2, 2, HALF], F32, offset=10 * ROW, align_bytes=64)
+
+        def message_sums(u, c, e, msg):
             for b in range(2):
-                add_turned(num_early[0][:, b, t, :], wide[:, t, 0, part(b)], wide[:, t, 1, part(b)])
-            add_turned(num_middle[:, 0, t, :], wide[:, t, 0, MIDDLE], wide[:, t, 1, MIDDLE])
-        early = keep.tile([P, 2, 2, HALF], F32)
+                add_turned(num[u, c][:, b, e, :], msg[:, e, 0, part(2 * c + b)], msg[:, e, 1, part(2 * c + b)])
+
+        for e in range(2):
+            messages(wide[:, e], e, slice(0, S))
+            message_sums(0, 0, e, wide)
         for e in range(2):
             messages(early[:, e], 2 + e, EARLY)
-            for b in range(2):
-                add_turned(num_early[1][:, b, e, :], early[:, e, 0, part(b)], early[:, e, 1, part(b)])
+            message_sums(1, 0, e, early)
 
-
-        def normalise(name, num, inv):
-            z = shared(name, name, [P, 2, P, 2], BF16)
-            nc.vector.tensor_tensor(z[:], num[:].rearrange("j a e p -> j a p e"), inv[:], ALU.mult)
+        def normalise(u, c, z):
+            nc.vector.tensor_tensor(z[:], num[u, c][:].rearrange(paired), inv[u, c][:], ALU.mult)
             return z
 
-        def turn_back(b, name, pairs, n, grouped):
-            zt = bank(b, name, [P, 2, n])
-            for (u, blk), z in pairs.items():
-                nc.tensor.transpose(zt[:, u, part(blk)], z.rearrange("j p e -> j (p e)").bitcast(F32), ident[:])
-            nc.scalar.copy(out=grouped[:].bitcast(F32).rearrange("p (j u) -> p j u", u=2), in_=zt[:].rearrange("p u j -> p j u"))
+        def turned_back(cols, z):
+            for b in range(2):
+                nc.tensor.transpose(cols[:, part(b)], z[:, b].rearrange("j p e -> j (p e)").bitcast(F32), ident[:])
 
         osc = keep.tile([P, S], U8, align_bytes=64)
+        oc = keep.tile([P, S], U32, align_bytes=64)
         out_rows = out_0.rearrange("(p t) j -> p t j", t=PACK)
         out_words = out_1[0].rearrange("p n t -> p (n t)").bitcast(I32)
         results = {}
 
-        def last_layer(name, nodes, grouped, zs, banks, store):
+        def last_layer(name, nodes, grouped, banks, store):
             n = nodes.stop - nodes.start
             zc = keep.tile([P, n], U32, name=f"zc_{name}", align_bytes=64)
-            nc.vector.quantize_mx(out=zc[:].bitcast(FP8X4), scales=zs[:], in_=grouped[:])
+            zs = keep.tile([P, n], U8, name=f"zs_{name}", align_bytes=64)
+            nc.vector.quantize_mx(out=zc[:].bitcast(FP8X4), scales=zs[:], in_=grouped)
             o_sb = keep.tile([P, PACK, n], F32, name=f"o_{name}")
             for u in range(2):
                 acc = bank(banks[u], f"out_{name}{u}", [P, 2, n])
@@ -308,59 +293,71 @@ def tile_picked_ggnorm_none_po_kernel(
                 store.dma_start(out=out_rows[:, :, nodes], in_=o_sb[:])
             results[name] = o_sb
 
-        def rounded(copy, tile, name):
-            copy(out=tile.rearrange("p (j t) -> p j t", t=PACK), in_=results[name][:].rearrange("p t j -> p j t"))
+        def rounded(tile, name):
+            nc.vector.tensor_copy(
+                out=tile.rearrange("p (c i t) -> p c t i", i=PACK, t=PACK),
+                in_=results[name][:].rearrange("p t (c i) -> p c t i", i=PACK),
+            )
 
         def planes(nodes, woven):
             nc.vector.quantize_mx(out=oc[:, nodes].bitcast(FP8X4), scales=osc[:, nodes], in_=woven)
 
-        z_early = [normalise("z_early0", num_early[0], inv_early[0])]
-        w4s = shared("sq0", "w4s", [P, N], U8)
+        w4d = reuse.tile([P, N], I32, offset=7 * ROW + ROW // 2, align_bytes=64)
+        w4s = reuse.tile([P, N], U8, offset=8 * ROW + ROW // 2, align_bytes=64)
+        deal_words(w4d[:], w4_raw[:], whole)
         deal_bytes(w4s[:], w4s_raw[:], whole)
-        z_early.append(normalise("z_early1", num_early[1], inv_early[1]))
+        zt_early = bank(6, "zt_early", [P, 2, HALF])
+        zt_late = bank(7, "zt_late", [P, HALF])
         zg_early = keep.tile([P, HALF * PACK], BF16, align_bytes=64)
-        turn_back(6, "zt_early", {(u, b): z_early[u][:, b] for u in range(2) for b in range(2)}, HALF, zg_early)
-        inv_middle = shared("z_early1", "inv_middle", [P, 2, P, 2], F32)
-        inverse(inv_middle[:], squares["middle"][:].rearrange("j (u e) p -> j u p e", e=2))
-        middle = reuse.tile([P, 2, 2, P], F32, offset=7 * ROW, align_bytes=64)
+        zg_late = keep.tile([P, HALF * PACK], BF16, align_bytes=64)
+        for u in range(2):
+            turned_back(zt_early[:, u, :], normalise(u, 0, shared(f"z{u}", f"z{u}0", [P, 2, P, 2], BF16)))
+        nc.scalar.copy(out=zg_early[:].bitcast(F32).rearrange("p (j u) -> p j u", u=2), in_=zt_early[:].rearrange("p u j -> p j u"))
+        inv_turned = shared("z1", "inv_turned", [P, 2, 2, P], F32)
+        inverse(inv_turned[:], sq_last)
+        num[0, 1] = bank(4, "num01", [P, 2, 2, P])
         for e in range(2):
-            messages(middle[:, e], 2 + e, MIDDLE)
-            add_turned(num_middle[:, 1, e, :], middle[:, e, 0, :], middle[:, e, 1, :])
-        last_a = reuse.tile([P, 2, P], F32, offset=6 * ROW + ROW // 2, align_bytes=64)
-        messages(last_a[:], 2, LAST)
-        zs_early = keep.tile([P, HALF], U8, align_bytes=64)
-        last_layer("early", EARLY, zg_early, zs_early, (2, 3), nc.sync)
-        inv_last = bank(5, "inv_last", [P, PACK, P])
-        for t in range(PACK):
-            nc.tensor.transpose(inv_last[:, t, :], inv_turned[:, t, :], ident[:])
-        last_b = reuse.tile([P, 2, P], F32, offset=9 * ROW, align_bytes=64)
-        messages(last_b[:], 3, LAST)
-        z_middle = normalise("z_middle", num_middle, inv_middle)
-        zg_middle = keep.tile([P, P * PACK], BF16, align_bytes=64)
-        turn_back(1, "zt_middle", {(u, 0): z_middle[:, u] for u in range(2)}, P, zg_middle)
-        num_last = reuse.tile([P, PACK, P], F32, offset=9 * ROW + ROW // 2, align_bytes=64)
-        nc.vector.tensor_tensor(num_last[:, 0:2, :], wide[:, :, 0, LAST], wide[:, :, 1, LAST], ALU.add)
-        nc.vector.tensor_tensor(num_last[:, 2, :], last_a[:, 0, :], last_a[:, 1, :], ALU.add)
-        nc.vector.tensor_tensor(num_last[:, 3, :], last_b[:, 0, :], last_b[:, 1, :], ALU.add)
-        zs_middle = keep.tile([P, P], U8, align_bytes=64)
-        last_layer("middle", MIDDLE, zg_middle, zs_middle, (6, 7), nc.sync)
-        zg_last = reuse.tile([P, P * PACK], BF16, offset=4 * ROW, align_bytes=64)
-        nc.vector.tensor_tensor(
-            zg_last[:].rearrange("p (a c t) -> p a t c", c=2, t=PACK),
-            num_last[:].rearrange("p t (a c) -> p a t c", c=2), inv_last[:].rearrange("p t (a c) -> p a t c", c=2), ALU.mult,
-        )
-        zs_last = keep.tile([P, P], U8, align_bytes=64)
-        last_layer("last", LAST, zg_last, zs_last, (0, 4), nc.scalar)
-        oc = keep.tile([P, S], U32, align_bytes=64)
-        woven_early = reuse.tile([P, HALF * PACK], BF16, offset=4 * ROW, align_bytes=64)
-        rounded(nc.vector.tensor_copy, woven_early[:], "early")
-        planes(EARLY, woven_early[:])
-        nc.sync.dma_start(out=out_words[:, EARLY], in_=oc[:, EARLY].bitcast(I32))
-        woven_late = keep.tile([P, 2, P * PACK], BF16, align_bytes=64)
-        rounded(nc.vector.tensor_copy, woven_late[:, 0, :], "middle")
-        rounded(nc.vector.tensor_copy, woven_late[:, 1, :], "last")
-        planes(slice(HALF, S), woven_late[:].rearrange("p b c -> p (b c)"))
-        nc.sync.dma_start(out=out_words[:, HALF:S], in_=oc[:, HALF:S].bitcast(I32))
+            message_sums(0, 1, e, wide)
+        late = [reuse.tile([P, 2, 2, P], F32, name="late0", offset=10 * ROW - ROW // 2, align_bytes=64)]
+        messages(late[0][:, 0], 2, LATE[0])
+        messages(late[0][:, 1], 3, LATE[0])
+        turned_back(zt_late[:], normalise(0, 1, keep.tile([P, 2, P, 2], BF16, name="z01", align_bytes=64)))
+        nc.scalar.copy(out=zg_late[:].bitcast(F32).rearrange("p (j u) -> p j u", u=2)[:, :, 0], in_=zt_late[:])
+        inv_late = bank(2, "inv_late", [P, 2, 2, P])
+        for b in range(2):
+            for e in range(2):
+                nc.tensor.transpose(inv_late[:, b, e, :], inv_turned[:, b, e, :], ident[:])
+
+        def summed(b, total):
+            nc.vector.tensor_tensor(total[:], late[b][:, :, 0, :], late[b][:, :, 1, :], ALU.add)
+            return total
+
+        def scaled(b, total):
+            nc.vector.tensor_tensor(
+                zg_late[:].rearrange("p (b j u e) -> p b u j e", b=2, u=2, e=2)[:, b, 1],
+                total[:].rearrange("p e j -> p j e"), inv_late[:, b].rearrange("p e j -> p j e"), ALU.mult,
+            )
+
+        total_third = summed(0, keep.tile([P, 2, P], F32, name="total_third"))
+        last_layer("early", EARLY, zg_early[:], (5, 0), nc.sync)
+        late.append(reuse.tile([P, 2, 2, P], F32, name="late1", offset=13 * ROW, align_bytes=64))
+        for e in range(2):
+            messages(late[1][:, e], 2 + e, LATE[1])
+        scaled(0, total_third)
+        total_fourth = summed(1, shared("z1", "total_fourth", [P, 2, P], F32))
+        last_layer("third", LATE[0], zg_late[:, 0 : P * PACK], (1, 3), nc.sync)
+        scaled(1, total_fourth)
+        last_layer("fourth", LATE[1], zg_late[:, P * PACK :], (4, 6), nc.scalar)
+        woven = shared("z1", "woven", [P, 3 * P * PACK], BF16)
+        rounded(woven[:, 0 : HALF * PACK], "early")
+        rounded(woven[:, HALF * PACK :], "third")
+        planes(EARLY, woven[:, 0 : HALF * PACK])
+        planes(LATE[0], woven[:, HALF * PACK :])
+        nc.sync.dma_start(out=out_words[:, 0 : S - P], in_=oc[:, 0 : S - P].bitcast(I32))
+        woven_last = keep.tile([P, P * PACK], BF16, align_bytes=64)
+        rounded(woven_last[:], "fourth")
+        planes(LATE[1], woven_last[:])
+        nc.sync.dma_start(out=out_words[:, LATE[1]], in_=oc[:, LATE[1]].bitcast(I32))
         out_planes = out_2[0].bitcast(I32)
         for q in range(4):
             engine = nc.sync if q % 2 == 0 else nc.scalar

@@ -257,6 +257,8 @@ def tile_picked_ggnorm_none_po_kernel(
         for e in range(2):
             messages(early[:, e], 2 + e, EARLY)
             message_sums(1, 0, e, early)
+        num[0, 1] = bank(1, "num01", [P, 2, 2, P])
+        message_sums(0, 1, 0, wide)
 
         def normalise(u, c, z):
             nc.vector.tensor_tensor(z[:], num[u, c][:].rearrange(paired), inv[u, c][:], ALU.mult)
@@ -315,13 +317,12 @@ def tile_picked_ggnorm_none_po_kernel(
         nc.scalar.copy(out=zg_early[:].bitcast(F32).rearrange("p (j u) -> p j u", u=2), in_=zt_early[:].rearrange("p u j -> p j u"))
         inv_turned = shared("z1", "inv_turned", [P, 2, 2, P], F32)
         inverse(inv_turned[:], sq_last)
-        num[0, 1] = bank(4, "num01", [P, 2, 2, P])
-        for e in range(2):
-            message_sums(0, 1, e, wide)
+        message_sums(0, 1, 1, wide)
         late = [reuse.tile([P, 2, 2, P], F32, name="late0", offset=10 * ROW - ROW // 2, align_bytes=64)]
         messages(late[0][:, 0], 2, LATE[0])
         messages(late[0][:, 1], 3, LATE[0])
-        turned_back(zt_late[:], normalise(0, 1, keep.tile([P, 2, P, 2], BF16, name="z01", align_bytes=64)))
+        z01 = keep.tile([P, 2, P, 2], BF16, align_bytes=64)
+        turned_back(zt_late[:], normalise(0, 1, z01))
         nc.scalar.copy(out=zg_late[:].bitcast(F32).rearrange("p (j u) -> p j u", u=2)[:, :, 0], in_=zt_late[:])
         inv_late = bank(2, "inv_late", [P, 2, 2, P])
         for b in range(2):
@@ -352,12 +353,12 @@ def tile_picked_ggnorm_none_po_kernel(
         rounded(woven[:, 0 : HALF * PACK], "early")
         rounded(woven[:, HALF * PACK :], "third")
         planes(EARLY, woven[:, 0 : HALF * PACK])
+        nc.sync.dma_start(out=out_words[:, EARLY], in_=oc[:, EARLY].bitcast(I32))
         planes(LATE[0], woven[:, HALF * PACK :])
-        nc.sync.dma_start(out=out_words[:, 0 : S - P], in_=oc[:, 0 : S - P].bitcast(I32))
         woven_last = keep.tile([P, P * PACK], BF16, align_bytes=64)
         rounded(woven_last[:], "fourth")
         planes(LATE[1], woven_last[:])
-        nc.sync.dma_start(out=out_words[:, LATE[1]], in_=oc[:, LATE[1]].bitcast(I32))
+        nc.sync.dma_start(out=out_words[:, HALF:S], in_=oc[:, HALF:S].bitcast(I32))
         out_planes = out_2[0].bitcast(I32)
         for q in range(4):
             engine = nc.sync if q % 2 == 0 else nc.scalar

from contextlib import ExitStack

import concourse.mybir as mybir
from concourse.masks import make_identity

K, T, S, N, H = 512, 2048, 512, 512, 512
FLOPS = 4 * 2 * 512 * 512 * 512

F32 = mybir.dt.float32
BF16 = mybir.dt.bfloat16
I32 = mybir.dt.int32
U32 = mybir.dt.uint32
U16 = mybir.dt.uint16
U8 = mybir.dt.uint8
FP8X4 = mybir.dt.float8_e4m3fn_x4
ACT = mybir.ActivationFunctionType
ALU = mybir.AluOpType

P = 128
PACK = 4
HALF = S // 2
ROW = 4 * S
EARLY = slice(0, 2 * P)
LATE = (slice(2 * P, 3 * P), slice(3 * P, 4 * P))


def tile_picked_ggnorm_none_po_kernel(
    tc, x_words, x_scales, w1_words, w1_scales, w2_words, w2_scales, w3, w4_words, w4_scales, offs, p1, p2,
    out_0, out_1, out_2,
):
    nc = tc.nc

    def words_of(dram):
        return dram[0].rearrange("p n t -> p (n t)").bitcast(I32)

    def load_scale_rows(plane, dram, quadrants=range(4)):
        rows = dram[0].bitcast(I32)
        for q in quadrants:
            nc.sync.dma_start(
                out=plane[32 * q : 32 * q + 32, :].bitcast(I32),
                in_=rows[4 * q : 4 * q + 4, :].unsqueeze(0).broadcast_to([8, 4, rows.shape[1]]),
            )

    def deal_words(out, in_, ts):
        nc.vector.tensor_copy(
            out=out.rearrange("p (t m) -> p m t", t=ts.stop - ts.start),
            in_=in_.rearrange("p (m t) -> p m t", t=PACK)[:, :, ts],
        )

    def deal_bytes(out, in_, ts):
        nc.vector.tensor_copy(
            out=out.rearrange("p (t m) -> p t m", t=ts.stop - ts.start),
            in_=in_.rearrange("p (m t) -> p t m", t=PACK)[:, ts],
        )

    def entries(offsets, nodes):
        return offsets[:, nodes.start // 16 : nodes.stop // 16]

    def part(t):
        return slice(t * P, (t + 1) * P)

    with ExitStack() as ctx:
        keep = ctx.enter_context(tc.tile_pool(name="keep", bufs=1))
        turns = ctx.enter_context(tc.tile_pool(name="turns", bufs=1))
        reuse = ctx.enter_context(tc.tile_pool(name="reuse", bufs=1))
        psum = ctx.enter_context(tc.psum_pool(name="psum", bufs=1))

        def shared(tag, name, shape, dtype):
            return turns.tile(shape, dtype, tag=tag, name=name, align_bytes=64)

        def bank(b, name, shape):
            return psum.tile(shape, F32, tag=f"bank{b}", name=name)

        offs_sb = keep.tile([P, S // 16], U16)
        lists = [keep.tile([P, S // 16], U16, name=f"p{i}_sb") for i in (1, 2)]
        xw = keep.tile([P, T], U32, align_bytes=64)
        xs = keep.tile([P, T], U8, align_bytes=64)
        w1s_raw = shared("w1s", "w1s_raw", [P, H], U8)
        w2s_raw = keep.tile([P, H], U8, align_bytes=64)
        w4s_raw = keep.tile([P, N], U8, align_bytes=64)
        w1_raw = keep.tile([P, H], I32, align_bytes=64)
        w2_raw = keep.tile([P, H], I32, align_bytes=64)
        w4_raw = keep.tile([P, N], I32, align_bytes=64)
        w3_raw = reuse.tile([P, PACK, H], F32, offset=2 * ROW, align_bytes=64)
        warm = keep.tile([P, 8], F32)

        nc.vector.memset(warm[:], 0.0)
        nc.scalar.activation(out=warm[:], in_=warm[:], func=ACT.Sigmoid)

        nc.sync.dma_start(offs_sb[:], offs)
        load_scale_rows(xs, x_scales)
        load_scale_rows(w2s_raw, w2_scales, range(2))
        nc.sync.dma_start(out=xw[:].bitcast(I32), in_=words_of(x_words))
        load_scale_rows(w2s_raw, w2_scales, range(2, 4))
        nc.sync.dma_start(out=w2_raw[:], in_=words_of(w2_words))
        nc.sync.dma_start(out=w1_raw[:], in_=words_of(w1_words))
        load_scale_rows(w1s_raw, w1_scales)
        nc.sync.dma_start(lists[0][:], p1)
        nc.sync.dma_start(lists[1][:], p2)
        nc.sync.dma_start(out=w3_raw[:], in_=w3.rearrange("(p j) c -> p j c", j=PACK))
        nc.sync.dma_start(out=w4_raw[:], in_=words_of(w4_words))
        load_scale_rows(w4s_raw, w4_scales)

        ident = keep.tile([P, P], F32)
        make_identity(nc, ident[:])

        xg_s = keep.tile([P, S], U8, align_bytes=64)
        xg_w = keep.tile([P, S], U32, align_bytes=64)
        w1d = shared("w1d", "w1d", [P, H], I32)
        w2d_first = keep.tile([P, P], I32, align_bytes=64)
        first, rest, whole = slice(0, 1), slice(1, PACK), slice(0, PACK)
        halves = (slice(0, HALF), slice(HALF, S))

        nc.vector.tensor_copy(out=xg_s[:], in_=xs[:].indirect(offs_sb[:]))
        for nodes in halves:
            nc.vector.tensor_copy(out=xg_w[:, nodes], in_=xw[:].indirect(entries(offs_sb, nodes)))
        w1s = keep.tile([P, H], U8, align_bytes=64)
        w2s = keep.tile([P, H], U8, align_bytes=64)
        deal_bytes(w2s[:], w2s_raw[:], whole)
        deal_words(w2d_first[:], w2_raw[:], first)
        deal_words(w1d[:], w1_raw[:], whole)
        deal_bytes(w1s[:, 0:P], w1s_raw[:], first)
        deal_bytes(w1s[:, P:H], w1s_raw[:], rest)
        w2d_rest = shared("w1s", "w2d_rest", [P, H - P], I32)
        deal_words(w2d_rest[:], w2_raw[:], rest)
        w1_parts = [w1d[:, part(t)] for t in range(PACK)]
        w2_parts = [w2d_first[:]] + [w2d_rest[:, part(t)] for t in range(PACK - 1)]

        def product(b, name, codes, plane, t, nodes=slice(0, S)):
            acc = bank(b, name, [P, nodes.stop - nodes.start])
            nc.tensor.matmul_mx(
                out=acc[:], lhsT=codes[t].bitcast(FP8X4), lhsT_scale=plane[:, part(t)],
                rhs=xg_w[:, nodes].bitcast(FP8X4), rhs_scale=xg_s[:, nodes], start=True, stop=True,
            )
            return acc

        def add_turned(cols, a, b):
            nc.tensor.matmul(cols, lhsT=a, rhs=ident[:], start=True, stop=False, is_transpose=True)
            nc.tensor.matmul(cols, lhsT=b, rhs=ident[:], start=False, stop=True, is_transpose=True)

        e_win = [keep.tile([P, S if t == 0 else 2 * S], F32, name=f"e_win{t}") for t in range(PACK)]
        h_win = [keep.tile([P, 2 * S if t < 2 else S], F32, name=f"h_win{t}") for t in range(PACK)]
        y_sb = [e_win[1][:, S:], e_win[2][:, S:], e_win[3][:, S:], h_win[0][:, S:]]
        key = {(t, i): keep.tile([P, S], F32, name=f"key{t}{i}")[:] for t in range(2) for i in range(2)}
        key[2, 0] = h_win[1][:, S:]
        gate = {t: keep.tile([P, 2, S], F32, name=f"gate{t}") for t in (2, 3)}

        e0 = [product(b, f"e0{b}", w2_parts, w2s, 0, nodes) for b, nodes in enumerate(halves)]
        y0 = [product(2 + b, f"y0{b}", w1_parts, w1s, 0, nodes) for b, nodes in enumerate(halves)]
        nc.scalar.copy(out=e_win[0][:, halves[0]], in_=e0[0][:])
        nc.scalar.copy(out=e_win[0][:, halves[1]], in_=e0[1][:])
        nc.vector.tensor_copy(out=y_sb[0][:, halves[0]], in_=y0[0][:])
        nc.scalar.copy(out=y_sb[0][:, halves[1]], in_=y0[1][:])

        def key_products(t, banks):
            nc.scalar.copy(out=e_win[t][:, 0:S], in_=product(banks[0], f"e{t}", w2_parts, w2s, t)[:])
            nc.scalar.copy(out=y_sb[t], in_=product(banks[1], f"y{t}", w1_parts, w1s, t)[:])

        def keys(t, i):
            for nodes in halves if t == 0 else (slice(0, S),):
                nc.vector.tensor_tensor(
                    key[t, i][:, nodes], e_win[t][:].indirect(entries(lists[i], nodes)), y_sb[t][:, nodes], ALU.add
                )

        def gates(t, i):
            nc.scalar.activation(out=gate[t][:, i, :], in_=key[t, i], func=ACT.Sigmoid, scale=3.0)

        den = {}

        def gate_sums(t):
            u, e = divmod(t, 2)
            for b in range(PACK):
                add_turned(den[u, b // 2][:, b % 2, e, :], gate[t][:, 0, part(b)], gate[t][:, 1, part(b)])

        def square(u, c):
            sq = reuse.tile([P, 2, 2, P], F32, name=f"sq{u}{c}", offset=(8 + u + 4 * c) * ROW, align_bytes=64)
            nc.scalar.activation(out=sq[:], in_=den[u, c][:], func=ACT.Square, bias=0.1)
            return sq[:]

        def inverse(out, sq):
            nc.scalar.activation(out=out, in_=sq, func=ACT.Abs_reciprocal_sqrt)

        key_products(1, (4, 5))
        key_products(2, (0, 2))
        for t in range(2):
            keys(t, 0)
            keys(t, 1)
        keys(2, 0)
        w3b = keep.tile([P, 2, 2, P, PACK], BF16, align_bytes=64)
        for u in range(2):
            nc.scalar.copy(
                out=w3b[:, u].rearrange("p e m j -> p m j e"),
                in_=w3_raw[:].rearrange("p j (m u e) -> p u m j e", u=2, e=2)[:, u],
            )
        w3c = keep.tile([P, H], U32, align_bytes=64)
        w3s = keep.tile([P, H], U8, align_bytes=64)
        nc.vector.quantize_mx(out=w3c[:].bitcast(FP8X4), scales=w3s[:], in_=w3b[:].rearrange("p u e m j -> p (u e m j)"))
        for t in range(2):
            gate[t] = reuse.tile([P, 2, S], F32, name=f"gate{t}", offset=5 * t * ROW + ROW // 2, align_bytes=64)
        for row, (t, i) in enumerate(((2, 1), (3, 0), (3, 1))):
            key[t, i] = reuse.tile([P, S], F32, name=f"key{t}{i}", offset=(2 + row) * ROW + ROW // 2, align_bytes=64)[:]
        keys(2, 1)
        key_products(3, (1, 3))
        keys(3, 0)
        keys(3, 1)
        w3_parts = [w3c[:, part(t)] for t in range(PACK)]
        h_acc = [product(b, f"h{t}", w3_parts, w3s, t) for t, b in enumerate((4, 5, 0, 2))]

        def values(t):
            nc.scalar.copy(out=h_win[t][:, 0:S], in_=h_acc[t][:])

        for (u, c), b in (((0, 0), 6), ((0, 1), 7), ((1, 0), 1), ((1, 1), 3)):
            den[u, c] = bank(b, f"den{u}{c}", [P, 2, 2, P])
        gates(0, 0)
        gates(0, 1)
        gate_sums(0)
        values(0)
        gates(1, 0)
        gates(1, 1)
        gate_sums(1)
        values(1)
        gates(2, 0)
        gates(2, 1)
        gate_sums(2)
        gates(3, 0)
        gates(3, 1)
        gate_sums(3)
        paired = "j b e p -> j b p e"
        inv = {(0, 0): reuse.tile([P, 2, P, 2], F32, name="inv00", offset=4 * ROW + ROW // 2, align_bytes=64)}
        sq_first = square(0, 0)
        values(2)
        values(3)
        inverse(inv[0, 0][:], sq_first.rearrange(paired))
        for u, c in ((1, 0), (0, 1)):
            inv[u, c] = keep.tile([P, 2, P, 2], F32, name=f"inv{u}{c}")
            inverse(inv[u, c][:], square(u, c).rearrange(paired))
        sq_last = square(1, 1)

        def message(msg, t, i, nodes):
            nc.vector.tensor_tensor(msg, h_win[t][:].indirect(entries(lists[i], nodes)), gate[t][:, i, nodes], ALU.mult)

        def messages(msg, t, nodes):
            for i in range(2):
                message(msg[:, i, :], t, i, nodes)

        num = {(0, 0): bank(4, "num00", [P, 2, 2, P]), (1, 0): bank(0, "num10", [P, 2, 2, P])}
        wide = keep.tile([P, 2, 2, S], F32)
        early = reuse.tile([P, 2, 2, HALF], F32, offset=10 * ROW, align_bytes=64)

        def message_sums(u, c, e, msg):
            for b in range(2):
                add_turned(num[u, c][:, b, e, :], msg[:, e, 0, part(2 * c + b)], msg[:, e, 1, part(2 * c + b)])

        for e in range(2):
            messages(wide[:, e], e, slice(0, S))
            message_sums(0, 0, e, wide)
        for e in range(2):
            messages(early[:, e], 2 + e, EARLY)
            message_sums(1, 0, e, early)
        num[0, 1] = bank(1, "num01", [P, 2, 2, P])
        message_sums(0, 1, 0, wide)

        def normalise(u, c, z):
            nc.vector.tensor_tensor(z[:], num[u, c][:].rearrange(paired), inv[u, c][:], ALU.mult)
            return z

        def turned_back(cols, z):
            for b in range(2):
                nc.tensor.transpose(cols[:, part(b)], z[:, b].rearrange("j p e -> j (p e)").bitcast(F32), ident[:])

        osc = keep.tile([P, S], U8, align_bytes=64)
        oc = keep.tile([P, S], U32, align_bytes=64)
        out_rows = out_0.rearrange("(p t) j -> p t j", t=PACK)
        out_words = out_1[0].rearrange("p n t -> p (n t)").bitcast(I32)
        results = {}

        def last_layer(name, nodes, grouped, banks, store):
            n = nodes.stop - nodes.start
            zc = keep.tile([P, n], U32, name=f"zc_{name}", align_bytes=64)
            zs = keep.tile([P, n], U8, name=f"zs_{name}", align_bytes=64)
            nc.vector.quantize_mx(out=zc[:].bitcast(FP8X4), scales=zs[:], in_=grouped)
            o_sb = keep.tile([P, PACK, n], F32, name=f"o_{name}")
            for u in range(2):
                acc = bank(banks[u], f"out_{name}{u}", [P, 2, n])
                for e in range(2):
                    wc = part(2 * u + e)
                    nc.tensor.matmul_mx(
                        out=acc[:, e, :], lhsT=w4d[:, wc].bitcast(FP8X4), lhsT_scale=w4s[:, wc],
                        rhs=zc[:].bitcast(FP8X4), rhs_scale=zs[:], start=True, stop=True,
                    )
                nc.scalar.copy(out=o_sb[:, 2 * u : 2 * u + 2, :], in_=acc[:])
                if n > P:
                    store.dma_start(out=out_rows[:, 2 * u : 2 * u + 2, nodes], in_=o_sb[:, 2 * u : 2 * u + 2, :])
            if n == P:
                store.dma_start(out=out_rows[:, :, nodes], in_=o_sb[:])
            results[name] = o_sb

        def rounded(tile, name):
            nc.vector.tensor_copy(
                out=tile.rearrange("p (c i t) -> p c t i", i=PACK, t=PACK),
                in_=results[name][:].rearrange("p t (c i) -> p c t i", i=PACK),
            )

        def planes(nodes, woven):
            nc.vector.quantize_mx(out=oc[:, nodes].bitcast(FP8X4), scales=osc[:, nodes], in_=woven)

        w4d = reuse.tile([P, N], I32, offset=7 * ROW + ROW // 2, align_bytes=64)
        w4s = reuse.tile([P, N], U8, offset=8 * ROW + ROW // 2, align_bytes=64)
        deal_words(w4d[:], w4_raw[:], whole)
        deal_bytes(w4s[:], w4s_raw[:], whole)
        zt_early = bank(6, "zt_early", [P, 2, HALF])
        zt_late = bank(7, "zt_late", [P, HALF])
        zg_early = keep.tile([P, HALF * PACK], BF16, align_bytes=64)
        zg_late = keep.tile([P, HALF * PACK], BF16, align_bytes=64)
        for u in range(2):
            turned_back(zt_early[:, u, :], normalise(u, 0, shared(f"z{u}", f"z{u}0", [P, 2, P, 2], BF16)))
        nc.scalar.copy(out=zg_early[:].bitcast(F32).rearrange("p (j u) -> p j u", u=2), in_=zt_early[:].rearrange("p u j -> p j u"))
        inv_turned = shared("z1", "inv_turned", [P, 2, 2, P], F32)
        inverse(inv_turned[:], sq_last)
        message_sums(0, 1, 1, wide)
        late = [reuse.tile([P, 2, 2, P], F32, name="late0", offset=10 * ROW - ROW // 2, align_bytes=64)]
        messages(late[0][:, 0], 2, LATE[0])
        messages(late[0][:, 1], 3, LATE[0])
        z01 = keep.tile([P, 2, P, 2], BF16, align_bytes=64)
        turned_back(zt_late[:], normalise(0, 1, z01))
        nc.scalar.copy(out=zg_late[:].bitcast(F32).rearrange("p (j u) -> p j u", u=2)[:, :, 0], in_=zt_late[:])
        inv_late = bank(2, "inv_late", [P, 2, 2, P])
        for b in range(2):
            for e in range(2):
                nc.tensor.transpose(inv_late[:, b, e, :], inv_turned[:, b, e, :], ident[:])

        def summed(b, total):
            nc.vector.tensor_tensor(total[:], late[b][:, :, 0, :], late[b][:, :, 1, :], ALU.add)
            return total

        def scaled(b, total):
            nc.vector.tensor_tensor(
                zg_late[:].rearrange("p (b j u e) -> p b u j e", b=2, u=2, e=2)[:, b, 1],
                total[:].rearrange("p e j -> p j e"), inv_late[:, b].rearrange("p e j -> p j e"), ALU.mult,
            )

        total_third = summed(0, keep.tile([P, 2, P], F32, name="total_third"))
        last_layer("early", EARLY, zg_early[:], (5, 0), nc.sync)
        late.append(reuse.tile([P, 2, 2, P], F32, name="late1", offset=13 * ROW, align_bytes=64))
        for e in range(2):
            messages(late[1][:, e], 2 + e, LATE[1])
        scaled(0, total_third)
        total_fourth = summed(1, shared("z1", "total_fourth", [P, 2, P], F32))
        last_layer("third", LATE[0], zg_late[:, 0 : P * PACK], (1, 3), nc.sync)
        scaled(1, total_fourth)
        last_layer("fourth", LATE[1], zg_late[:, P * PACK :], (4, 6), nc.scalar)
        woven = shared("z1", "woven", [P, 3 * P * PACK], BF16)
        rounded(woven[:, 0 : HALF * PACK], "early")
        rounded(woven[:, HALF * PACK :], "third")
        planes(EARLY, woven[:, 0 : HALF * PACK])
        nc.sync.dma_start(out=out_words[:, EARLY], in_=oc[:, EARLY].bitcast(I32))
        planes(LATE[0], woven[:, HALF * PACK :])
        woven_last = keep.tile([P, P * PACK], BF16, align_bytes=64)
        rounded(woven_last[:], "fourth")
        planes(LATE[1], woven_last[:])
        nc.sync.dma_start(out=out_words[:, HALF:S], in_=oc[:, HALF:S].bitcast(I32))
        out_planes = out_2[0].bitcast(I32)
        for q in range(4):
            engine = nc.sync if q % 2 == 0 else nc.scalar
            engine.dma_start(out=out_planes[4 * q : 4 * q + 4, :], in_=osc[32 * q : 32 * q + 4, :].bitcast(I32))
